import numpy as np
import ml_dtypes


def mxq(x, axis, fmt="e4m3"):
    dtype, down = {"e4m3": (ml_dtypes.float8_e4m3fn, 7), "e5m2": (ml_dtypes.float8_e5m2, 14)}[fmt]
    v = np.moveaxis(np.asarray(x, np.float32).astype(ml_dtypes.bfloat16).astype(np.float64), axis, -1)
    blocks = v.reshape(v.shape[:-1] + (-1, 32))
    amax = np.abs(blocks).max(-1, keepdims=True)
    byte = np.maximum(np.where(amax > 0, np.frexp(amax)[1] - 1 + 127, 0) - down, 1)
    scale = np.exp2(byte - 127.0)
    codes = (blocks / scale).astype(np.float32).astype(dtype).astype(np.float64)
    return np.moveaxis((codes * scale).reshape(v.shape), -1, axis)


WIDE = False


def mx_kscale(k):
    if not WIDE:
        return np.ones(k)
    levels = np.array([10, -10, 5, -5, 0])
    if k % 512:
        return np.exp2(np.random.permutation(np.resize(levels, k // 32))).repeat(32)
    a = np.empty((k // 512, 16))
    for p in range(k // 512):
        a[p, :8] = np.random.permutation(np.resize(levels, 8))
        for g in range(8):
            far = levels[np.abs(levels - a[p, g]) >= 10]
            a[p, g + 8] = far[np.random.randint(len(far))]
    return np.exp2(a.ravel()).repeat(32)


BF16 = ml_dtypes.bfloat16


def bf(x):
    return np.asarray(x, np.float32).astype(BF16)


def f64(x):
    return np.asarray(x).astype(np.float64)


B, I, J, P, Q = 16, 512, 1024, 256, 128


def silu(v):
    return v / (1.0 + np.exp(-v))


def two_sided(xq, a, b):
    t = xq @ mxq(f64(b), 0, "e4m3")
    return mxq(f64(a), 1, "e4m3") @ mxq(t, 1, "e4m3")


def draw0():
    s, u = mx_kscale(J), mx_kscale(I)
    x = np.random.standard_normal((B, I, J)) * s[None, None, :] * u[None, :, None]
    b1 = np.random.standard_normal((J, Q)) / np.sqrt(J) / s[:, None]
    b2 = np.random.standard_normal((J, Q)) / np.sqrt(J) / s[:, None]
    a1 = np.random.standard_normal((P, I)) / np.sqrt(I) / u[None, :]
    a2 = np.random.standard_normal((P, I)) / np.sqrt(I) / u[None, :]
    c = 0.5 * np.random.standard_normal((P, Q))
    return {"x": bf(x), "b1": bf(b1), "b2": bf(b2), "a1": bf(a1), "a2": bf(a2), "c": bf(c)}


def core(x, b1, b2, a1, a2, c):
    xq = mxq(f64(x), 2, "e4m3")
    u1 = two_sided(xq, a1, b1)
    u2 = two_sided(xq, a2, b2)
    z = u1 + u2 + f64(c)[None, :, :]
    return silu(z)


def e4m3fn_bytes(y):
    return np.clip(np.asarray(y, np.float64), -448.0, 448.0).astype(np.float32).astype(ml_dtypes.float8_e4m3fn).view(np.uint8)


def e4m3fn_values(b):
    return np.asarray(b, np.uint8).view(ml_dtypes.float8_e4m3fn).astype(np.float64)


def setup_inputs():
    d = draw0()
    x0 = np.asarray(d['b2']).astype(np.float64)
    s = (np.max(np.abs(x0), axis=(1,), keepdims=True) / 448.0).astype(np.float32)
    out = {}
    for k, v in d.items():
        if k == 'b2':
            out['b2_bytes'] = e4m3fn_bytes(x0 / s.astype(np.float64))
            out['b2_scale'] = s
        else:
            out[k] = v
    return out


def reference(x, b1, b2_bytes, b2_scale, a1, a2, c):
    return core(x, b1, e4m3fn_values(b2_bytes) * b2_scale.astype(np.float64), a1, a2, c)

@@ -1,0 +1,388 @@
+from contextlib import ExitStack
+
+import concourse.mybir as mybir
+from concourse.masks import make_identity
+
+FLOPS = 2 * 16 * 512 * 1024 * 256 + 2 * 2 * 16 * 256 * 512 * 128
+
+P = 128
+NB = 16
+F32 = mybir.dt.float32
+BF16 = mybir.dt.bfloat16
+U32 = mybir.dt.uint32
+U8 = mybir.dt.uint8
+FP8 = mybir.dt.float8_e4m3fn
+FP8X4 = mybir.dt.float8_e4m3fn_x4
+ACT = mybir.ActivationFunctionType
+ALU = mybir.AluOpType
+
+X_BUFS = 16
+WARM = 5
+DUMMY = {(0, 3): 2, (2, 3): 2}
+FP = (0, 2, 2, 2)
+FQ = (3, 4)
+CV = (1, 0, 1, 0)
+FV = (0, 0, 0, 0)
+
+
+def tile_ranktwokroneckersumlayer_t_kernel(tc, x, b1, b2_bytes, b2_scale, a1, a2, c, out):
+    nc = tc.nc
+
+    def permuted_slots(n):
+        return FP[n] if n < len(FP) else FQ[n % len(FQ)]
+
+    with ExitStack() as ctx:
+        keep = ctx.enter_context(tc.tile_pool(name="keep", bufs=1))
+        xpool = ctx.enter_context(tc.tile_pool(name="xpool", bufs=X_BUFS))
+        ppool = ctx.enter_context(tc.tile_pool(name="ppool", bufs=2))
+        gpool = ctx.enter_context(tc.tile_pool(name="gpool", bufs=4))
+        qpool = ctx.enter_context(tc.tile_pool(name="qpool", bufs=6))
+        tpool = ctx.enter_context(tc.tile_pool(name="tpool", bufs=2))
+        zpool = ctx.enter_context(tc.tile_pool(name="zpool", bufs=3))
+        ps_t = ctx.enter_context(tc.psum_pool(name="ps_t", bufs=4))
+        ps_s = ctx.enter_context(tc.psum_pool(name="ps_s", bufs=3))
+        ps_z = ctx.enter_context(tc.psum_pool(name="ps_z", bufs=1))
+        ctx.enter_context(tc.manual_schedule())
+
+        ident = keep.tile([P, P], F32, name="ident")
+        warm = keep.tile([P, 1], F32, name="warm")
+        b2_raw = keep.tile([P, 2, 4, P], U8, name="b2_raw")
+        b2_s = keep.tile([P, 2, 4], F32, name="b2_s")
+        b2_w = keep.tile([P, 2, 4, P], BF16, name="b2_w")
+        b1_raw = keep.tile([P, 2, 4, P], BF16, name="b1_raw")
+        b_grp = keep.tile([P, 2 * 1024], BF16, name="b_grp", align_bytes=64)
+        b_codes = keep.tile([P, 512], U32, name="b_codes", align_bytes=64)
+        b_scales = keep.tile([P, 512], U8, name="b_scales", align_bytes=64)
+        a_raw = keep.tile([P, 2, 1024], BF16, name="a_raw")
+        a_grp = keep.tile([P, 2048], BF16, name="a_grp", align_bytes=64)
+        a_codes = keep.tile([P, 512], U32, name="a_codes", align_bytes=64)
+        a_scales = keep.tile([P, 512], U8, name="a_scales", align_bytes=64)
+        c_t = keep.tile([P, 2, 256], BF16, name="c_t")
+
+        xs = {}
+
+        loaded = {}
+
+        def load_x(n, pieces=(4,)):
+            if n not in xs:
+                xs[n] = xpool.tile([P, 4, 1024], BF16, name="x_t")
+            src = x[n].rearrange("(m s) k -> m s k", s=4)
+            for step in pieces:
+                s = loaded.get(n, 0)
+                nc.sync.dma_start(out=xs[n][:, s : s + step, :], in_=src[:, s : s + step, :])
+                loaded[n] = s + step
+
+        nc.sync.dma_start(out=b2_s[:], in_=b2_scale.rearrange("(g p t) o -> p g (t o)", g=2, t=4))
+        nc.sync.dma_start(out=b2_raw[:], in_=b2_bytes.rearrange("(g p t) q -> p g t q", g=2, t=4))
+        load_x(0, (1,))
+        nc.sync.dma_start(out=b1_raw[:], in_=b1.rearrange("(g p t) q -> p g t q", g=2, t=4))
+        load_x(0, (1, 2))
+        load_x(1, (2, 2))
+        load_x(2, (2, 2))
+        load_x(3, (2, 2))
+        nc.sync.dma_start(out=a_raw[:, 0, :], in_=a1.rearrange("(m h) k -> m (h k)", h=2))
+        nc.sync.dma_start(out=a_raw[:, 1, :], in_=a2.rearrange("(m h) k -> m (h k)", h=2))
+        for i in range(2):
+            nc.sync.dma_start(out=c_t[:, i, :], in_=c.rearrange("(m h) q -> m (h q)", h=2))
+        for n in range(4, X_BUFS):
+            load_x(n)
+
+        nc.gpsimd.memset(warm[:], 0.0)
+        make_identity(nc, ident[:])
+        zero = keep.tile([P, 512], BF16, name="zero")
+        nc.vector.memset(zero[:], 0.0)
+
+        def warm_tensor(count):
+            for i in range(count):
+                bank = ps_z.tile([P, 2, 256], F32, name="z_bank")
+                nc.tensor.matmul(
+                    bank[:].rearrange("p h x -> p (h x)"), lhsT=zero[:, :P], rhs=zero[:], start=True, stop=True
+                )
+
+        warm_tensor(WARM)
+        nc.scalar.activation(out=warm[:], in_=warm[:], func=ACT.Silu)
+
+        for i in range(8):
+            g, t = divmod(i, 4)
+            src = b2_raw[:, g, t, :].bitcast(FP8)
+            if i < 3:
+                nc.vector.tensor_scalar(
+                    out=b2_w[:, g, t, :], in0=src, scalar1=b2_s[:, g, t : t + 1], scalar2=None, op0=ALU.mult
+                )
+            else:
+                nc.scalar.activation(out=b2_w[:, g, t, :], in_=src, func=ACT.Copy, scale=b2_s[:, g, t : t + 1])
+
+        def interleave_b(i, src):
+            nc.vector.tensor_copy(
+                out=b_grp[:, 1024 * i : 1024 * (i + 1)].rearrange("p (g q t) -> p g q t", g=2, t=4),
+                in_=src[:].rearrange("p g t q -> p g q t"),
+            )
+
+        def quantize_b(i):
+            nc.vector.quantize_mx(
+                out=b_codes[:, 256 * i : 256 * (i + 1)].bitcast(FP8X4),
+                scales=b_scales[:, 256 * i : 256 * (i + 1)],
+                in_=b_grp[:, 1024 * i : 1024 * (i + 1)],
+            )
+
+        perm = {}
+        banks = {}
+        grp = {}
+        codes = {}
+        s1 = {}
+        tg = {}
+        tcodes = {}
+        zb = {}
+        zs = {}
+
+        def permute(n):
+            k = permuted_slots(n)
+            if k == 0:
+                return
+            t = ppool.tile([P, 4096], BF16, name="x_p")
+            nc.vector.tensor_copy(
+                out=t[:, : 1024 * k].bitcast(F32).rearrange("p (a u w) -> p a u w", u=2, w=P),
+                in_=xs[n][:, :k, :].rearrange("p s k -> p (s k)").bitcast(F32).rearrange("p (a w u) -> p a u w", u=2, w=P),
+            )
+            perm[n] = t
+
+        def transposes(n, s):
+            bank = ps_t.tile([P, 4, P], F32, name="t_bank")
+            for g in range(2):
+                for u in range(2):
+                    if s < permuted_slots(n):
+                        w = perm[n][:].bitcast(F32)
+                        lo = 512 * s + 256 * g + 128 * u
+                        src = w[:, lo : lo + 128]
+                    else:
+                        w = xs[n][:, s, :].bitcast(F32)
+                        src = w[:, 256 * g + u : 256 * (g + 1) : 2]
+                    nc.tensor.transpose(bank[:, 2 * g + u, :], src, ident[:])
+            banks[n, s] = bank
+
+        def unload(n, s, eng):
+            h, s2 = divmod(s, 2)
+            if s2 == 0:
+                grp[n, h] = gpool.tile([P, 2048], BF16, name="x_g", align_bytes=64)
+            dst = grp[n, h][:].bitcast(F32)[:, 512 * s2 : 512 * (s2 + 1)].rearrange("p (g m u) -> p g m u", g=2, u=2)
+            src = banks[n, s][:].rearrange("p (g u) m -> p g m u", g=2)
+            if eng == "S":
+                nc.scalar.copy(out=dst, in_=src)
+            else:
+                nc.vector.tensor_copy(out=dst, in_=src)
+
+        def quantize_x(n, h):
+            q = qpool.tile([P, 512], U32, name="x_q", align_bytes=64)
+            sc = qpool.tile([P, 512], U8, name="x_s", align_bytes=64)
+            nc.vector.quantize_mx(out=q[:].bitcast(FP8X4), scales=sc[:], in_=grp[n, h][:])
+            codes[n, h] = (q, sc)
+
+        def stage1(n, part=None):
+            if part != 1:
+                for b in range(2):
+                    if part == 0:
+                        s1[n, b] = ps_t.tile([P, 4, P], F32, name="t_bank")
+                    else:
+                        s1[n, b] = ps_s.tile([P, 4, P], F32, name="s_bank")
+            ts = range(4) if part is None else (2 * part, 2 * part + 1)
+            for b, t in [(b, t) for b in range(2) for t in ts]:
+                q, sc = codes[n, t // 2]
+                for g in range(2):
+                    cols = slice(256 * (t % 2) + 128 * g, 256 * (t % 2) + 128 * (g + 1))
+                    bcols = slice(256 * b + 128 * g, 256 * b + 128 * (g + 1))
+                    nc.tensor.matmul_mx(
+                        out=s1[n, b][:, t, :],
+                        lhsT=q[:, cols].bitcast(FP8X4),
+                        lhsT_scale=sc[:, cols],
+                        rhs=b_codes[:, bcols].bitcast(FP8X4),
+                        rhs_scale=b_scales[:, bcols],
+                        start=(g == 0),
+                        stop=(g == 1),
+                    )
+
+        def unload1(n, b, eng):
+            pair, i = divmod(n, 2)
+            if i == 0 and b == 0:
+                tg[pair] = tpool.tile([P, 2048], BF16, name="t_g", align_bytes=64)
+            lo = 512 * (2 * b + i)
+            dst = tg[pair][:, lo : lo + 512].rearrange("p (q t) -> p q t", t=4)
+            src = s1[n, b][:].rearrange("p t q -> p q t")
+            if eng == "S":
+                nc.scalar.copy(out=dst, in_=src)
+            else:
+                nc.vector.tensor_copy(out=dst, in_=src)
+
+        def quantize_t_one(n):
+            pair, i = divmod(n, 2)
+            if i == 0:
+                q = tpool.tile([P, 512], U32, name="t_q", align_bytes=64)
+                sc = tpool.tile([P, 512], U8, name="t_s", align_bytes=64)
+                tcodes[pair] = (q, sc)
+            q, sc = tcodes[pair]
+            for b in range(2):
+                lo = 128 * (2 * b + i)
+                nc.vector.quantize_mx(
+                    out=q[:, lo : lo + 128].bitcast(FP8X4), scales=sc[:, lo : lo + 128], in_=tg[pair][:, 4 * lo : 4 * lo + 512]
+                )
+
+        def stage2_one(n):
+            pair, i = divmod(n, 2)
+            bank = ps_t.tile([P, 4, P], F32, name="t_bank")
+            q, sc = tcodes[pair]
+            for h in range(2):
+                for b in range(2):
+                    acols = slice(128 * (2 * b + h), 128 * (2 * b + h + 1))
+                    tcols = slice(128 * (2 * b + i), 128 * (2 * b + i + 1))
+                    nc.tensor.matmul_mx(
+                        out=bank[:, h, :],
+                        lhsT=a_codes[:, acols].bitcast(FP8X4),
+                        lhsT_scale=a_scales[:, acols],
+                        rhs=q[:, tcols].bitcast(FP8X4),
+                        rhs_scale=sc[:, tcols],
+                        start=(b == 0),
+                        stop=(b == 1),
+                    )
+            zb[n, "one"] = bank
+
+        def add_c_one(n):
+            t = zpool.tile([P, 2, P], F32, name="z_one")
+            nc.vector.tensor_tensor(
+                out=t[:], in0=zb[n, "one"][:, :2, :], in1=c_t[:, 0, :].rearrange("p (h q) -> p h q", h=2), op=ALU.add
+            )
+            zs[n, "one"] = t
+
+        def silu_store_one(n):
+            o = zpool.tile([P, 2, P], F32, name="o_one")
+            nc.scalar.activation(out=o[:], in_=zs[n, "one"][:], func=ACT.Silu)
+            nc.sync.dma_start(out=out[n].rearrange("(m h) q -> m (h q)", h=2), in_=o[:].rearrange("p h q -> p (h q)"))
+
+        def quantize_t(pair):
+            q = tpool.tile([P, 512], U32, name="t_q", align_bytes=64)
+            sc = tpool.tile([P, 512], U8, name="t_s", align_bytes=64)
+            nc.vector.quantize_mx(out=q[:].bitcast(FP8X4), scales=sc[:], in_=tg[pair][:])
+            tcodes[pair] = (q, sc)
+
+        def stage2(pair):
+            bank = ps_z.tile([P, 2, 256], F32, name="z_bank")
+            q, sc = tcodes[pair]
+            for h in range(2):
+                for b in range(2):
+                    acols = slice(128 * (2 * b + h), 128 * (2 * b + h + 1))
+                    tcols = slice(256 * b, 256 * (b + 1))
+                    nc.tensor.matmul_mx(
+                        out=bank[:, h, :],
+                        lhsT=a_codes[:, acols].bitcast(FP8X4),
+                        lhsT_scale=a_scales[:, acols],
+                        rhs=q[:, tcols].bitcast(FP8X4),
+                        rhs_scale=sc[:, tcols],
+                        start=(b == 0),
+                        stop=(b == 1),
+                    )
+            zb[pair] = bank
+
+        def add_c(pair):
+            t = zpool.tile([P, 2, 2, P], F32, name="z_s")
+            nc.vector.tensor_tensor(
+                out=t[:],
+                in0=zb[pair][:].rearrange("p h (n q) -> p n h q", n=2),
+                in1=c_t[:].rearrange("p n (h q) -> p n h q", h=2),
+                op=ALU.add,
+            )
+            zs[pair] = t
+
+        def silu_store(pair):
+            o = zpool.tile([P, 2, 256], F32, name="o_t")
+            nc.scalar.activation(out=o[:].rearrange("p n (h q) -> p n h q", h=2), in_=zs[pair][:], func=ACT.Silu)
+            nc.sync.dma_start(out=out[2 * pair : 2 * pair + 2].rearrange("n (m h) q -> m n (h q)", h=2), in_=o[:])
+
+        def prepare_a():
+            for b in range(2):
+                bank = ps_s.tile([P, 4, P], F32, name="s_bank")
+                w = a_raw[:, b, :].bitcast(F32)
+                for h in range(2):
+                    for u in range(2):
+                        nc.tensor.transpose(bank[:, 2 * h + u, :], w[:, 256 * h + u : 256 * (h + 1) : 2], ident[:])
+                dst = a_grp[:].bitcast(F32)[:, 512 * b : 512 * (b + 1)].rearrange("p (h m u) -> p h m u", h=2, u=2)
+                src = bank[:].rearrange("p (h u) m -> p h m u", h=2)
+                if b < 2:
+                    nc.scalar.copy(out=dst, in_=src)
+                else:
+                    nc.vector.tensor_copy(out=dst, in_=src)
+
+        def quantize_a():
+            nc.vector.quantize_mx(out=a_codes[:].bitcast(FP8X4), scales=a_scales[:], in_=a_grp[:])
+
+        interleave_b(1, b2_w)
+        interleave_b(0, b1_raw)
+        quantize_b(1)
+        quantize_b(0)
+        for j in range(NB - 1):
+            if j:
+                quantize_x(j - 1, 1)
+            if j == 4:
+                quantize_a()
+            for s in range(4):
+                transposes(j, s)
+                warm_tensor(DUMMY.get((j, s), 0))
+            unload(j, 0, "S")
+            unload(j, 1, "S")
+            if j + 1 < NB:
+                permute(j + 1)
+            unload(j, 2, "S")
+            if not CV[j % 4]:
+                unload(j, 3, "S")
+            if j >= 7 and j % 2:
+                silu_store((j - 7) // 2)
+            if j == 2:
+                prepare_a()
+            if j >= 4 and j % 2 == 0:
+                quantize_t((j - 4) // 2)
+            if CV[j % 4]:
+                unload(j, 3, "V")
+            quantize_x(j, 0)
+            if j >= 5 and j % 2:
+                stage2((j - 5) // 2)
+            k = 0 if j == 1 else j - 2
+            if k >= 0 and j != 2:
+                stage1(k)
+                unload1(k, 0, "S")
+                unload1(k, 1, "S")
+            if j >= 6 and j % 2 == 0:
+                add_c((j - 6) // 2)
+        quantize_x(14, 1)
+        transposes(15, 0)
+        transposes(15, 1)
+        transposes(15, 2)
+        transposes(15, 3)
+        unload(15, 0, "V")
+        unload(15, 1, "S")
+        unload(15, 2, "V")
+        unload(15, 3, "S")
+        stage1(13)
+        quantize_x(15, 0)
+        unload1(13, 0, "S")
+        quantize_x(15, 1)
+        unload1(13, 1, "S")
+        stage1(14)
+        quantize_t(6)
+        unload1(14, 0, "S")
+        unload1(14, 1, "S")
+        stage1(15, 0)
+        stage2(5)
+        stage1(15, 1)
+        silu_store(4)
+        quantize_t_one(14)
+        add_c(5)
+        unload1(15, 0, "S")
+        stage2_one(14)
+        unload1(15, 1, "V")
+        stage2(6)
+        add_c_one(14)
+        silu_store(5)
+        quantize_t_one(15)
+        add_c(6)
+        silu_store_one(14)
+        stage2_one(15)
+        add_c_one(15)
+        silu_store(6)
+        silu_store_one(15)

@@ -16,116 +16,86 @@ FP8X4 = mybir.dt.float8_e4m3fn_x4
 ACT = mybir.ActivationFunctionType
 ALU = mybir.AluOpType
 
-X_BUFS = 16
-WARM = 5
-DUMMY = {(0, 3): 2, (2, 3): 2}
-FP = (0, 2, 2, 2)
-FQ = (3, 4)
-CV = (1, 0, 1, 0)
-FV = (0, 0, 0, 0)
-
 
 def tile_ranktwokroneckersumlayer_t_kernel(tc, x, b1, b2_bytes, b2_scale, a1, a2, c, out):
     nc = tc.nc
 
-    def permuted_slots(n):
-        return FP[n] if n < len(FP) else FQ[n % len(FQ)]
-
     with ExitStack() as ctx:
         keep = ctx.enter_context(tc.tile_pool(name="keep", bufs=1))
-        xpool = ctx.enter_context(tc.tile_pool(name="xpool", bufs=X_BUFS))
-        ppool = ctx.enter_context(tc.tile_pool(name="ppool", bufs=2))
+        xpool = ctx.enter_context(tc.tile_pool(name="xpool", bufs=NB))
+        upool = ctx.enter_context(tc.tile_pool(name="upool", bufs=2))
         gpool = ctx.enter_context(tc.tile_pool(name="gpool", bufs=4))
         qpool = ctx.enter_context(tc.tile_pool(name="qpool", bufs=6))
-        tpool = ctx.enter_context(tc.tile_pool(name="tpool", bufs=2))
-        zpool = ctx.enter_context(tc.tile_pool(name="zpool", bufs=3))
+        tpool = ctx.enter_context(tc.tile_pool(name="tpool", bufs=3))
+        zpool = ctx.enter_context(tc.tile_pool(name="zpool", bufs=4))
         ps_t = ctx.enter_context(tc.psum_pool(name="ps_t", bufs=4))
         ps_s = ctx.enter_context(tc.psum_pool(name="ps_s", bufs=3))
         ps_z = ctx.enter_context(tc.psum_pool(name="ps_z", bufs=1))
         ctx.enter_context(tc.manual_schedule())
 
         ident = keep.tile([P, P], F32, name="ident")
-        warm = keep.tile([P, 1], F32, name="warm")
+        table = keep.tile([P, 1], F32, name="table")
+        pick = keep.tile([P, 2, 2, P], BF16, name="pick")
         b2_raw = keep.tile([P, 2, 4, P], U8, name="b2_raw")
         b2_s = keep.tile([P, 2, 4], F32, name="b2_s")
         b2_w = keep.tile([P, 2, 4, P], BF16, name="b2_w")
         b1_raw = keep.tile([P, 2, 4, P], BF16, name="b1_raw")
-        b_grp = keep.tile([P, 2 * 1024], BF16, name="b_grp", align_bytes=64)
+        b_grp = keep.tile([P, 2048], BF16, name="b_grp", align_bytes=64)
         b_codes = keep.tile([P, 512], U32, name="b_codes", align_bytes=64)
         b_scales = keep.tile([P, 512], U8, name="b_scales", align_bytes=64)
         a_raw = keep.tile([P, 2, 1024], BF16, name="a_raw")
         a_grp = keep.tile([P, 2048], BF16, name="a_grp", align_bytes=64)
         a_codes = keep.tile([P, 512], U32, name="a_codes", align_bytes=64)
         a_scales = keep.tile([P, 512], U8, name="a_scales", align_bytes=64)
-        c_t = keep.tile([P, 2, 256], BF16, name="c_t")
+        c_t = keep.tile([P, 2, P], BF16, name="c_t")
 
         xs = {}
 
-        loaded = {}
-
-        def load_x(n, pieces=(4,)):
+        def load_x(n, lo, hi):
             if n not in xs:
-                xs[n] = xpool.tile([P, 4, 1024], BF16, name="x_t")
-            src = x[n].rearrange("(m s) k -> m s k", s=4)
-            for step in pieces:
-                s = loaded.get(n, 0)
-                nc.sync.dma_start(out=xs[n][:, s : s + step, :], in_=src[:, s : s + step, :])
-                loaded[n] = s + step
+                xs[n] = xpool.tile([P, 4096], BF16, name="x_t")
+            src = x[n].rearrange("(m s) k -> m (s k)", s=4)
+            nc.sync.dma_start(out=xs[n][:, 1024 * lo : 1024 * hi], in_=src[:, 1024 * lo : 1024 * hi])
 
+        nc.sync.dma_start(out=b1_raw[:], in_=b1.rearrange("(g p t) q -> p g t q", g=2, t=4))
         nc.sync.dma_start(out=b2_s[:], in_=b2_scale.rearrange("(g p t) o -> p g (t o)", g=2, t=4))
         nc.sync.dma_start(out=b2_raw[:], in_=b2_bytes.rearrange("(g p t) q -> p g t q", g=2, t=4))
-        load_x(0, (1,))
-        nc.sync.dma_start(out=b1_raw[:], in_=b1.rearrange("(g p t) q -> p g t q", g=2, t=4))
-        load_x(0, (1, 2))
-        load_x(1, (2, 2))
-        load_x(2, (2, 2))
-        load_x(3, (2, 2))
+        load_x(0, 0, 1)
+        load_x(0, 1, 2)
+        load_x(0, 2, 4)
+        for n in (1, 2, 3):
+            load_x(n, 0, 2)
+            load_x(n, 2, 4)
         nc.sync.dma_start(out=a_raw[:, 0, :], in_=a1.rearrange("(m h) k -> m (h k)", h=2))
+        load_x(4, 0, 4)
         nc.sync.dma_start(out=a_raw[:, 1, :], in_=a2.rearrange("(m h) k -> m (h k)", h=2))
-        for i in range(2):
-            nc.sync.dma_start(out=c_t[:, i, :], in_=c.rearrange("(m h) q -> m (h q)", h=2))
-        for n in range(4, X_BUFS):
-            load_x(n)
+        load_x(5, 0, 4)
+        nc.sync.dma_start(out=c_t[:], in_=c.rearrange("(m h) q -> m h q", h=2))
+        for n in range(6, NB):
+            load_x(n, 0, 4)
 
-        nc.gpsimd.memset(warm[:], 0.0)
+        nc.gpsimd.memset(table[:], 0.0)
         make_identity(nc, ident[:])
-        zero = keep.tile([P, 512], BF16, name="zero")
-        nc.vector.memset(zero[:], 0.0)
+        nc.scalar.activation(out=table[:], in_=table[:], func=ACT.Silu)
 
-        def warm_tensor(count):
-            for i in range(count):
-                bank = ps_z.tile([P, 2, 256], F32, name="z_bank")
-                nc.tensor.matmul(
-                    bank[:].rearrange("p h x -> p (h x)"), lhsT=zero[:, :P], rhs=zero[:], start=True, stop=True
+        nc.vector.memset(pick[:], 0.0)
+        for u in range(2):
+            for odd in range(2):
+                nc.vector.tensor_copy(
+                    out=pick[:, u, odd, :].rearrange("p (j r i o) -> p j r i o", r=2, i=4, o=2)[:, :, :, :, odd],
+                    in_=ident[:].rearrange("p (r j u i) -> p u j r i", r=2, u=2, i=4)[:, u],
                 )
 
-        warm_tensor(WARM)
-        nc.scalar.activation(out=warm[:], in_=warm[:], func=ACT.Silu)
-
-        for i in range(8):
-            g, t = divmod(i, 4)
+        def widen_b2(g, t, eng):
             src = b2_raw[:, g, t, :].bitcast(FP8)
-            if i < 3:
+            if eng == "V":
                 nc.vector.tensor_scalar(
                     out=b2_w[:, g, t, :], in0=src, scalar1=b2_s[:, g, t : t + 1], scalar2=None, op0=ALU.mult
                 )
             else:
                 nc.scalar.activation(out=b2_w[:, g, t, :], in_=src, func=ACT.Copy, scale=b2_s[:, g, t : t + 1])
 
-        def interleave_b(i, src):
-            nc.vector.tensor_copy(
-                out=b_grp[:, 1024 * i : 1024 * (i + 1)].rearrange("p (g q t) -> p g q t", g=2, t=4),
-                in_=src[:].rearrange("p g t q -> p g q t"),
-            )
-
-        def quantize_b(i):
-            nc.vector.quantize_mx(
-                out=b_codes[:, 256 * i : 256 * (i + 1)].bitcast(FP8X4),
-                scales=b_scales[:, 256 * i : 256 * (i + 1)],
-                in_=b_grp[:, 1024 * i : 1024 * (i + 1)],
-            )
-
-        perm = {}
+        upper = {}
         banks = {}
         grp = {}
         codes = {}
@@ -135,41 +105,76 @@ def tile_ranktwokroneckersumlayer_t_kernel(tc, x, b1, b2_bytes, b2_scale, a1, a2
         zb = {}
         zs = {}
 
-        def permute(n):
-            k = permuted_slots(n)
-            if k == 0:
-                return
-            t = ppool.tile([P, 4096], BF16, name="x_p")
-            nc.vector.tensor_copy(
-                out=t[:, : 1024 * k].bitcast(F32).rearrange("p (a u w) -> p a u w", u=2, w=P),
-                in_=xs[n][:, :k, :].rearrange("p s k -> p (s k)").bitcast(F32).rearrange("p (a w u) -> p a u w", u=2, w=P),
-            )
-            perm[n] = t
-
-        def transposes(n, s):
-            bank = ps_t.tile([P, 4, P], F32, name="t_bank")
-            for g in range(2):
-                for u in range(2):
-                    if s < permuted_slots(n):
-                        w = perm[n][:].bitcast(F32)
-                        lo = 512 * s + 256 * g + 128 * u
-                        src = w[:, lo : lo + 128]
-                    else:
-                        w = xs[n][:, s, :].bitcast(F32)
-                        src = w[:, 256 * g + u : 256 * (g + 1) : 2]
-                    nc.tensor.transpose(bank[:, 2 * g + u, :], src, ident[:])
-            banks[n, s] = bank
-
-        def unload(n, s, eng):
-            h, s2 = divmod(s, 2)
-            if s2 == 0:
-                grp[n, h] = gpool.tile([P, 2048], BF16, name="x_g", align_bytes=64)
-            dst = grp[n, h][:].bitcast(F32)[:, 512 * s2 : 512 * (s2 + 1)].rearrange("p (g m u) -> p g m u", g=2, u=2)
-            src = banks[n, s][:].rearrange("p (g u) m -> p g m u", g=2)
+        def copy(eng, dst, src):
             if eng == "S":
                 nc.scalar.copy(out=dst, in_=src)
             else:
                 nc.vector.tensor_copy(out=dst, in_=src)
+
+        def reorder_b(b, src):
+            bank = ps_s.tile([P, 2, P, 2, 2], BF16, name="s_bank")
+            for g in range(2):
+                for u in range(2):
+                    for odd in range(2):
+                        nc.tensor.matmul(
+                            bank[:, g, :, u, :],
+                            lhsT=pick[:, u, odd, :],
+                            rhs=src[:, g, 2 * odd : 2 * odd + 2, :].rearrange("p e q -> p q e"),
+                            start=(odd == 0),
+                            stop=(odd == 1),
+                        )
+            banks["b", b] = bank
+
+        def unload_b(b, eng):
+            copy(eng, b_grp[:, 1024 * b : 1024 * (b + 1)], banks["b", b][:].rearrange("p g q u e -> p (g q u e)"))
+
+        def quantize_b():
+            nc.vector.quantize_mx(out=b_codes[:].bitcast(FP8X4), scales=b_scales[:], in_=b_grp[:])
+
+        def turn_a(b):
+            bank = ps_s.tile([P, 4, P], F32, name="s_bank")
+            w = a_raw[:, b, :].bitcast(F32)
+            for h in range(2):
+                for u in range(2):
+                    nc.tensor.transpose(bank[:, 2 * h + u, :], w[:, 256 * h + u : 256 * (h + 1) : 2], ident[:])
+            banks["a", b] = bank
+
+        def unload_a(b, eng):
+            dst = a_grp[:].bitcast(F32)[:, 512 * b : 512 * (b + 1)].rearrange("p (h m u) -> p h m u", h=2, u=2)
+            copy(eng, dst, banks["a", b][:].rearrange("p (h u) m -> p h m u", h=2))
+
+        def quantize_a():
+            nc.vector.quantize_mx(out=a_codes[:].bitcast(FP8X4), scales=a_scales[:], in_=a_grp[:])
+
+        def halves(n, lo, hi):
+            return xs[n][:, 1024 * lo : 1024 * hi].rearrange("p (a r j u w) -> p u a j r w", r=2, j=8, u=2, w=16)
+
+        def gather_upper(n, lo, hi):
+            if lo == 0:
+                upper[n] = upool.tile([P, 2048], BF16, name="x_u")
+            dst = upper[n][:, 512 * lo : 512 * hi].rearrange("p (a j r w) -> p a j r w", j=8, r=2, w=16)
+            nc.vector.tensor_copy(out=dst, in_=halves(n, lo, hi)[:, 1])
+
+        def close_lower(n, lo, hi):
+            view = halves(n, lo, hi)
+            nc.vector.tensor_copy(out=view[:, 1, :, :, 0, :], in_=view[:, 0, :, :, 1, :])
+
+        def turn_x(n, s):
+            bank = ps_t.tile([P, 4, P], F32, name="t_bank")
+            lower_w = xs[n][:].bitcast(F32)
+            upper_w = upper[n][:].bitcast(F32)
+            for g in range(2):
+                lo = 512 * s + 256 * g
+                nc.tensor.transpose(bank[:, 2 * g, :], lower_w[:, lo : lo + P], ident[:])
+                nc.tensor.transpose(bank[:, 2 * g + 1, :], upper_w[:, lo // 2 : lo // 2 + P], ident[:])
+            banks[n, s] = bank
+
+        def unload_x(n, s, eng):
+            h, s2 = divmod(s, 2)
+            if s2 == 0:
+                grp[n, h] = gpool.tile([P, 2048], BF16, name="x_g", align_bytes=64)
+            dst = grp[n, h][:].bitcast(F32)[:, 512 * s2 : 512 * (s2 + 1)].rearrange("p (g m u) -> p g m u", g=2, u=2)
+            copy(eng, dst, banks[n, s][:].rearrange("p (g u) m -> p g m u", g=2))
 
         def quantize_x(n, h):
             q = qpool.tile([P, 512], U32, name="x_q", align_bytes=64)
@@ -177,21 +182,15 @@ def tile_ranktwokroneckersumlayer_t_kernel(tc, x, b1, b2_bytes, b2_scale, a1, a2
             nc.vector.quantize_mx(out=q[:].bitcast(FP8X4), scales=sc[:], in_=grp[n, h][:])
             codes[n, h] = (q, sc)
 
-        def stage1(n, part=None):
-            if part != 1:
-                for b in range(2):
-                    if part == 0:
-                        s1[n, b] = ps_t.tile([P, 4, P], F32, name="t_bank")
-                    else:
-                        s1[n, b] = ps_s.tile([P, 4, P], F32, name="s_bank")
-            ts = range(4) if part is None else (2 * part, 2 * part + 1)
-            for b, t in [(b, t) for b in range(2) for t in ts]:
-                q, sc = codes[n, t // 2]
+        def first_product(n, b):
+            bank = ps_s.tile([P, 4, P], F32, name="s_bank")
+            for s in range(4):
+                q, sc = codes[n, s // 2]
                 for g in range(2):
-                    cols = slice(256 * (t % 2) + 128 * g, 256 * (t % 2) + 128 * (g + 1))
-                    bcols = slice(256 * b + 128 * g, 256 * b + 128 * (g + 1))
+                    cols = slice(256 * (s % 2) + P * g, 256 * (s % 2) + P * (g + 1))
+                    bcols = slice(256 * b + P * g, 256 * b + P * (g + 1))
                     nc.tensor.matmul_mx(
-                        out=s1[n, b][:, t, :],
+                        out=bank[:, s, :],
                         lhsT=q[:, cols].bitcast(FP8X4),
                         lhsT_scale=sc[:, cols],
                         rhs=b_codes[:, bcols].bitcast(FP8X4),
@@ -199,40 +198,27 @@ def tile_ranktwokroneckersumlayer_t_kernel(tc, x, b1, b2_bytes, b2_scale, a1, a2
                         start=(g == 0),
                         stop=(g == 1),
                     )
+            s1[n, b] = bank
 
-        def unload1(n, b, eng):
-            pair, i = divmod(n, 2)
-            if i == 0 and b == 0:
-                tg[pair] = tpool.tile([P, 2048], BF16, name="t_g", align_bytes=64)
-            lo = 512 * (2 * b + i)
-            dst = tg[pair][:, lo : lo + 512].rearrange("p (q t) -> p q t", t=4)
-            src = s1[n, b][:].rearrange("p t q -> p q t")
-            if eng == "S":
-                nc.scalar.copy(out=dst, in_=src)
-            else:
-                nc.vector.tensor_copy(out=dst, in_=src)
+        def unload_t(n, b, first, size, eng):
+            if n == first and b == 0:
+                tg[first] = tpool.tile([P, 1024 * size], BF16, name="t_g", align_bytes=64)
+            lo = 512 * (size * b + n - first)
+            copy(eng, tg[first][:, lo : lo + 512].rearrange("p (q s) -> p q s", s=4), s1[n, b][:].rearrange("p s q -> p q s"))
 
-        def quantize_t_one(n):
-            pair, i = divmod(n, 2)
-            if i == 0:
-                q = tpool.tile([P, 512], U32, name="t_q", align_bytes=64)
-                sc = tpool.tile([P, 512], U8, name="t_s", align_bytes=64)
-                tcodes[pair] = (q, sc)
-            q, sc = tcodes[pair]
-            for b in range(2):
-                lo = 128 * (2 * b + i)
-                nc.vector.quantize_mx(
-                    out=q[:, lo : lo + 128].bitcast(FP8X4), scales=sc[:, lo : lo + 128], in_=tg[pair][:, 4 * lo : 4 * lo + 512]
-                )
+        def quantize_t(first, size):
+            q = tpool.tile([P, 256 * size], U32, name="t_q", align_bytes=64)
+            sc = tpool.tile([P, 256 * size], U8, name="t_s", align_bytes=64)
+            nc.vector.quantize_mx(out=q[:].bitcast(FP8X4), scales=sc[:], in_=tg[first][:])
+            tcodes[first] = (q, sc)
 
-        def stage2_one(n):
-            pair, i = divmod(n, 2)
-            bank = ps_t.tile([P, 4, P], F32, name="t_bank")
-            q, sc = tcodes[pair]
+        def second_product(first, size, pool, tag):
+            bank = pool.tile([P, 2, P * size], F32, name=tag)
+            q, sc = tcodes[first]
             for h in range(2):
                 for b in range(2):
-                    acols = slice(128 * (2 * b + h), 128 * (2 * b + h + 1))
-                    tcols = slice(128 * (2 * b + i), 128 * (2 * b + i + 1))
+                    acols = slice(P * (2 * b + h), P * (2 * b + h + 1))
+                    tcols = slice(P * size * b, P * size * (b + 1))
                     nc.tensor.matmul_mx(
                         out=bank[:, h, :],
                         lhsT=a_codes[:, acols].bitcast(FP8X4),
@@ -242,147 +228,117 @@ def tile_ranktwokroneckersumlayer_t_kernel(tc, x, b1, b2_bytes, b2_scale, a1, a2
                         start=(b == 0),
                         stop=(b == 1),
                     )
-            zb[n, "one"] = bank
+            zb[first] = bank
 
-        def add_c_one(n):
-            t = zpool.tile([P, 2, P], F32, name="z_one")
+        def add_c(first, size):
+            z = zpool.tile([P, size, 2, P], F32, name="z_s")
             nc.vector.tensor_tensor(
-                out=t[:], in0=zb[n, "one"][:, :2, :], in1=c_t[:, 0, :].rearrange("p (h q) -> p h q", h=2), op=ALU.add
-            )
-            zs[n, "one"] = t
-
-        def silu_store_one(n):
-            o = zpool.tile([P, 2, P], F32, name="o_one")
-            nc.scalar.activation(out=o[:], in_=zs[n, "one"][:], func=ACT.Silu)
-            nc.sync.dma_start(out=out[n].rearrange("(m h) q -> m (h q)", h=2), in_=o[:].rearrange("p h q -> p (h q)"))
-
-        def quantize_t(pair):
-            q = tpool.tile([P, 512], U32, name="t_q", align_bytes=64)
-            sc = tpool.tile([P, 512], U8, name="t_s", align_bytes=64)
-            nc.vector.quantize_mx(out=q[:].bitcast(FP8X4), scales=sc[:], in_=tg[pair][:])
-            tcodes[pair] = (q, sc)
-
-        def stage2(pair):
-            bank = ps_z.tile([P, 2, 256], F32, name="z_bank")
-            q, sc = tcodes[pair]
-            for h in range(2):
-                for b in range(2):
-                    acols = slice(128 * (2 * b + h), 128 * (2 * b + h + 1))
-                    tcols = slice(256 * b, 256 * (b + 1))
-                    nc.tensor.matmul_mx(
-                        out=bank[:, h, :],
-                        lhsT=a_codes[:, acols].bitcast(FP8X4),
-                        lhsT_scale=a_scales[:, acols],
-                        rhs=q[:, tcols].bitcast(FP8X4),
-                        rhs_scale=sc[:, tcols],
-                        start=(b == 0),
-                        stop=(b == 1),
-                    )
-            zb[pair] = bank
-
-        def add_c(pair):
-            t = zpool.tile([P, 2, 2, P], F32, name="z_s")
-            nc.vector.tensor_tensor(
-                out=t[:],
-                in0=zb[pair][:].rearrange("p h (n q) -> p n h q", n=2),
-                in1=c_t[:].rearrange("p n (h q) -> p n h q", h=2),
+                out=z[:],
+                in0=zb[first][:].rearrange("p h (n q) -> p n h q", n=size),
+                in1=c_t[:].unsqueeze(1).to_broadcast([P, size, 2, P]),
                 op=ALU.add,
             )
-            zs[pair] = t
+            zs[first] = z
 
-        def silu_store(pair):
-            o = zpool.tile([P, 2, 256], F32, name="o_t")
-            nc.scalar.activation(out=o[:].rearrange("p n (h q) -> p n h q", h=2), in_=zs[pair][:], func=ACT.Silu)
-            nc.sync.dma_start(out=out[2 * pair : 2 * pair + 2].rearrange("n (m h) q -> m n (h q)", h=2), in_=o[:])
+        def silu_store(first, size):
+            o = zpool.tile([P, size, 2, P], F32, name="o_t")
+            nc.scalar.activation(out=o[:], in_=zs[first][:], func=ACT.Silu)
+            nc.sync.dma_start(
+                out=out[first : first + size].rearrange("n (m h) q -> m n (h q)", h=2), in_=o[:].rearrange("p n h q -> p n (h q)")
+            )
 
-        def prepare_a():
-            for b in range(2):
-                bank = ps_s.tile([P, 4, P], F32, name="s_bank")
-                w = a_raw[:, b, :].bitcast(F32)
-                for h in range(2):
-                    for u in range(2):
-                        nc.tensor.transpose(bank[:, 2 * h + u, :], w[:, 256 * h + u : 256 * (h + 1) : 2], ident[:])
-                dst = a_grp[:].bitcast(F32)[:, 512 * b : 512 * (b + 1)].rearrange("p (h m u) -> p h m u", h=2, u=2)
-                src = bank[:].rearrange("p (h u) m -> p h m u", h=2)
-                if b < 2:
-                    nc.scalar.copy(out=dst, in_=src)
-                else:
-                    nc.vector.tensor_copy(out=dst, in_=src)
+        PAIRS = NB - 2
 
-        def quantize_a():
-            nc.vector.quantize_mx(out=a_codes[:].bitcast(FP8X4), scales=a_scales[:], in_=a_grp[:])
+        def group(k):
+            return (k - k % 2, 2) if k < PAIRS else (k, 1)
 
-        interleave_b(1, b2_w)
-        interleave_b(0, b1_raw)
-        quantize_b(1)
-        quantize_b(0)
-        for j in range(NB - 1):
-            if j:
+        def product_and_unload(k, b, eng="S"):
+            first_product(k, b)
+            unload_t(k, b, *group(k), eng)
+
+        reorder_b(0, b1_raw)
+        for i in range(8):
+            widen_b2(i // 4, i % 4, "V" if i < 4 else "S")
+        for s in range(2):
+            gather_upper(0, s, s + 1)
+            close_lower(0, s, s + 1)
+            turn_x(0, s)
+        unload_b(0, "V")
+        reorder_b(1, b2_w)
+        gather_upper(0, 2, 4)
+        unload_x(0, 0, "S")
+        close_lower(0, 2, 4)
+        unload_x(0, 1, "S")
+        turn_x(0, 2)
+        turn_x(0, 3)
+        gather_upper(1, 0, 2)
+        unload_b(1, "S")
+        close_lower(1, 0, 2)
+        quantize_x(0, 0)
+        unload_x(0, 2, "S")
+        unload_x(0, 3, "S")
+        gather_upper(1, 2, 4)
+        close_lower(1, 2, 4)
+        quantize_b()
+        quantize_x(0, 1)
+
+
+        for j in range(1, NB):
+            last = j == NB - 1
+            if j in (3, 4):
+                turn_a(j - 3)
+                unload_a(j - 3, "S")
+            for s in range(4):
+                turn_x(j, s)
+            if not last:
+                gather_upper(j + 1, 0, 4)
+            unload_x(j, 0, "S" if j in (1, 6, 11) else "V")
+            unload_x(j, 1, "S")
+            if not last:
+                close_lower(j + 1, 0, 4)
+            if j > 3:
                 quantize_x(j - 1, 1)
+            unload_x(j, 2, "V" if last else "S")
+            unload_x(j, 3, "S")
             if j == 4:
                 quantize_a()
-            for s in range(4):
-                transposes(j, s)
-                warm_tensor(DUMMY.get((j, s), 0))
-            unload(j, 0, "S")
-            unload(j, 1, "S")
-            if j + 1 < NB:
-                permute(j + 1)
-            unload(j, 2, "S")
-            if not CV[j % 4]:
-                unload(j, 3, "S")
-            if j >= 7 and j % 2:
-                silu_store((j - 7) // 2)
-            if j == 2:
-                prepare_a()
             if j >= 4 and j % 2 == 0:
-                quantize_t((j - 4) // 2)
-            if CV[j % 4]:
-                unload(j, 3, "V")
-            quantize_x(j, 0)
-            if j >= 5 and j % 2:
-                stage2((j - 5) // 2)
-            k = 0 if j == 1 else j - 2
-            if k >= 0 and j != 2:
-                stage1(k)
-                unload1(k, 0, "S")
-                unload1(k, 1, "S")
+                quantize_t(j - 4, 2)
             if j >= 6 and j % 2 == 0:
-                add_c((j - 6) // 2)
-        quantize_x(14, 1)
-        transposes(15, 0)
-        transposes(15, 1)
-        transposes(15, 2)
-        transposes(15, 3)
-        unload(15, 0, "V")
-        unload(15, 1, "S")
-        unload(15, 2, "V")
-        unload(15, 3, "S")
-        stage1(13)
-        quantize_x(15, 0)
-        unload1(13, 0, "S")
-        quantize_x(15, 1)
-        unload1(13, 1, "S")
-        stage1(14)
-        quantize_t(6)
-        unload1(14, 0, "S")
-        unload1(14, 1, "S")
-        stage1(15, 0)
-        stage2(5)
-        stage1(15, 1)
-        silu_store(4)
-        quantize_t_one(14)
-        add_c(5)
-        unload1(15, 0, "S")
-        stage2_one(14)
-        unload1(15, 1, "V")
-        stage2(6)
-        add_c_one(14)
-        silu_store(5)
-        quantize_t_one(15)
-        add_c(6)
-        silu_store_one(14)
-        stage2_one(15)
-        add_c_one(15)
-        silu_store(6)
-        silu_store_one(15)
+                silu_store(j - 6, 2)
+            quantize_x(j, 0)
+            if j < 3:
+                quantize_x(j, 1)
+            if j >= 5 and j % 2 == 1:
+                second_product(j - 5, 2, ps_z, "z_bank")
+                if not last:
+                    add_c(j - 5, 2)
+            if j < 3:
+                product_and_unload(j - 1, 0)
+                product_and_unload(j - 1, 1)
+            elif j < 5:
+                product_and_unload(2, j - 3)
+            else:
+                product_and_unload(j - 2, 0)
+                product_and_unload(j - 2, 1)
+        quantize_x(NB - 1, 1)
+        product_and_unload(NB - 2, 0)
+        product_and_unload(NB - 2, 1)
+        add_c(NB - 6, 2)
+        quantize_t(NB - 4, 2)
+        silu_store(NB - 6, 2)
+        first_product(NB - 1, 0)
+        first_product(NB - 1, 1)
+        second_product(NB - 4, 2, ps_z, "z_bank")
+        quantize_t(NB - 2, 1)
+        unload_t(NB - 1, 0, NB - 1, 1, "V")
+        unload_t(NB - 1, 1, NB - 1, 1, "S")
+        second_product(NB - 2, 1, ps_t, "t_bank")
+        add_c(NB - 4, 2)
+        quantize_t(NB - 1, 1)
+        silu_store(NB - 4, 2)
+        add_c(NB - 2, 1)
+        second_product(NB - 1, 1, ps_t, "t_bank")
+        silu_store(NB - 2, 1)
+        add_c(NB - 1, 1)
+        silu_store(NB - 1, 1)

@@ -204,7 +204,8 @@ def tile_ranktwokroneckersumlayer_t_kernel(tc, x, b1, b2_bytes, b2_scale, a1, a2
             if n == first and b == 0:
                 tg[first] = tpool.tile([P, 1024 * size], BF16, name="t_g", align_bytes=64)
             lo = 512 * (size * b + n - first)
-            copy(eng, tg[first][:, lo : lo + 512].rearrange("p (q s) -> p q s", s=4), s1[n, b][:].rearrange("p s q -> p q s"))
+            dst = tg[first][:, lo : lo + 512].rearrange("p (q i s) -> p q s i", i=2, s=4)
+            copy(eng, dst, s1[n, b][:].rearrange("p s (q i) -> p q s i", i=2))
 
         def quantize_t(first, size):
             q = tpool.tile([P, 256 * size], U32, name="t_q", align_bytes=64)

@@ -22,11 +22,11 @@ def tile_ranktwokroneckersumlayer_t_kernel(tc, x, b1, b2_bytes, b2_scale, a1, a2
 
     with ExitStack() as ctx:
         keep = ctx.enter_context(tc.tile_pool(name="keep", bufs=1))
-        xpool = ctx.enter_context(tc.tile_pool(name="xpool", bufs=NB))
+        xpool = ctx.enter_context(tc.tile_pool(name="xpool", bufs=7))
         upool = ctx.enter_context(tc.tile_pool(name="upool", bufs=2))
-        gpool = ctx.enter_context(tc.tile_pool(name="gpool", bufs=4))
-        qpool = ctx.enter_context(tc.tile_pool(name="qpool", bufs=6))
-        tpool = ctx.enter_context(tc.tile_pool(name="tpool", bufs=3))
+        gpool = ctx.enter_context(tc.tile_pool(name="gpool", bufs=3))
+        qpool = ctx.enter_context(tc.tile_pool(name="qpool", bufs=4))
+        tpool = ctx.enter_context(tc.tile_pool(name="tpool", bufs=2))
         zpool = ctx.enter_context(tc.tile_pool(name="zpool", bufs=4))
         ps_t = ctx.enter_context(tc.psum_pool(name="ps_t", bufs=4))
         ps_s = ctx.enter_context(tc.psum_pool(name="ps_s", bufs=3))
@@ -52,10 +52,17 @@ def tile_ranktwokroneckersumlayer_t_kernel(tc, x, b1, b2_bytes, b2_scale, a1, a2
         xs = {}
 
         def load_x(n, lo, hi):
-            if n not in xs:
-                xs[n] = xpool.tile([P, 4096], BF16, name="x_t")
+            if n // 2 not in xs:
+                xs[n // 2] = xpool.tile([P, 8192], BF16, name="x_t")
             src = x[n].rearrange("(m s) k -> m (s k)", s=4)
-            nc.sync.dma_start(out=xs[n][:, 1024 * lo : 1024 * hi], in_=src[:, 1024 * lo : 1024 * hi])
+            at = 4096 * (n % 2)
+            nc.sync.dma_start(out=xs[n // 2][:, at + 1024 * lo : at + 1024 * hi], in_=src[:, 1024 * lo : 1024 * hi])
+
+        def load_pair(n):
+            xs[n // 2] = xpool.tile([P, 8192], BF16, name="x_t")
+            nc.sync.dma_start(
+                out=xs[n // 2][:].rearrange("m (n k) -> m n k", n=2), in_=x[n : n + 2].rearrange("n (m s) k -> m n (s k)", s=4)
+            )
 
         nc.sync.dma_start(out=b1_raw[:], in_=b1.rearrange("(g p t) q -> p g t q", g=2, t=4))
         nc.sync.dma_start(out=b2_s[:], in_=b2_scale.rearrange("(g p t) o -> p g (t o)", g=2, t=4))
@@ -63,16 +70,16 @@ def tile_ranktwokroneckersumlayer_t_kernel(tc, x, b1, b2_bytes, b2_scale, a1, a2
         load_x(0, 0, 1)
         load_x(0, 1, 2)
         load_x(0, 2, 4)
-        for n in (1, 2, 3):
+        for n in range(1, 6):
             load_x(n, 0, 2)
             load_x(n, 2, 4)
         nc.sync.dma_start(out=a_raw[:, 0, :], in_=a1.rearrange("(m h) k -> m (h k)", h=2))
-        load_x(4, 0, 4)
         nc.sync.dma_start(out=a_raw[:, 1, :], in_=a2.rearrange("(m h) k -> m (h k)", h=2))
-        load_x(5, 0, 4)
+        load_x(6, 0, 4)
+        load_x(7, 0, 4)
         nc.sync.dma_start(out=c_t[:], in_=c.rearrange("(m h) q -> m h q", h=2))
-        for n in range(6, NB):
-            load_x(n, 0, 4)
+        for n in range(8, NB - 2, 2):
+            load_pair(n)
 
         nc.gpsimd.memset(table[:], 0.0)
         make_identity(nc, ident[:])
@@ -147,12 +154,14 @@ def tile_ranktwokroneckersumlayer_t_kernel(tc, x, b1, b2_bytes, b2_scale, a1, a2
             nc.vector.quantize_mx(out=a_codes[:].bitcast(FP8X4), scales=a_scales[:], in_=a_grp[:])
 
         def halves(n, lo, hi):
-            return xs[n][:, 1024 * lo : 1024 * hi].rearrange("p (a r j u w) -> p u a j r w", r=2, j=8, u=2, w=16)
+            at = 4096 * (n % 2)
+            return xs[n // 2][:, at + 1024 * lo : at + 1024 * hi].rearrange("p (a r j u w) -> p u a j r w", r=2, j=8, u=2, w=16)
 
         def gather_upper(n, lo, hi):
-            if lo == 0:
-                upper[n] = upool.tile([P, 2048], BF16, name="x_u")
-            dst = upper[n][:, 512 * lo : 512 * hi].rearrange("p (a j r w) -> p a j r w", j=8, r=2, w=16)
+            if lo == 0 and n % 2 == 0:
+                upper[n // 2] = upool.tile([P, 4096], BF16, name="x_u")
+            at = 2048 * (n % 2)
+            dst = upper[n // 2][:, at + 512 * lo : at + 512 * hi].rearrange("p (a j r w) -> p a j r w", j=8, r=2, w=16)
             nc.vector.tensor_copy(out=dst, in_=halves(n, lo, hi)[:, 1])
 
         def close_lower(n, lo, hi):
@@ -161,33 +170,35 @@ def tile_ranktwokroneckersumlayer_t_kernel(tc, x, b1, b2_bytes, b2_scale, a1, a2
 
         def turn_x(n, s):
             bank = ps_t.tile([P, 4, P], F32, name="t_bank")
-            lower_w = xs[n][:].bitcast(F32)
-            upper_w = upper[n][:].bitcast(F32)
+            lower_w = xs[n // 2][:].bitcast(F32)
+            upper_w = upper[n // 2][:].bitcast(F32)
             for g in range(2):
-                lo = 512 * s + 256 * g
+                lo = 2048 * (n % 2) + 512 * s + 256 * g
                 nc.tensor.transpose(bank[:, 2 * g, :], lower_w[:, lo : lo + P], ident[:])
                 nc.tensor.transpose(bank[:, 2 * g + 1, :], upper_w[:, lo // 2 : lo // 2 + P], ident[:])
             banks[n, s] = bank
 
         def unload_x(n, s, eng):
-            h, s2 = divmod(s, 2)
-            if s2 == 0:
-                grp[n, h] = gpool.tile([P, 2048], BF16, name="x_g", align_bytes=64)
-            dst = grp[n, h][:].bitcast(F32)[:, 512 * s2 : 512 * (s2 + 1)].rearrange("p (g m u) -> p g m u", g=2, u=2)
+            if s == 0:
+                grp[n] = gpool.tile([P, 4096], BF16, name="x_g", align_bytes=64)
+            dst = grp[n][:].bitcast(F32)[:, 512 * s : 512 * (s + 1)].rearrange("p (g m u) -> p g m u", g=2, u=2)
             copy(eng, dst, banks[n, s][:].rearrange("p (g u) m -> p g m u", g=2))
 
-        def quantize_x(n, h):
-            q = qpool.tile([P, 512], U32, name="x_q", align_bytes=64)
-            sc = qpool.tile([P, 512], U8, name="x_s", align_bytes=64)
-            nc.vector.quantize_mx(out=q[:].bitcast(FP8X4), scales=sc[:], in_=grp[n, h][:])
-            codes[n, h] = (q, sc)
+        def quantize_x(n, lo, hi):
+            if lo == 0:
+                q = qpool.tile([P, 1024], U32, name="x_q", align_bytes=64)
+                sc = qpool.tile([P, 1024], U8, name="x_s", align_bytes=64)
+                codes[n] = (q, sc)
+            q, sc = codes[n]
+            cols = slice(256 * lo, 256 * hi)
+            nc.vector.quantize_mx(out=q[:, cols].bitcast(FP8X4), scales=sc[:, cols], in_=grp[n][:, 1024 * lo : 1024 * hi])
 
         def first_product(n, b):
             bank = ps_s.tile([P, 4, P], F32, name="s_bank")
             for s in range(4):
-                q, sc = codes[n, s // 2]
+                q, sc = codes[n]
                 for g in range(2):
-                    cols = slice(256 * (s % 2) + P * g, 256 * (s % 2) + P * (g + 1))
+                    cols = slice(256 * s + P * g, 256 * s + P * (g + 1))
                     bcols = slice(256 * b + P * g, 256 * b + P * (g + 1))
                     nc.tensor.matmul_mx(
                         out=bank[:, s, :],
@@ -213,8 +224,11 @@ def tile_ranktwokroneckersumlayer_t_kernel(tc, x, b1, b2_bytes, b2_scale, a1, a2
             nc.vector.quantize_mx(out=q[:].bitcast(FP8X4), scales=sc[:], in_=tg[first][:])
             tcodes[first] = (q, sc)
 
-        def second_product(first, size, pool, tag):
-            bank = pool.tile([P, 2, P * size], F32, name=tag)
+        def second_product(first, size):
+            if size == 2:
+                bank = ps_z.tile([P, 2, P * size], F32, name="z_bank")
+            else:
+                bank = ps_t.tile([P, 2, P * size], F32, name="t_bank")
             q, sc = tcodes[first]
             for h in range(2):
                 for b in range(2):
@@ -275,54 +289,78 @@ def tile_ranktwokroneckersumlayer_t_kernel(tc, x, b1, b2_bytes, b2_scale, a1, a2
         gather_upper(1, 0, 2)
         unload_b(1, "S")
         close_lower(1, 0, 2)
-        quantize_x(0, 0)
+        quantize_x(0, 0, 2)
         unload_x(0, 2, "S")
         unload_x(0, 3, "S")
         gather_upper(1, 2, 4)
         close_lower(1, 2, 4)
         quantize_b()
-        quantize_x(0, 1)
+        quantize_x(0, 2, 4)
 
 
+        A_STEP = 4
+        WIDE = 8
         for j in range(1, NB):
             last = j == NB - 1
-            if j in (3, 4):
-                turn_a(j - 3)
-                unload_a(j - 3, "S")
+            if j == 2:
+                load_pair(NB - 2)
+            if j == A_STEP + 1:
+                turn_a(1)
+                unload_a(1, "S")
             for s in range(4):
                 turn_x(j, s)
-            if not last:
-                gather_upper(j + 1, 0, 4)
-            unload_x(j, 0, "S" if j in (1, 6, 11) else "V")
-            unload_x(j, 1, "S")
-            if not last:
-                close_lower(j + 1, 0, 4)
-            if j > 3:
-                quantize_x(j - 1, 1)
-            unload_x(j, 2, "V" if last else "S")
-            unload_x(j, 3, "S")
-            if j == 4:
-                quantize_a()
-            if j >= 4 and j % 2 == 0:
-                quantize_t(j - 4, 2)
             if j >= 6 and j % 2 == 0:
-                silu_store(j - 6, 2)
-            quantize_x(j, 0)
-            if j < 3:
-                quantize_x(j, 1)
-            if j >= 5 and j % 2 == 1:
-                second_product(j - 5, 2, ps_z, "z_bank")
-                if not last:
-                    add_c(j - 5, 2)
-            if j < 3:
+                add_c(j - 6, 2)
+            ahead = 4 if j + 1 < WIDE else 8 if j % 2 == 1 and not last else 0
+            if j <= A_STEP:
+                gather_upper(j + 1, 0, 2)
+                unload_x(j, 0, "S" if j == 1 else "V")
+                close_lower(j + 1, 0, 2)
+                unload_x(j, 1, "S")
+                unload_x(j, 2, "S")
+                unload_x(j, 3, "S")
+                gather_upper(j + 1, 2, 4)
+                quantize_x(j, 0, 2)
+                close_lower(j + 1, 2, 4)
+                if j < A_STEP:
+                    quantize_x(j, 2, 4)
+            else:
+                if ahead:
+                    gather_upper(j + 1, 0, ahead)
+                unload_x(j, 0, "S" if j in (6, 11) else "V")
+                unload_x(j, 1, "S")
+                if ahead:
+                    close_lower(j + 1, 0, ahead)
+                if j == A_STEP + 1:
+                    quantize_a()
+                if last:
+                    quantize_x(j - 1, 0, 4)
+                unload_x(j, 2, "V" if last else "S")
+                unload_x(j, 3, "S")
+                if j >= 6 and j % 2 == 0:
+                    silu_store(j - 6, 2)
+                    quantize_t(j - 4, 2)
+                if last:
+                    quantize_x(j, 0, 2)
+                else:
+                    quantize_x(j - 1, 2 if j == A_STEP + 1 else 0, 4)
+            if j == A_STEP:
+                turn_a(0)
+                unload_a(0, "S")
+                quantize_t(0, 2)
+            if j > A_STEP + 1 and j % 2 == 1:
+                second_product(j - 5, 2)
+            if j < A_STEP:
                 product_and_unload(j - 1, 0)
                 product_and_unload(j - 1, 1)
-            elif j < 5:
-                product_and_unload(2, j - 3)
+            elif j < A_STEP + 2:
+                product_and_unload(A_STEP - 1, j - A_STEP)
             else:
                 product_and_unload(j - 2, 0)
                 product_and_unload(j - 2, 1)
-        quantize_x(NB - 1, 1)
+            if j == A_STEP + 1:
+                second_product(0, 2)
+        quantize_x(NB - 1, 2, 4)
         product_and_unload(NB - 2, 0)
         product_and_unload(NB - 2, 1)
         add_c(NB - 6, 2)
@@ -330,16 +368,16 @@ def tile_ranktwokroneckersumlayer_t_kernel(tc, x, b1, b2_bytes, b2_scale, a1, a2
         silu_store(NB - 6, 2)
         first_product(NB - 1, 0)
         first_product(NB - 1, 1)
-        second_product(NB - 4, 2, ps_z, "z_bank")
+        second_product(NB - 4, 2)
         quantize_t(NB - 2, 1)
         unload_t(NB - 1, 0, NB - 1, 1, "V")
         unload_t(NB - 1, 1, NB - 1, 1, "S")
-        second_product(NB - 2, 1, ps_t, "t_bank")
+        second_product(NB - 2, 1)
         add_c(NB - 4, 2)
         quantize_t(NB - 1, 1)
         silu_store(NB - 4, 2)
         add_c(NB - 2, 1)
-        second_product(NB - 1, 1, ps_t, "t_bank")
+        second_product(NB - 1, 1)
         silu_store(NB - 2, 1)
         add_c(NB - 1, 1)
         silu_store(NB - 1, 1)

@@ -85,6 +85,15 @@ def tile_ranktwokroneckersumlayer_t_kernel(tc, x, b1, b2_bytes, b2_scale, a1, a2
         make_identity(nc, ident[:])
         nc.scalar.activation(out=table[:], in_=table[:], func=ACT.Silu)
 
+        zero = keep.tile([P, 512], BF16, name="zero")
+        nc.vector.memset(zero[:], 0.0)
+
+        def warm_tensor(count):
+            for i in range(count):
+                bank = ps_z.tile([P, 512], F32, name="z_bank")
+                nc.tensor.matmul(bank[:], lhsT=zero[:, :P], rhs=zero[:], start=True, stop=True)
+
+        warm_tensor(5)
         nc.vector.memset(pick[:], 0.0)
         for u in range(2):
             for odd in range(2):
@@ -309,6 +318,8 @@ def tile_ranktwokroneckersumlayer_t_kernel(tc, x, b1, b2_bytes, b2_scale, a1, a2
                 unload_a(1, "S")
             for s in range(4):
                 turn_x(j, s)
+                if (j, s) == (1, 1):
+                    warm_tensor(2)
             if j >= 6 and j % 2 == 0:
                 add_c(j - 6, 2)
             ahead = 4 if j + 1 < WIDE else 8 if j % 2 == 1 and not last else 0

@@ -70,15 +70,19 @@ def tile_ranktwokroneckersumlayer_t_kernel(tc, x, b1, b2_bytes, b2_scale, a1, a2
         load_x(0, 0, 1)
         load_x(0, 1, 2)
         load_x(0, 2, 4)
-        for n in range(1, 6):
+        for n in range(1, 3):
             load_x(n, 0, 2)
             load_x(n, 2, 4)
+        for n in range(3, 6):
+            load_x(n, 0, 4)
         nc.sync.dma_start(out=a_raw[:, 0, :], in_=a1.rearrange("(m h) k -> m (h k)", h=2))
         nc.sync.dma_start(out=a_raw[:, 1, :], in_=a2.rearrange("(m h) k -> m (h k)", h=2))
         load_x(6, 0, 4)
         load_x(7, 0, 4)
         nc.sync.dma_start(out=c_t[:], in_=c.rearrange("(m h) q -> m h q", h=2))
-        for n in range(8, NB - 2, 2):
+        load_x(8, 0, 4)
+        load_x(9, 0, 4)
+        for n in range(10, NB - 2, 2):
             load_pair(n)
 
         nc.gpsimd.memset(table[:], 0.0)
@@ -227,17 +231,20 @@ def tile_ranktwokroneckersumlayer_t_kernel(tc, x, b1, b2_bytes, b2_scale, a1, a2
             dst = tg[first][:, lo : lo + 512].rearrange("p (q i s) -> p q s i", i=2, s=4)
             copy(eng, dst, s1[n, b][:].rearrange("p s (q i) -> p q s i", i=2))
 
-        def quantize_t(first, size):
-            q = tpool.tile([P, 256 * size], U32, name="t_q", align_bytes=64)
-            sc = tpool.tile([P, 256 * size], U8, name="t_s", align_bytes=64)
-            nc.vector.quantize_mx(out=q[:].bitcast(FP8X4), scales=sc[:], in_=tg[first][:])
-            tcodes[first] = (q, sc)
+        def quantize_t(first, size, lo=0, hi=2):
+            if lo == 0:
+                q = tpool.tile([P, 256 * size], U32, name="t_q", align_bytes=64)
+                sc = tpool.tile([P, 256 * size], U8, name="t_s", align_bytes=64)
+                tcodes[first] = (q, sc)
+            q, sc = tcodes[first]
+            cols = slice(P * size * lo, P * size * hi)
+            nc.vector.quantize_mx(out=q[:, cols].bitcast(FP8X4), scales=sc[:, cols], in_=tg[first][:, 4 * cols.start : 4 * cols.stop])
 
-        def second_product(first, size):
-            if size == 2:
-                bank = ps_z.tile([P, 2, P * size], F32, name="z_bank")
-            else:
+        def second_product(first, size, late=False):
+            if late:
                 bank = ps_t.tile([P, 2, P * size], F32, name="t_bank")
+            else:
+                bank = ps_z.tile([P, 2, P * size], F32, name="z_bank")
             q, sc = tcodes[first]
             for h in range(2):
                 for b in range(2):
@@ -253,6 +260,33 @@ def tile_ranktwokroneckersumlayer_t_kernel(tc, x, b1, b2_bytes, b2_scale, a1, a2
                         stop=(b == 1),
                     )
             zb[first] = bank
+
+        def last_second_product(n, b):
+            q, sc = tcodes[n]
+            for h in range(2):
+                if b == 0:
+                    zb[n, h] = ps_t.tile([P, P], F32, name="t_bank")
+                acols = slice(P * (2 * b + h), P * (2 * b + h + 1))
+                tcols = slice(P * b, P * (b + 1))
+                nc.tensor.matmul_mx(
+                    out=zb[n, h][:],
+                    lhsT=a_codes[:, acols].bitcast(FP8X4),
+                    lhsT_scale=a_scales[:, acols],
+                    rhs=q[:, tcols].bitcast(FP8X4),
+                    rhs_scale=sc[:, tcols],
+                    start=(b == 0),
+                    stop=(b == 1),
+                )
+
+        def last_add_c(n, h):
+            z = zpool.tile([P, P], F32, name="z_s")
+            nc.vector.tensor_tensor(out=z[:], in0=zb[n, h][:], in1=c_t[:, h, :], op=ALU.add)
+            zs[n, h] = z
+
+        def last_silu_store(n, h):
+            o = zpool.tile([P, P], F32, name="o_t")
+            nc.scalar.activation(out=o[:], in_=zs[n, h][:], func=ACT.Silu)
+            nc.sync.dma_start(out=out[n].rearrange("(m h) q -> h m q", h=2)[h], in_=o[:])
 
         def add_c(first, size):
             z = zpool.tile([P, size, 2, P], F32, name="z_s")
@@ -276,8 +310,7 @@ def tile_ranktwokroneckersumlayer_t_kernel(tc, x, b1, b2_bytes, b2_scale, a1, a2
         def group(k):
             return (k - k % 2, 2) if k < PAIRS else (k, 1)
 
-        def product_and_unload(k, b, eng="S"):
-            first_product(k, b)
+        def unload_product(k, b, eng):
             unload_t(k, b, *group(k), eng)
 
         reorder_b(0, b1_raw)
@@ -309,86 +342,119 @@ def tile_ranktwokroneckersumlayer_t_kernel(tc, x, b1, b2_bytes, b2_scale, a1, a2
 
         A_STEP = 4
         WIDE = 8
-        for j in range(1, NB):
-            last = j == NB - 1
+        for j in range(1, A_STEP + 1):
             if j == 2:
                 load_pair(NB - 2)
-            if j == A_STEP + 1:
-                turn_a(1)
-                unload_a(1, "S")
             for s in range(4):
                 turn_x(j, s)
                 if (j, s) == (1, 1):
                     warm_tensor(2)
-            if j >= 6 and j % 2 == 0:
-                add_c(j - 6, 2)
-            ahead = 4 if j + 1 < WIDE else 8 if j % 2 == 1 and not last else 0
-            if j <= A_STEP:
+            if j == 1:
                 gather_upper(j + 1, 0, 2)
-                unload_x(j, 0, "S" if j == 1 else "V")
+                unload_x(j, 0, "S")
                 close_lower(j + 1, 0, 2)
-                unload_x(j, 1, "S")
-                unload_x(j, 2, "S")
-                unload_x(j, 3, "S")
                 gather_upper(j + 1, 2, 4)
-                quantize_x(j, 0, 2)
-                close_lower(j + 1, 2, 4)
-                if j < A_STEP:
-                    quantize_x(j, 2, 4)
             else:
-                if ahead:
-                    gather_upper(j + 1, 0, ahead)
-                unload_x(j, 0, "S" if j in (6, 11) else "V")
-                unload_x(j, 1, "S")
-                if ahead:
-                    close_lower(j + 1, 0, ahead)
-                if j == A_STEP + 1:
-                    quantize_a()
-                if last:
-                    quantize_x(j - 1, 0, 4)
-                unload_x(j, 2, "V" if last else "S")
-                unload_x(j, 3, "S")
-                if j >= 6 and j % 2 == 0:
-                    silu_store(j - 6, 2)
-                    quantize_t(j - 4, 2)
-                if last:
-                    quantize_x(j, 0, 2)
-                else:
-                    quantize_x(j - 1, 2 if j == A_STEP + 1 else 0, 4)
-            if j == A_STEP:
+                gather_upper(j + 1, 0, 4)
+                unload_x(j, 0, "V")
+                close_lower(j + 1, 0, 4)
+            for s in range(1, 4):
+                unload_x(j, s, "S")
+            quantize_x(j, 0, 2)
+            if j == 1:
+                close_lower(j + 1, 2, 4)
+            if j < A_STEP:
+                quantize_x(j, 2, 4)
+            else:
                 turn_a(0)
                 unload_a(0, "S")
                 quantize_t(0, 2)
-            if j > A_STEP + 1 and j % 2 == 1:
-                second_product(j - 5, 2)
-            if j < A_STEP:
-                product_and_unload(j - 1, 0)
-                product_and_unload(j - 1, 1)
-            elif j < A_STEP + 2:
-                product_and_unload(A_STEP - 1, j - A_STEP)
+            for b in range(2 if j < A_STEP else 1):
+                first_product(j - 1, b)
+                unload_product(j - 1, b, "S")
+
+        j = A_STEP + 1
+        turn_a(1)
+        unload_a(1, "S")
+        gather_upper(j + 1, 0, 4)
+        for s in range(4):
+            turn_x(j, s)
+            unload_x(j, s, "V" if s == 0 else "S")
+        close_lower(j + 1, 0, 4)
+        quantize_x(j - 1, 2, 4)
+        quantize_a()
+        first_product(j - 2, 1)
+
+        for j in range(A_STEP + 2, NB):
+            last = j == NB - 1
+            for s in range(4):
+                turn_x(j, s)
+            late = "S" if j in (6, 7, 12) else "V"
+            if late == "S":
+                unload_product(j - 3, 1, "S")
+            if late == "V":
+                unload_product(j - 3, 1, "V")
+            for s in range(4):
+                unload_x(j, s, "S")
+            if j == WIDE - 2:
+                gather_upper(j + 1, 0, 4)
+                quantize_x(j - 1, 0, 4)
+                close_lower(j + 1, 0, 4)
+                quantize_t(j - 4, 2)
+            elif j == WIDE - 1:
+                gather_upper(j + 1, 0, 4)
+                add_c(0, 2)
+                close_lower(j + 1, 0, 4)
+                gather_upper(j + 2, 0, 4)
+                quantize_x(j - 1, 0, 4)
+                close_lower(j + 2, 0, 4)
+            elif j % 2 == 0:
+                add_c(j - 6, 2)
+                quantize_x(j - 1, 0, 4)
+                if j + 2 < NB:
+                    gather_upper(j + 2, 0, 8)
+                quantize_t(j - 4, 2)
+                if j + 2 < NB:
+                    close_lower(j + 2, 0, 8)
             else:
-                product_and_unload(j - 2, 0)
-                product_and_unload(j - 2, 1)
-            if j == A_STEP + 1:
+                quantize_x(j - 1, 0, 4)
+            first_product(j - 2, 0)
+            unload_product(j - 2, 0, "V" if last else "S")
+            if j == WIDE - 1:
+                silu_store(0, 2)
+            elif j >= WIDE and j % 2 == 0 and j + 2 < NB:
+                silu_store(j - 6, 2)
+            first_product(j - 2, 1)
+            if j == WIDE - 2:
                 second_product(0, 2)
-        quantize_x(NB - 1, 2, 4)
-        product_and_unload(NB - 2, 0)
-        product_and_unload(NB - 2, 1)
-        add_c(NB - 6, 2)
-        quantize_t(NB - 4, 2)
-        silu_store(NB - 6, 2)
-        first_product(NB - 1, 0)
-        first_product(NB - 1, 1)
-        second_product(NB - 4, 2)
-        quantize_t(NB - 2, 1)
-        unload_t(NB - 1, 0, NB - 1, 1, "V")
-        unload_t(NB - 1, 1, NB - 1, 1, "S")
-        second_product(NB - 2, 1)
-        add_c(NB - 4, 2)
-        quantize_t(NB - 1, 1)
-        silu_store(NB - 4, 2)
-        add_c(NB - 2, 1)
-        second_product(NB - 1, 1)
-        silu_store(NB - 2, 1)
-        add_c(NB - 1, 1)
-        silu_store(NB - 1, 1)
+            if j % 2 == 1:
+                second_product(j - 5, 2)
+        last = NB - 1
+        quantize_x(last, 0, 2)
+        unload_product(last - 2, 1, "S")
+        silu_store(last - 7, 2)
+        quantize_x(last, 2, 4)
+        for b in range(2):
+            first_product(last - 1, b)
+            unload_product(last - 1, b, "S")
+        add_c(last - 5, 2)
+        quantize_t(last - 3, 2)
+        first_product(last, 0)
+        first_product(last, 1)
+        silu_store(last - 5, 2)
+        second_product(last - 3, 2)
+        quantize_t(last - 1, 1)
+        unload_product(last, 0, "V")
+        unload_product(last, 1, "S")
+        second_product(last - 1, 1, True)
+        add_c(last - 3, 2)
+        quantize_t(last, 1, 0, 1)
+        last_second_product(last, 0)
+        quantize_t(last, 1, 1, 2)
+        last_second_product(last, 1)
+        silu_store(last - 3, 2)
+        add_c(last - 1, 1)
+        silu_store(last - 1, 1)
+        for h in range(2):
+            last_add_c(last, h)
+            last_silu_store(last, h)

@@ -7,6 +7,7 @@ FLOPS = 2 * 16 * 512 * 1024 * 256 + 2 * 2 * 16 * 256 * 512 * 128
 
 P = 128
 NB = 16
+WIDE = 8
 F32 = mybir.dt.float32
 BF16 = mybir.dt.bfloat16
 U32 = mybir.dt.uint32
@@ -27,7 +28,7 @@ def tile_ranktwokroneckersumlayer_t_kernel(tc, x, b1, b2_bytes, b2_scale, a1, a2
         gpool = ctx.enter_context(tc.tile_pool(name="gpool", bufs=3))
         qpool = ctx.enter_context(tc.tile_pool(name="qpool", bufs=4))
         tpool = ctx.enter_context(tc.tile_pool(name="tpool", bufs=2))
-        zpool = ctx.enter_context(tc.tile_pool(name="zpool", bufs=4))
+        zpool = ctx.enter_context(tc.tile_pool(name="zpool", bufs=5))
         ps_t = ctx.enter_context(tc.psum_pool(name="ps_t", bufs=4))
         ps_s = ctx.enter_context(tc.psum_pool(name="ps_s", bufs=3))
         ps_z = ctx.enter_context(tc.psum_pool(name="ps_z", bufs=1))
@@ -70,10 +71,9 @@ def tile_ranktwokroneckersumlayer_t_kernel(tc, x, b1, b2_bytes, b2_scale, a1, a2
         load_x(0, 0, 1)
         load_x(0, 1, 2)
         load_x(0, 2, 4)
-        for n in range(1, 3):
-            load_x(n, 0, 2)
-            load_x(n, 2, 4)
-        for n in range(3, 6):
+        load_x(1, 0, 2)
+        load_x(1, 2, 4)
+        for n in range(2, 6):
             load_x(n, 0, 4)
         nc.sync.dma_start(out=a_raw[:, 0, :], in_=a1.rearrange("(m h) k -> m (h k)", h=2))
         nc.sync.dma_start(out=a_raw[:, 1, :], in_=a2.rearrange("(m h) k -> m (h k)", h=2))
@@ -97,7 +97,7 @@ def tile_ranktwokroneckersumlayer_t_kernel(tc, x, b1, b2_bytes, b2_scale, a1, a2
                 bank = ps_z.tile([P, 512], F32, name="z_bank")
                 nc.tensor.matmul(bank[:], lhsT=zero[:, :P], rhs=zero[:], start=True, stop=True)
 
-        warm_tensor(5)
+        warm_tensor(3)
         nc.vector.memset(pick[:], 0.0)
         for u in range(2):
             for odd in range(2):
@@ -185,10 +185,13 @@ def tile_ranktwokroneckersumlayer_t_kernel(tc, x, b1, b2_bytes, b2_scale, a1, a2
             bank = ps_t.tile([P, 4, P], F32, name="t_bank")
             lower_w = xs[n // 2][:].bitcast(F32)
             upper_w = upper[n // 2][:].bitcast(F32)
+            at = 2048 * (n % 2) + 512 * s
             for g in range(2):
-                lo = 2048 * (n % 2) + 512 * s + 256 * g
+                lo = (at + 256 * g) // 2
+                nc.tensor.transpose(bank[:, 2 * g + 1, :], upper_w[:, lo : lo + P], ident[:])
+            for g in range(2):
+                lo = at + 256 * g
                 nc.tensor.transpose(bank[:, 2 * g, :], lower_w[:, lo : lo + P], ident[:])
-                nc.tensor.transpose(bank[:, 2 * g + 1, :], upper_w[:, lo // 2 : lo // 2 + P], ident[:])
             banks[n, s] = bank
 
         def unload_x(n, s, eng):
@@ -286,7 +289,8 @@ def tile_ranktwokroneckersumlayer_t_kernel(tc, x, b1, b2_bytes, b2_scale, a1, a2
         def last_silu_store(n, h):
             o = zpool.tile([P, P], F32, name="o_t")
             nc.scalar.activation(out=o[:], in_=zs[n, h][:], func=ACT.Silu)
-            nc.sync.dma_start(out=out[n].rearrange("(m h) q -> h m q", h=2)[h], in_=o[:])
+            queue = nc.scalar if h == 1 else nc.sync
+            queue.dma_start(out=out[n].rearrange("(m h) q -> h m q", h=2)[h], in_=o[:])
 
         def add_c(first, size):
             z = zpool.tile([P, size, 2, P], F32, name="z_s")
@@ -341,7 +345,6 @@ def tile_ranktwokroneckersumlayer_t_kernel(tc, x, b1, b2_bytes, b2_scale, a1, a2
 
 
         A_STEP = 4
-        WIDE = 8
         for j in range(1, A_STEP + 1):
             if j == 2:
                 load_pair(NB - 2)
@@ -349,20 +352,12 @@ def tile_ranktwokroneckersumlayer_t_kernel(tc, x, b1, b2_bytes, b2_scale, a1, a2
                 turn_x(j, s)
                 if (j, s) == (1, 1):
                     warm_tensor(2)
-            if j == 1:
-                gather_upper(j + 1, 0, 2)
-                unload_x(j, 0, "S")
-                close_lower(j + 1, 0, 2)
-                gather_upper(j + 1, 2, 4)
-            else:
-                gather_upper(j + 1, 0, 4)
-                unload_x(j, 0, "V")
-                close_lower(j + 1, 0, 4)
+            gather_upper(j + 1, 0, 4)
+            unload_x(j, 0, "S" if j == 1 else "V")
+            close_lower(j + 1, 0, 4)
             for s in range(1, 4):
                 unload_x(j, s, "S")
             quantize_x(j, 0, 2)
-            if j == 1:
-                close_lower(j + 1, 2, 4)
             if j < A_STEP:
                 quantize_x(j, 2, 4)
             else:
@@ -410,12 +405,18 @@ def tile_ranktwokroneckersumlayer_t_kernel(tc, x, b1, b2_bytes, b2_scale, a1, a2
                 close_lower(j + 2, 0, 4)
             elif j % 2 == 0:
                 add_c(j - 6, 2)
-                quantize_x(j - 1, 0, 4)
-                if j + 2 < NB:
+                if j == WIDE:
+                    quantize_x(j - 1, 0, 4)
                     gather_upper(j + 2, 0, 8)
-                quantize_t(j - 4, 2)
-                if j + 2 < NB:
+                    quantize_t(j - 4, 2)
                     close_lower(j + 2, 0, 8)
+                else:
+                    if j + 2 < NB:
+                        gather_upper(j + 2, 0, 8)
+                    quantize_x(j - 1, 0, 4)
+                    if j + 2 < NB:
+                        close_lower(j + 2, 0, 8)
+                    quantize_t(j - 4, 2)
             else:
                 quantize_x(j - 1, 0, 4)
             first_product(j - 2, 0)

@@ -8,6 +8,7 @@ FLOPS = 2 * 16 * 512 * 1024 * 256 + 2 * 2 * 16 * 256 * 512 * 128
 P = 128
 NB = 16
 WIDE = 8
+PITCH = 1088
 F32 = mybir.dt.float32
 BF16 = mybir.dt.bfloat16
 U32 = mybir.dt.uint32
@@ -23,8 +24,7 @@ def tile_ranktwokroneckersumlayer_t_kernel(tc, x, b1, b2_bytes, b2_scale, a1, a2
 
     with ExitStack() as ctx:
         keep = ctx.enter_context(tc.tile_pool(name="keep", bufs=1))
-        xpool = ctx.enter_context(tc.tile_pool(name="xpool", bufs=7))
-        upool = ctx.enter_context(tc.tile_pool(name="upool", bufs=2))
+        xpool = ctx.enter_context(tc.tile_pool(name="xpool", bufs=8))
         gpool = ctx.enter_context(tc.tile_pool(name="gpool", bufs=3))
         qpool = ctx.enter_context(tc.tile_pool(name="qpool", bufs=4))
         tpool = ctx.enter_context(tc.tile_pool(name="tpool", bufs=2))
@@ -37,10 +37,10 @@ def tile_ranktwokroneckersumlayer_t_kernel(tc, x, b1, b2_bytes, b2_scale, a1, a2
         ident = keep.tile([P, P], F32, name="ident")
         table = keep.tile([P, 1], F32, name="table")
         pick = keep.tile([P, 2, 2, P], BF16, name="pick")
-        b2_raw = keep.tile([P, 2, 4, P], U8, name="b2_raw")
-        b2_s = keep.tile([P, 2, 4], F32, name="b2_s")
-        b2_w = keep.tile([P, 2, 4, P], BF16, name="b2_w")
-        b1_raw = keep.tile([P, 2, 4, P], BF16, name="b1_raw")
+        b2_raw = keep.tile([P, 4, 2, P], U8, name="b2_raw")
+        b2_s = keep.tile([P, 4, 2], F32, name="b2_s")
+        b2_w = keep.tile([P, 4, 2, P], BF16, name="b2_w")
+        b1_raw = keep.tile([P, 4, 2, P], BF16, name="b1_raw")
         b_grp = keep.tile([P, 2048], BF16, name="b_grp", align_bytes=64)
         b_codes = keep.tile([P, 512], U32, name="b_codes", align_bytes=64)
         b_scales = keep.tile([P, 512], U8, name="b_scales", align_bytes=64)
@@ -52,27 +52,21 @@ def tile_ranktwokroneckersumlayer_t_kernel(tc, x, b1, b2_bytes, b2_scale, a1, a2
 
         xs = {}
 
+        def slots(n):
+            return xs[n // 2][:, 16:].rearrange("p (s u) -> p s u", u=PITCH)
+
         def load_x(n, lo, hi):
             if n // 2 not in xs:
-                xs[n // 2] = xpool.tile([P, 8192], BF16, name="x_t")
-            src = x[n].rearrange("(m s) k -> m (s k)", s=4)
-            at = 4096 * (n % 2)
-            nc.sync.dma_start(out=xs[n // 2][:, at + 1024 * lo : at + 1024 * hi], in_=src[:, 1024 * lo : 1024 * hi])
+                xs[n // 2] = xpool.tile([P, 16 + 8 * PITCH], BF16, name="x_t", align_bytes=64)
+            at = 4 * (n % 2)
+            nc.sync.dma_start(out=slots(n)[:, at + lo : at + hi, 16:1040], in_=x[n].rearrange("(m s) k -> m s k", s=4)[:, lo:hi, :])
 
-        def load_pair(n):
-            xs[n // 2] = xpool.tile([P, 8192], BF16, name="x_t")
-            nc.sync.dma_start(
-                out=xs[n // 2][:].rearrange("m (n k) -> m n k", n=2), in_=x[n : n + 2].rearrange("n (m s) k -> m n (s k)", s=4)
-            )
-
-        nc.sync.dma_start(out=b1_raw[:], in_=b1.rearrange("(g p t) q -> p g t q", g=2, t=4))
-        nc.sync.dma_start(out=b2_s[:], in_=b2_scale.rearrange("(g p t) o -> p g (t o)", g=2, t=4))
-        nc.sync.dma_start(out=b2_raw[:], in_=b2_bytes.rearrange("(g p t) q -> p g t q", g=2, t=4))
-        load_x(0, 0, 1)
-        load_x(0, 1, 2)
-        load_x(0, 2, 4)
-        load_x(1, 0, 2)
-        load_x(1, 2, 4)
+        nc.sync.dma_start(out=b1_raw[:], in_=b1.rearrange("(g p t) q -> p g t q", g=4, t=2))
+        nc.sync.dma_start(out=b2_s[:], in_=b2_scale.rearrange("(g p t) o -> p g (t o)", g=4, t=2))
+        nc.sync.dma_start(out=b2_raw[:], in_=b2_bytes.rearrange("(g p t) q -> p g t q", g=4, t=2))
+        for n in range(2):
+            load_x(n, 0, 2)
+            load_x(n, 2, 4)
         for n in range(2, 6):
             load_x(n, 0, 4)
         nc.sync.dma_start(out=a_raw[:, 0, :], in_=a1.rearrange("(m h) k -> m (h k)", h=2))
@@ -80,10 +74,8 @@ def tile_ranktwokroneckersumlayer_t_kernel(tc, x, b1, b2_bytes, b2_scale, a1, a2
         load_x(6, 0, 4)
         load_x(7, 0, 4)
         nc.sync.dma_start(out=c_t[:], in_=c.rearrange("(m h) q -> m h q", h=2))
-        load_x(8, 0, 4)
-        load_x(9, 0, 4)
-        for n in range(10, NB - 2, 2):
-            load_pair(n)
+        for n in range(8, NB):
+            load_x(n, 0, 4)
 
         nc.gpsimd.memset(table[:], 0.0)
         make_identity(nc, ident[:])
@@ -100,10 +92,10 @@ def tile_ranktwokroneckersumlayer_t_kernel(tc, x, b1, b2_bytes, b2_scale, a1, a2
         warm_tensor(3)
         nc.vector.memset(pick[:], 0.0)
         for u in range(2):
-            for odd in range(2):
+            for r in range(2):
                 nc.vector.tensor_copy(
-                    out=pick[:, u, odd, :].rearrange("p (j r i o) -> p j r i o", r=2, i=4, o=2)[:, :, :, :, odd],
-                    in_=ident[:].rearrange("p (r j u i) -> p u j r i", r=2, u=2, i=4)[:, u],
+                    out=pick[:, u, r, :].rearrange("p (j o i) -> p j o i", o=2, i=8)[:, :, 1 - r, :],
+                    in_=ident[:].rearrange("p (j o i) -> p j o i", o=2, i=8)[:, :, u if r == 0 else 1 - u, :],
                 )
 
         def widen_b2(g, t, eng):
@@ -115,7 +107,6 @@ def tile_ranktwokroneckersumlayer_t_kernel(tc, x, b1, b2_bytes, b2_scale, a1, a2
             else:
                 nc.scalar.activation(out=b2_w[:, g, t, :], in_=src, func=ACT.Copy, scale=b2_s[:, g, t : t + 1])
 
-        upper = {}
         banks = {}
         grp = {}
         codes = {}
@@ -135,13 +126,13 @@ def tile_ranktwokroneckersumlayer_t_kernel(tc, x, b1, b2_bytes, b2_scale, a1, a2
             bank = ps_s.tile([P, 2, P, 2, 2], BF16, name="s_bank")
             for g in range(2):
                 for u in range(2):
-                    for odd in range(2):
+                    for r in range(2):
                         nc.tensor.matmul(
                             bank[:, g, :, u, :],
-                            lhsT=pick[:, u, odd, :],
-                            rhs=src[:, g, 2 * odd : 2 * odd + 2, :].rearrange("p e q -> p q e"),
-                            start=(odd == 0),
-                            stop=(odd == 1),
+                            lhsT=pick[:, u, r, :],
+                            rhs=src[:, 2 * r + g, :, :].rearrange("p e q -> p q e"),
+                            start=(r == 0),
+                            stop=(r == 1),
                         )
             banks["b", b] = bank
 
@@ -166,32 +157,21 @@ def tile_ranktwokroneckersumlayer_t_kernel(tc, x, b1, b2_bytes, b2_scale, a1, a2
         def quantize_a():
             nc.vector.quantize_mx(out=a_codes[:].bitcast(FP8X4), scales=a_scales[:], in_=a_grp[:])
 
-        def halves(n, lo, hi):
-            at = 4096 * (n % 2)
-            return xs[n // 2][:, at + 1024 * lo : at + 1024 * hi].rearrange("p (a r j u w) -> p u a j r w", r=2, j=8, u=2, w=16)
-
-        def gather_upper(n, lo, hi):
-            if lo == 0 and n % 2 == 0:
-                upper[n // 2] = upool.tile([P, 4096], BF16, name="x_u")
-            at = 2048 * (n % 2)
-            dst = upper[n // 2][:, at + 512 * lo : at + 512 * hi].rearrange("p (a j r w) -> p a j r w", j=8, r=2, w=16)
-            nc.vector.tensor_copy(out=dst, in_=halves(n, lo, hi)[:, 1])
-
-        def close_lower(n, lo, hi):
-            view = halves(n, lo, hi)
-            nc.vector.tensor_copy(out=view[:, 1, :, :, 0, :], in_=view[:, 0, :, :, 1, :])
+        def regroup(n, lo, hi):
+            at = 4 * (n % 2)
+            v = slots(n)[:, at + lo : at + hi, :]
+            src = v[:, :, 32:1056].rearrange("p s (r i t w) -> p s i r t w", r=2, t=2, w=16)[:, :, :, ::-1, 0, :]
+            dst = v.rearrange("p s (r y) -> p s r y", r=2)[:, :, :, :512].rearrange("p s r (i t w) -> p s i r t w", t=2, w=16)[:, :, :, :, 0, :]
+            nc.vector.tensor_copy(out=dst, in_=src)
 
         def turn_x(n, s):
             bank = ps_t.tile([P, 4, P], F32, name="t_bank")
-            lower_w = xs[n // 2][:].bitcast(F32)
-            upper_w = upper[n // 2][:].bitcast(F32)
-            at = 2048 * (n % 2) + 512 * s
+            words = xs[n // 2][:].bitcast(F32)
+            at = 8 + (PITCH // 2) * (4 * (n % 2) + s)
             for g in range(2):
-                lo = (at + 256 * g) // 2
-                nc.tensor.transpose(bank[:, 2 * g + 1, :], upper_w[:, lo : lo + P], ident[:])
-            for g in range(2):
-                lo = at + 256 * g
-                nc.tensor.transpose(bank[:, 2 * g, :], lower_w[:, lo : lo + P], ident[:])
+                for u in range(2):
+                    lo = at + 264 * u + P * g
+                    nc.tensor.transpose(bank[:, 2 * g + u, :], words[:, lo : lo + P], ident[:])
             banks[n, s] = bank
 
         def unload_x(n, s, eng):
@@ -319,42 +299,35 @@ def tile_ranktwokroneckersumlayer_t_kernel(tc, x, b1, b2_bytes, b2_scale, a1, a2
 
         reorder_b(0, b1_raw)
         for i in range(8):
-            widen_b2(i // 4, i % 4, "V" if i < 4 else "S")
+            widen_b2(i // 2, i % 2, "V" if i < 4 else "S")
+        regroup(0, 0, 2)
         for s in range(2):
-            gather_upper(0, s, s + 1)
-            close_lower(0, s, s + 1)
             turn_x(0, s)
         unload_b(0, "V")
         reorder_b(1, b2_w)
-        gather_upper(0, 2, 4)
+        regroup(0, 2, 4)
         unload_x(0, 0, "S")
-        close_lower(0, 2, 4)
         unload_x(0, 1, "S")
         turn_x(0, 2)
         turn_x(0, 3)
-        gather_upper(1, 0, 2)
+        regroup(1, 0, 2)
         unload_b(1, "S")
-        close_lower(1, 0, 2)
         quantize_x(0, 0, 2)
         unload_x(0, 2, "S")
         unload_x(0, 3, "S")
-        gather_upper(1, 2, 4)
-        close_lower(1, 2, 4)
+        regroup(1, 2, 4)
         quantize_b()
         quantize_x(0, 2, 4)
 
 
         A_STEP = 4
         for j in range(1, A_STEP + 1):
-            if j == 2:
-                load_pair(NB - 2)
             for s in range(4):
                 turn_x(j, s)
                 if (j, s) == (1, 1):
                     warm_tensor(2)
-            gather_upper(j + 1, 0, 4)
+            regroup(j + 1, 0, 4)
             unload_x(j, 0, "S" if j == 1 else "V")
-            close_lower(j + 1, 0, 4)
             for s in range(1, 4):
                 unload_x(j, s, "S")
             quantize_x(j, 0, 2)
@@ -371,11 +344,10 @@ def tile_ranktwokroneckersumlayer_t_kernel(tc, x, b1, b2_bytes, b2_scale, a1, a2
         j = A_STEP + 1
         turn_a(1)
         unload_a(1, "S")
-        gather_upper(j + 1, 0, 4)
+        regroup(j + 1, 0, 4)
         for s in range(4):
             turn_x(j, s)
             unload_x(j, s, "V" if s == 0 else "S")
-        close_lower(j + 1, 0, 4)
         quantize_x(j - 1, 2, 4)
         quantize_a()
         first_product(j - 2, 1)
@@ -384,7 +356,7 @@ def tile_ranktwokroneckersumlayer_t_kernel(tc, x, b1, b2_bytes, b2_scale, a1, a2
             last = j == NB - 1
             for s in range(4):
                 turn_x(j, s)
-            late = "S" if j in (6, 7, 12) else "V"
+            late = "V"
             if late == "S":
                 unload_product(j - 3, 1, "S")
             if late == "V":
@@ -392,30 +364,24 @@ def tile_ranktwokroneckersumlayer_t_kernel(tc, x, b1, b2_bytes, b2_scale, a1, a2
             for s in range(4):
                 unload_x(j, s, "S")
             if j == WIDE - 2:
-                gather_upper(j + 1, 0, 4)
+                regroup(j + 1, 0, 4)
                 quantize_x(j - 1, 0, 4)
-                close_lower(j + 1, 0, 4)
                 quantize_t(j - 4, 2)
             elif j == WIDE - 1:
-                gather_upper(j + 1, 0, 4)
+                regroup(j + 1, 0, 4)
                 add_c(0, 2)
-                close_lower(j + 1, 0, 4)
-                gather_upper(j + 2, 0, 4)
+                regroup(j + 2, 0, 4)
                 quantize_x(j - 1, 0, 4)
-                close_lower(j + 2, 0, 4)
             elif j % 2 == 0:
                 add_c(j - 6, 2)
                 if j == WIDE:
                     quantize_x(j - 1, 0, 4)
-                    gather_upper(j + 2, 0, 8)
+                    regroup(j + 2, 0, 8)
                     quantize_t(j - 4, 2)
-                    close_lower(j + 2, 0, 8)
                 else:
                     if j + 2 < NB:
-                        gather_upper(j + 2, 0, 8)
+                        regroup(j + 2, 0, 8)
                     quantize_x(j - 1, 0, 4)
-                    if j + 2 < NB:
-                        close_lower(j + 2, 0, 8)
                     quantize_t(j - 4, 2)
             else:
                 quantize_x(j - 1, 0, 4)

@@ -7,8 +7,10 @@ FLOPS = 2 * 16 * 512 * 1024 * 256 + 2 * 2 * 16 * 256 * 512 * 128
 
 P = 128
 NB = 16
-WIDE = 8
-PITCH = 1088
+PIECE = 16
+PITCH = 134 * PIECE
+HALF_PITCH = 70 * PIECE
+HALVED = 5
 F32 = mybir.dt.float32
 BF16 = mybir.dt.bfloat16
 U32 = mybir.dt.uint32
@@ -24,9 +26,10 @@ def tile_ranktwokroneckersumlayer_t_kernel(tc, x, b1, b2_bytes, b2_scale, a1, a2
 
     with ExitStack() as ctx:
         keep = ctx.enter_context(tc.tile_pool(name="keep", bufs=1))
-        xpool = ctx.enter_context(tc.tile_pool(name="xpool", bufs=8))
+        xpool = ctx.enter_context(tc.tile_pool(name="xpool", bufs=NB - HALVED))
+        hpool = ctx.enter_context(tc.tile_pool(name="hpool", bufs=2 * HALVED))
         gpool = ctx.enter_context(tc.tile_pool(name="gpool", bufs=3))
-        qpool = ctx.enter_context(tc.tile_pool(name="qpool", bufs=4))
+        qpool = ctx.enter_context(tc.tile_pool(name="qpool", bufs=3))
         tpool = ctx.enter_context(tc.tile_pool(name="tpool", bufs=2))
         zpool = ctx.enter_context(tc.tile_pool(name="zpool", bufs=5))
         ps_t = ctx.enter_context(tc.psum_pool(name="ps_t", bufs=4))
@@ -36,6 +39,7 @@ def tile_ranktwokroneckersumlayer_t_kernel(tc, x, b1, b2_bytes, b2_scale, a1, a2
 
         ident = keep.tile([P, P], F32, name="ident")
         table = keep.tile([P, 1], F32, name="table")
+        zero = keep.tile([P, 512], BF16, name="zero")
         pick = keep.tile([P, 2, 2, P], BF16, name="pick")
         b2_raw = keep.tile([P, 4, 2, P], U8, name="b2_raw")
         b2_s = keep.tile([P, 4, 2], F32, name="b2_s")
@@ -51,52 +55,33 @@ def tile_ranktwokroneckersumlayer_t_kernel(tc, x, b1, b2_bytes, b2_scale, a1, a2
         c_t = keep.tile([P, 2, P], BF16, name="c_t")
 
         xs = {}
+        banks = {}
+        grp = {}
+        codes = {}
+        s1 = {}
+        tg = {}
+        tcodes = {}
+        zb = {}
+        zs = {}
 
-        def slots(n):
-            return xs[n // 2][:, 16:].rearrange("p (s u) -> p s u", u=PITCH)
+        def rows(key):
+            return xs[key][:].rearrange("p (d y) -> p d y", d=2)[:, :, PIECE:]
 
-        def load_x(n, lo, hi):
-            if n // 2 not in xs:
-                xs[n // 2] = xpool.tile([P, 16 + 8 * PITCH], BF16, name="x_t", align_bytes=64)
-            at = 4 * (n % 2)
-            nc.sync.dma_start(out=slots(n)[:, at + lo : at + hi, 16:1040], in_=x[n].rearrange("(m s) k -> m s k", s=4)[:, lo:hi, :])
+        def load_x(n):
+            xs[n] = xpool.tile([P, 2 * PITCH], BF16, name="x_t", align_bytes=64)
+            nc.sync.dma_start(out=rows(n)[:, :, PIECE : PIECE + 2048], in_=x[n].rearrange("(m d f) k -> m d (f k)", d=2, f=2))
 
-        nc.sync.dma_start(out=b1_raw[:], in_=b1.rearrange("(g p t) q -> p g t q", g=4, t=2))
-        nc.sync.dma_start(out=b2_s[:], in_=b2_scale.rearrange("(g p t) o -> p g (t o)", g=4, t=2))
-        nc.sync.dma_start(out=b2_raw[:], in_=b2_bytes.rearrange("(g p t) q -> p g t q", g=4, t=2))
-        for n in range(2):
-            load_x(n, 0, 2)
-            load_x(n, 2, 4)
-        for n in range(2, 6):
-            load_x(n, 0, 4)
-        nc.sync.dma_start(out=a_raw[:, 0, :], in_=a1.rearrange("(m h) k -> m (h k)", h=2))
-        nc.sync.dma_start(out=a_raw[:, 1, :], in_=a2.rearrange("(m h) k -> m (h k)", h=2))
-        load_x(6, 0, 4)
-        load_x(7, 0, 4)
-        nc.sync.dma_start(out=c_t[:], in_=c.rearrange("(m h) q -> m h q", h=2))
-        for n in range(8, NB):
-            load_x(n, 0, 4)
+        def load_half(n, f):
+            xs[n, f] = hpool.tile([P, 2 * HALF_PITCH], BF16, name="x_h", align_bytes=64)
+            nc.sync.dma_start(out=rows((n, f))[:, :, PIECE : PIECE + 1024], in_=x[n].rearrange("(m d f) k -> f m d k", d=2, f=2)[f])
 
-        nc.gpsimd.memset(table[:], 0.0)
-        make_identity(nc, ident[:])
-        nc.scalar.activation(out=table[:], in_=table[:], func=ACT.Silu)
-
-        zero = keep.tile([P, 512], BF16, name="zero")
-        nc.vector.memset(zero[:], 0.0)
+        def load_a(b):
+            nc.sync.dma_start(out=a_raw[:, b, :], in_=(a1, a2)[b].rearrange("(m h) k -> m (h k)", h=2))
 
         def warm_tensor(count):
             for i in range(count):
                 bank = ps_z.tile([P, 512], F32, name="z_bank")
                 nc.tensor.matmul(bank[:], lhsT=zero[:, :P], rhs=zero[:], start=True, stop=True)
-
-        warm_tensor(3)
-        nc.vector.memset(pick[:], 0.0)
-        for u in range(2):
-            for r in range(2):
-                nc.vector.tensor_copy(
-                    out=pick[:, u, r, :].rearrange("p (j o i) -> p j o i", o=2, i=8)[:, :, 1 - r, :],
-                    in_=ident[:].rearrange("p (j o i) -> p j o i", o=2, i=8)[:, :, u if r == 0 else 1 - u, :],
-                )
 
         def widen_b2(g, t, eng):
             src = b2_raw[:, g, t, :].bitcast(FP8)
@@ -106,15 +91,6 @@ def tile_ranktwokroneckersumlayer_t_kernel(tc, x, b1, b2_bytes, b2_scale, a1, a2
                 )
             else:
                 nc.scalar.activation(out=b2_w[:, g, t, :], in_=src, func=ACT.Copy, scale=b2_s[:, g, t : t + 1])
-
-        banks = {}
-        grp = {}
-        codes = {}
-        s1 = {}
-        tg = {}
-        tcodes = {}
-        zb = {}
-        zs = {}
 
         def copy(eng, dst, src):
             if eng == "S":
@@ -139,11 +115,12 @@ def tile_ranktwokroneckersumlayer_t_kernel(tc, x, b1, b2_bytes, b2_scale, a1, a2
         def unload_b(b, eng):
             copy(eng, b_grp[:, 1024 * b : 1024 * (b + 1)], banks["b", b][:].rearrange("p g q u e -> p (g q u e)"))
 
-        def quantize_b():
-            nc.vector.quantize_mx(out=b_codes[:].bitcast(FP8X4), scales=b_scales[:], in_=b_grp[:])
+        def quantize_b(b):
+            cols = slice(256 * b, 256 * (b + 1))
+            nc.vector.quantize_mx(out=b_codes[:, cols].bitcast(FP8X4), scales=b_scales[:, cols], in_=b_grp[:, 1024 * b : 1024 * (b + 1)])
 
         def turn_a(b):
-            bank = ps_s.tile([P, 4, P], F32, name="s_bank")
+            bank = ps_t.tile([P, 4, P], F32, name="t_bank")
             w = a_raw[:, b, :].bitcast(F32)
             for h in range(2):
                 for u in range(2):
@@ -157,28 +134,37 @@ def tile_ranktwokroneckersumlayer_t_kernel(tc, x, b1, b2_bytes, b2_scale, a1, a2
         def quantize_a():
             nc.vector.quantize_mx(out=a_codes[:].bitcast(FP8X4), scales=a_scales[:], in_=a_grp[:])
 
-        def regroup(n, lo, hi):
-            at = 4 * (n % 2)
-            v = slots(n)[:, at + lo : at + hi, :]
-            src = v[:, :, 32:1056].rearrange("p s (r i t w) -> p s i r t w", r=2, t=2, w=16)[:, :, :, ::-1, 0, :]
-            dst = v.rearrange("p s (r y) -> p s r y", r=2)[:, :, :, :512].rearrange("p s r (i t w) -> p s i r t w", t=2, w=16)[:, :, :, :, 0, :]
-            nc.vector.tensor_copy(out=dst, in_=src)
+        def stepped(view, w, first, far):
+            view = view[:, :, w * first : w * (first + 2 * far)].rearrange("p d (r y) -> p d r y", r=2)[:, :, :, : 32 * w]
+            return view.rearrange("p d r (i t w) -> p d i r t w", t=2, w=w)[:, :, :, :, 0, :]
 
-        def turn_x(n, s):
+        def regroup(n, f, eng="V", lo=0, hi=16):
+            view, w, engine = rows((n, f) if n < HALVED else n), PIECE, nc.vector
+            if eng == "G":
+                view, w, engine = view.bitcast(U32), PIECE // 2, nc.gpsimd
+            if n < HALVED or f == 0:
+                dst, src = stepped(view, w, 0, 34), stepped(view, w, 2, 32)[:, :, :, ::-1, :]
+            else:
+                dst, src = stepped(view, w, 65, 34)[:, :, ::-1, ::-1, :], stepped(view, w, 65, 32)[:, :, ::-1, :, :]
+            engine.tensor_copy(out=dst[:, :, lo:hi], in_=src[:, :, lo:hi])
+
+        def turn_x(n, o):
+            f, d = divmod(o, 2)
             bank = ps_t.tile([P, 4, P], F32, name="t_bank")
-            words = xs[n // 2][:].bitcast(F32)
-            at = 8 + (PITCH // 2) * (4 * (n % 2) + s)
+            key, pitch = ((n, f), HALF_PITCH) if n < HALVED else (n, PITCH)
+            windows = (0, 33) if n < HALVED or f == 0 else (98, 65)
+            words = xs[key][:].bitcast(F32)
             for g in range(2):
                 for u in range(2):
-                    lo = at + 264 * u + P * g
+                    lo = (pitch * d + PIECE * (1 + windows[u] + 16 * g)) // 2
                     nc.tensor.transpose(bank[:, 2 * g + u, :], words[:, lo : lo + P], ident[:])
-            banks[n, s] = bank
+            banks[n, o] = bank
 
-        def unload_x(n, s, eng):
-            if s == 0:
+        def unload_x(n, o, eng):
+            if n not in grp:
                 grp[n] = gpool.tile([P, 4096], BF16, name="x_g", align_bytes=64)
-            dst = grp[n][:].bitcast(F32)[:, 512 * s : 512 * (s + 1)].rearrange("p (g m u) -> p g m u", g=2, u=2)
-            copy(eng, dst, banks[n, s][:].rearrange("p (g u) m -> p g m u", g=2))
+            dst = grp[n][:].bitcast(F32)[:, 512 * o : 512 * (o + 1)].rearrange("p (g m u) -> p g m u", g=2, u=2)
+            copy(eng, dst, banks[n, o][:].rearrange("p (g u) m -> p g m u", g=2))
 
         def quantize_x(n, lo, hi):
             if lo == 0:
@@ -189,15 +175,17 @@ def tile_ranktwokroneckersumlayer_t_kernel(tc, x, b1, b2_bytes, b2_scale, a1, a2
             cols = slice(256 * lo, 256 * hi)
             nc.vector.quantize_mx(out=q[:, cols].bitcast(FP8X4), scales=sc[:, cols], in_=grp[n][:, 1024 * lo : 1024 * hi])
 
-        def first_product(n, b):
-            bank = ps_s.tile([P, 4, P], F32, name="s_bank")
-            for s in range(4):
-                q, sc = codes[n]
+        def first_product(n, b, lo=0, hi=4, pool=ps_s, tag="s_bank"):
+            if lo == 0:
+                s1[n, b] = pool.tile([P, 4, P], F32, name=tag)
+            q, sc = codes[n]
+            for o in range(lo, hi):
+                f, d = divmod(o, 2)
                 for g in range(2):
-                    cols = slice(256 * s + P * g, 256 * s + P * (g + 1))
+                    cols = slice(256 * o + P * g, 256 * o + P * (g + 1))
                     bcols = slice(256 * b + P * g, 256 * b + P * (g + 1))
                     nc.tensor.matmul_mx(
-                        out=bank[:, s, :],
+                        out=s1[n, b][:, 2 * d + f, :],
                         lhsT=q[:, cols].bitcast(FP8X4),
                         lhsT_scale=sc[:, cols],
                         rhs=b_codes[:, bcols].bitcast(FP8X4),
@@ -205,16 +193,20 @@ def tile_ranktwokroneckersumlayer_t_kernel(tc, x, b1, b2_bytes, b2_scale, a1, a2
                         start=(g == 0),
                         stop=(g == 1),
                     )
-            s1[n, b] = bank
 
-        def unload_t(n, b, first, size, eng):
-            if n == first and b == 0:
+        def group(k):
+            return (k - k % 2, 2) if k < PAIRS else (k, 1)
+
+        def unload_t(n, b, eng):
+            first, size = group(n)
+            if first not in tg:
                 tg[first] = tpool.tile([P, 1024 * size], BF16, name="t_g", align_bytes=64)
             lo = 512 * (size * b + n - first)
             dst = tg[first][:, lo : lo + 512].rearrange("p (q i s) -> p q s i", i=2, s=4)
             copy(eng, dst, s1[n, b][:].rearrange("p s (q i) -> p q s i", i=2))
 
-        def quantize_t(first, size, lo=0, hi=2):
+        def quantize_t(n, lo=0, hi=2):
+            first, size = group(n)
             if lo == 0:
                 q = tpool.tile([P, 256 * size], U32, name="t_q", align_bytes=64)
                 sc = tpool.tile([P, 256 * size], U8, name="t_s", align_bytes=64)
@@ -223,11 +215,9 @@ def tile_ranktwokroneckersumlayer_t_kernel(tc, x, b1, b2_bytes, b2_scale, a1, a2
             cols = slice(P * size * lo, P * size * hi)
             nc.vector.quantize_mx(out=q[:, cols].bitcast(FP8X4), scales=sc[:, cols], in_=tg[first][:, 4 * cols.start : 4 * cols.stop])
 
-        def second_product(first, size, late=False):
-            if late:
-                bank = ps_t.tile([P, 2, P * size], F32, name="t_bank")
-            else:
-                bank = ps_z.tile([P, 2, P * size], F32, name="z_bank")
+        def second_product(n, pool=ps_z, tag="z_bank"):
+            first, size = group(n)
+            bank = pool.tile([P, 2, P * size], F32, name=tag)
             q, sc = tcodes[first]
             for h in range(2):
                 for b in range(2):
@@ -272,7 +262,8 @@ def tile_ranktwokroneckersumlayer_t_kernel(tc, x, b1, b2_bytes, b2_scale, a1, a2
             queue = nc.scalar if h == 1 else nc.sync
             queue.dma_start(out=out[n].rearrange("(m h) q -> h m q", h=2)[h], in_=o[:])
 
-        def add_c(first, size):
+        def add_c(n):
+            first, size = group(n)
             z = zpool.tile([P, size, 2, P], F32, name="z_s")
             nc.vector.tensor_tensor(
                 out=z[:],
@@ -282,146 +273,228 @@ def tile_ranktwokroneckersumlayer_t_kernel(tc, x, b1, b2_bytes, b2_scale, a1, a2
             )
             zs[first] = z
 
-        def silu_store(first, size):
+        def silu_store(n, queue=nc.sync):
+            first, size = group(n)
             o = zpool.tile([P, size, 2, P], F32, name="o_t")
             nc.scalar.activation(out=o[:], in_=zs[first][:], func=ACT.Silu)
-            nc.sync.dma_start(
+            queue.dma_start(
                 out=out[first : first + size].rearrange("n (m h) q -> m n (h q)", h=2), in_=o[:].rearrange("p n h q -> p n (h q)")
             )
 
+        def load_b():
+            nc.sync.dma_start(out=b1_raw[:], in_=b1.rearrange("(g p t) q -> p g t q", g=4, t=2))
+            nc.sync.dma_start(out=b2_s[:], in_=b2_scale.rearrange("(g p t) o -> p g (t o)", g=4, t=2))
+            nc.sync.dma_start(out=b2_raw[:], in_=b2_bytes.rearrange("(g p t) q -> p g t q", g=4, t=2))
+
+        def load_c():
+            nc.sync.dma_start(out=c_t[:], in_=c.rearrange("(m h) q -> m h q", h=2))
+
+        def constants():
+            nc.vector.memset(ident[:], 0.0)
+            make_identity(nc, ident[:], nomemset=True)
+            nc.vector.memset(table[:], 0.0)
+            nc.vector.memset(zero[:], 0.0)
+            nc.scalar.activation(out=table[:], in_=table[:], func=ACT.Silu)
+            nc.vector.memset(pick[:], 0.0)
+            for u in range(2):
+                for r in range(2):
+                    nc.vector.tensor_copy(
+                        out=pick[:, u, r, :].rearrange("p (j o i) -> p j o i", o=2, i=8)[:, :, 1 - r, :],
+                        in_=ident[:].rearrange("p (j o i) -> p j o i", o=2, i=8)[:, :, u if r == 0 else 1 - u, :],
+                    )
+
+        TURN = 6
+        HELP = "G"
+        LEAD = 1
         PAIRS = NB - 2
-
-        def group(k):
-            return (k - k % 2, 2) if k < PAIRS else (k, 1)
-
-        def unload_product(k, b, eng):
-            unload_t(k, b, *group(k), eng)
-
+        load_b()
+        load_half(0, 0)
+        load_a(0)
+        load_half(0, 1)
+        load_a(1)
+        for n in range(1, NB):
+            if n < HALVED:
+                load_half(n, 0)
+                load_half(n, 1)
+            else:
+                load_x(n)
+            if n == 4:
+                load_c()
+        constants()
+        warm_tensor(3)
         reorder_b(0, b1_raw)
         for i in range(8):
-            widen_b2(i // 2, i % 2, "V" if i < 4 else "S")
-        regroup(0, 0, 2)
-        for s in range(2):
-            turn_x(0, s)
-        unload_b(0, "V")
+            widen_b2(i // 2, i % 2, "V" if i < 5 else "S")
+        unload_b(0, "S")
         reorder_b(1, b2_w)
-        regroup(0, 2, 4)
+        regroup(0, 0)
+        quantize_b(0)
+        turn_x(0, 0)
+        turn_x(0, 1)
+        turn_a(0)
+        unload_b(1, "V")
+        regroup(0, 1)
         unload_x(0, 0, "S")
         unload_x(0, 1, "S")
+        unload_a(0, "S")
         turn_x(0, 2)
         turn_x(0, 3)
-        regroup(1, 0, 2)
-        unload_b(1, "S")
+        turn_a(1)
+        quantize_b(1)
         quantize_x(0, 0, 2)
         unload_x(0, 2, "S")
-        unload_x(0, 3, "S")
-        regroup(1, 2, 4)
-        quantize_b()
-        quantize_x(0, 2, 4)
-
-
-        A_STEP = 4
-        for j in range(1, A_STEP + 1):
-            for s in range(4):
-                turn_x(j, s)
-                if (j, s) == (1, 1):
-                    warm_tensor(2)
-            regroup(j + 1, 0, 4)
-            unload_x(j, 0, "S" if j == 1 else "V")
-            for s in range(1, 4):
-                unload_x(j, s, "S")
-            quantize_x(j, 0, 2)
-            if j < A_STEP:
-                quantize_x(j, 2, 4)
-            else:
-                turn_a(0)
-                unload_a(0, "S")
-                quantize_t(0, 2)
-            for b in range(2 if j < A_STEP else 1):
-                first_product(j - 1, b)
-                unload_product(j - 1, b, "S")
-
-        j = A_STEP + 1
-        turn_a(1)
+        unload_x(0, 3, "V")
+        regroup(1, 0)
         unload_a(1, "S")
-        regroup(j + 1, 0, 4)
-        for s in range(4):
-            turn_x(j, s)
-            unload_x(j, s, "V" if s == 0 else "S")
-        quantize_x(j - 1, 2, 4)
-        quantize_a()
-        first_product(j - 2, 1)
-
-        for j in range(A_STEP + 2, NB):
-            last = j == NB - 1
-            for s in range(4):
-                turn_x(j, s)
-            late = "V"
-            if late == "S":
-                unload_product(j - 3, 1, "S")
-            if late == "V":
-                unload_product(j - 3, 1, "V")
-            for s in range(4):
-                unload_x(j, s, "S")
-            if j == WIDE - 2:
-                regroup(j + 1, 0, 4)
-                quantize_x(j - 1, 0, 4)
-                quantize_t(j - 4, 2)
-            elif j == WIDE - 1:
-                regroup(j + 1, 0, 4)
-                add_c(0, 2)
-                regroup(j + 2, 0, 4)
-                quantize_x(j - 1, 0, 4)
-            elif j % 2 == 0:
-                add_c(j - 6, 2)
-                if j == WIDE:
-                    quantize_x(j - 1, 0, 4)
-                    regroup(j + 2, 0, 8)
-                    quantize_t(j - 4, 2)
-                else:
-                    if j + 2 < NB:
-                        regroup(j + 2, 0, 8)
-                    quantize_x(j - 1, 0, 4)
-                    quantize_t(j - 4, 2)
-            else:
-                quantize_x(j - 1, 0, 4)
-            first_product(j - 2, 0)
-            unload_product(j - 2, 0, "V" if last else "S")
-            if j == WIDE - 1:
-                silu_store(0, 2)
-            elif j >= WIDE and j % 2 == 0 and j + 2 < NB:
-                silu_store(j - 6, 2)
-            first_product(j - 2, 1)
-            if j == WIDE - 2:
-                second_product(0, 2)
-            if j % 2 == 1:
-                second_product(j - 5, 2)
-        last = NB - 1
-        quantize_x(last, 0, 2)
-        unload_product(last - 2, 1, "S")
-        silu_store(last - 7, 2)
-        quantize_x(last, 2, 4)
         for b in range(2):
-            first_product(last - 1, b)
-            unload_product(last - 1, b, "S")
-        add_c(last - 5, 2)
-        quantize_t(last - 3, 2)
-        first_product(last, 0)
-        first_product(last, 1)
-        silu_store(last - 5, 2)
-        second_product(last - 3, 2)
-        quantize_t(last - 1, 1)
-        unload_product(last, 0, "V")
-        unload_product(last, 1, "S")
-        second_product(last - 1, 1, True)
-        add_c(last - 3, 2)
-        quantize_t(last, 1, 0, 1)
+            first_product(0, b, 0, 2)
+        quantize_x(0, 2, 4)
+        regroup(1, 1)
+        turn_x(1, 0)
+        turn_x(1, 1)
+        unload_x(1, 0, "S")
+        unload_x(1, 1, "V")
+        for b in range(2):
+            first_product(0, b, 2, 4)
+        turn_x(1, 2)
+        turn_x(1, 3)
+        unload_t(0, 0, "S")
+        regroup(2, 0)
+        quantize_x(1, 0, 2)
+        unload_x(1, 2, "S")
+        unload_x(1, 3, "S")
+        quantize_a()
+        regroup(2, 1)
+        turn_x(2, 0)
+        turn_x(2, 1)
+        for b in range(2):
+            first_product(1, b, 0, 2)
+        quantize_x(1, 2, 4)
+        turn_x(2, 2)
+        turn_x(2, 3)
+        regroup(3, 0)
+        unload_x(2, 0, "S")
+        unload_x(2, 1, "S")
+        unload_x(2, 2, "V")
+        unload_t(0, 1, "S")
+        unload_x(2, 3, "S")
+        for b in range(2):
+            first_product(1, b, 2, 4)
+        regroup(3, 1)
+        quantize_x(2, 0, 2)
+        unload_t(1, 0, "S")
+        unload_t(1, 1, "S")
+
+        last = NB - 1
+        for j in range(3, TURN):
+            for o in range(4):
+                turn_x(j, o)
+            if j > 3:
+                unload_t(j - 2, 1, "V")
+            quantize_x(j - 1, 2, 4)
+            if j == 3:
+                quantize_t(j - 3)
+            regroup(j + 1, 0)
+            if j % 2 == 0:
+                add_c(j - 4)
+            elif j > 3:
+                quantize_t(j - 3)
+            for o in range(4):
+                unload_x(j, o, "S")
+            regroup(j + 1, 1)
+            quantize_x(j, 0, 2)
+            if j == TURN - 1:
+                regroup(j + 2, 0)
+            for lo in (0, 2):
+                for b in range(2):
+                    first_product(j - 1, b, lo, lo + 2)
+            unload_t(j - 1, 0, "S")
+            if j % 2 == 0:
+                silu_store(j - 4)
+            else:
+                second_product(j - 3)
+        j = TURN
+        for o in range(4):
+            turn_x(j, o)
+        unload_t(j - 2, 1, "V")
+        regroup(j + 1, 1)
+        for o in range(4):
+            unload_x(j, o, "SV"[o % 2])
+        quantize_x(j - 1, 2, 4)
+        regroup(j + 2, 0)
+        add_c(j - 4)
+        regroup(j + 2, 1)
+        for j in range(TURN + 1, last):
+            for o in range(4):
+                turn_x(j, o)
+            if j > TURN + 1:
+                if j > TURN + 2:
+                    regroup(j + 1, 1, HELP, LEAD, 16)
+                unload_t(j - 3, 1, "V")
+                if j == TURN + 2:
+                    regroup(j + 1, 1)
+            adds = j % 2 == 1 and j > TURN + 1
+            if adds:
+                add_c(j - 5)
+            unload_x(j, 0, "V" if j % 2 == 0 and j > TURN + 2 else "S")
+            if j % 2 == 0:
+                quantize_t(j - 4)
+            quantize_x(j - 1, 0, 4)
+            if j + 2 < NB:
+                if j > TURN + 1:
+                    regroup(j + 2, 1, "V", 0, LEAD)
+                regroup(j + 2, 0)
+            for o in range(1, 4):
+                unload_x(j, o, "S")
+            if j == TURN + 1:
+                for lo in (0, 2):
+                    for b in range(2):
+                        first_product(j - 2, b, lo, lo + 2)
+                unload_t(j - 2, 0, "S")
+            else:
+                first_product(j - 2, 0)
+                unload_t(j - 2, 0, "S")
+                first_product(j - 2, 1)
+            if j % 2 == 1:
+                silu_store(j - 5)
+            if j % 2 == 0:
+                second_product(j - 4)
+
+        for o in range(4):
+            turn_x(last, o)
+        unload_t(last - 3, 1, "V")
+        quantize_x(last - 1, 0, 4)
+        add_c(last - 5)
+        for o in range(4):
+            unload_x(last, o, "S")
+        first_product(last - 2, 0)
+        first_product(last - 2, 1)
+        unload_t(last - 2, 0, "V")
+        quantize_x(last, 0, 2)
+        unload_t(last - 2, 1, "S")
+        quantize_x(last, 2, 4)
+        first_product(last - 1, 0)
+        first_product(last - 1, 1, 0, 4, ps_t, "t_bank")
+        unload_t(last - 1, 0, "S")
+        quantize_t(last - 3)
+        unload_t(last - 1, 1, "S")
+        silu_store(last - 5)
+        for lo in (0, 2):
+            for b in range(2):
+                first_product(last, b, lo, lo + 2)
+        second_product(last - 3)
+        quantize_t(last - 1)
+        second_product(last - 1, ps_t, "t_bank")
+        unload_t(last, 0, "V")
+        unload_t(last, 1, "S")
+        add_c(last - 3)
+        quantize_t(last, 0, 1)
         last_second_product(last, 0)
-        quantize_t(last, 1, 1, 2)
+        quantize_t(last, 1, 2)
         last_second_product(last, 1)
-        silu_store(last - 3, 2)
-        add_c(last - 1, 1)
-        silu_store(last - 1, 1)
+        add_c(last - 1)
+        silu_store(last - 3)
+        silu_store(last - 1)
         for h in range(2):
             last_add_c(last, h)
             last_silu_store(last, h)

@@ -8,8 +8,9 @@ FLOPS = 2 * 16 * 512 * 1024 * 256 + 2 * 2 * 16 * 256 * 512 * 128
 P = 128
 NB = 16
 PIECE = 16
-PITCH = 134 * PIECE
-HALF_PITCH = 70 * PIECE
+PITCH = 70 * PIECE
+WIDE_PITCH = 134 * PIECE
+PLAIN = 10
 HALVED = 5
 F32 = mybir.dt.float32
 BF16 = mybir.dt.bfloat16
@@ -64,15 +65,22 @@ def tile_ranktwokroneckersumlayer_t_kernel(tc, x, b1, b2_bytes, b2_scale, a1, a2
         zb = {}
         zs = {}
 
+        def wide(key):
+            return key in range(HALVED, PLAIN)
+
         def rows(key):
-            return xs[key][:].rearrange("p (d y) -> p d y", d=2)[:, :, PIECE:]
+            return xs[key][:].rearrange("p (d y) -> p d y", y=WIDE_PITCH if wide(key) else PITCH)[:, :, PIECE:]
 
         def load_x(n):
-            xs[n] = xpool.tile([P, 2 * PITCH], BF16, name="x_t", align_bytes=64)
-            nc.sync.dma_start(out=rows(n)[:, :, PIECE : PIECE + 2048], in_=x[n].rearrange("(m d f) k -> m d (f k)", d=2, f=2))
+            if wide(n):
+                xs[n] = xpool.tile([P, 2 * WIDE_PITCH], BF16, name="x_t", align_bytes=64)
+                nc.sync.dma_start(out=rows(n)[:, :, PIECE : PIECE + 2048], in_=x[n].rearrange("(m d f) k -> m d (f k)", d=2, f=2))
+            else:
+                xs[n] = xpool.tile([P, 4 * PITCH], BF16, name="x_t", align_bytes=64)
+                nc.sync.dma_start(out=rows(n)[:, :, PIECE : PIECE + 1024], in_=x[n].rearrange("(m s) k -> m s k", s=4))
 
         def load_half(n, f):
-            xs[n, f] = hpool.tile([P, 2 * HALF_PITCH], BF16, name="x_h", align_bytes=64)
+            xs[n, f] = hpool.tile([P, 2 * PITCH], BF16, name="x_h", align_bytes=64)
             nc.sync.dma_start(out=rows((n, f))[:, :, PIECE : PIECE + 1024], in_=x[n].rearrange("(m d f) k -> f m d k", d=2, f=2)[f])
 
         def load_a(b):
@@ -98,9 +106,11 @@ def tile_ranktwokroneckersumlayer_t_kernel(tc, x, b1, b2_bytes, b2_scale, a1, a2
             else:
                 nc.vector.tensor_copy(out=dst, in_=src)
 
-        def reorder_b(b, src):
-            bank = ps_s.tile([P, 2, P, 2, 2], BF16, name="s_bank")
-            for g in range(2):
+        def reorder_b(b, src, lo=0, hi=2):
+            if lo == 0:
+                banks["b", b] = ps_s.tile([P, 2, P, 2, 2], BF16, name="s_bank")
+            bank = banks["b", b]
+            for g in range(lo, hi):
                 for u in range(2):
                     for r in range(2):
                         nc.tensor.matmul(
@@ -110,7 +120,6 @@ def tile_ranktwokroneckersumlayer_t_kernel(tc, x, b1, b2_bytes, b2_scale, a1, a2
                             start=(r == 0),
                             stop=(r == 1),
                         )
-            banks["b", b] = bank
 
         def unload_b(b, eng):
             copy(eng, b_grp[:, 1024 * b : 1024 * (b + 1)], banks["b", b][:].rearrange("p g q u e -> p (g q u e)"))
@@ -138,25 +147,38 @@ def tile_ranktwokroneckersumlayer_t_kernel(tc, x, b1, b2_bytes, b2_scale, a1, a2
             view = view[:, :, w * first : w * (first + 2 * far)].rearrange("p d (r y) -> p d r y", r=2)[:, :, :, : 32 * w]
             return view.rearrange("p d r (i t w) -> p d i r t w", t=2, w=w)[:, :, :, :, 0, :]
 
-        def regroup(n, f, eng="V", lo=0, hi=16):
-            view, w, engine = rows((n, f) if n < HALVED else n), PIECE, nc.vector
+        def regroup(key, eng="V", lo=0, hi=16):
+            view, w, engine = rows(key), PIECE, nc.vector
             if eng == "G":
                 view, w, engine = view.bitcast(U32), PIECE // 2, nc.gpsimd
-            if n < HALVED or f == 0:
-                dst, src = stepped(view, w, 0, 34), stepped(view, w, 2, 32)[:, :, :, ::-1, :]
-            else:
-                dst, src = stepped(view, w, 65, 34)[:, :, ::-1, ::-1, :], stepped(view, w, 65, 32)[:, :, ::-1, :, :]
+            dst, src = stepped(view, w, 0, 34), stepped(view, w, 2, 32)[:, :, :, ::-1, :]
             engine.tensor_copy(out=dst[:, :, lo:hi], in_=src[:, :, lo:hi])
+
+        def regroup_back(key):
+            view = rows(key)
+            dst, src = stepped(view, PIECE, 65, 34)[:, :, ::-1, ::-1, :], stepped(view, PIECE, 65, 32)[:, :, ::-1, :, :]
+            nc.vector.tensor_copy(out=dst, in_=src)
+
+        def regroup_all(n):
+            if n < HALVED:
+                regroup((n, 0))
+                regroup((n, 1))
+            else:
+                regroup(n)
+                if wide(n):
+                    regroup_back(n)
 
         def turn_x(n, o):
             f, d = divmod(o, 2)
             bank = ps_t.tile([P, 4, P], F32, name="t_bank")
-            key, pitch = ((n, f), HALF_PITCH) if n < HALVED else (n, PITCH)
-            windows = (0, 33) if n < HALVED or f == 0 else (98, 65)
+            key, row = ((n, f), d) if n < HALVED else (n, 2 * d + f)
+            start, windows = PITCH * row, (0, 33)
+            if wide(n):
+                start, windows = WIDE_PITCH * d, ((0, 33), (98, 65))[f]
             words = xs[key][:].bitcast(F32)
             for g in range(2):
                 for u in range(2):
-                    lo = (pitch * d + PIECE * (1 + windows[u] + 16 * g)) // 2
+                    lo = (start + PIECE * (1 + windows[u] + 16 * g)) // 2
                     nc.tensor.transpose(bank[:, 2 * g + u, :], words[:, lo : lo + P], ident[:])
             banks[n, o] = bank
 
@@ -304,21 +326,20 @@ def tile_ranktwokroneckersumlayer_t_kernel(tc, x, b1, b2_bytes, b2_scale, a1, a2
                     )
 
         TURN = 6
-        HELP = "G"
-        LEAD = 1
+        LEAD = 7
+        A_AFTER = 3
         PAIRS = NB - 2
         load_b()
-        load_half(0, 0)
-        load_a(0)
-        load_half(0, 1)
-        load_a(1)
-        for n in range(1, NB):
+        for n in range(NB):
             if n < HALVED:
                 load_half(n, 0)
                 load_half(n, 1)
             else:
                 load_x(n)
-            if n == 4:
+            if n == A_AFTER:
+                load_a(0)
+                load_a(1)
+            if n == 5:
                 load_c()
         constants()
         warm_tensor(3)
@@ -326,139 +347,150 @@ def tile_ranktwokroneckersumlayer_t_kernel(tc, x, b1, b2_bytes, b2_scale, a1, a2
         for i in range(8):
             widen_b2(i // 2, i % 2, "V" if i < 5 else "S")
         unload_b(0, "S")
-        reorder_b(1, b2_w)
-        regroup(0, 0)
+        reorder_b(1, b2_w, 0, 1)
+        regroup((0, 0))
         quantize_b(0)
         turn_x(0, 0)
         turn_x(0, 1)
-        turn_a(0)
-        unload_b(1, "V")
-        regroup(0, 1)
+        reorder_b(1, b2_w, 1, 2)
+        regroup((0, 1))
         unload_x(0, 0, "S")
         unload_x(0, 1, "S")
-        unload_a(0, "S")
+        unload_b(1, "S")
         turn_x(0, 2)
         turn_x(0, 3)
-        turn_a(1)
-        quantize_b(1)
+        regroup((1, 0))
         quantize_x(0, 0, 2)
+        quantize_b(1)
         unload_x(0, 2, "S")
-        unload_x(0, 3, "V")
-        regroup(1, 0)
-        unload_a(1, "S")
+        unload_x(0, 3, "S")
+        turn_x(1, 0)
+        turn_x(1, 1)
+        regroup((1, 1))
+        unload_x(1, 0, "V")
+        unload_x(1, 1, "S")
         for b in range(2):
             first_product(0, b, 0, 2)
         quantize_x(0, 2, 4)
-        regroup(1, 1)
-        turn_x(1, 0)
-        turn_x(1, 1)
-        unload_x(1, 0, "S")
-        unload_x(1, 1, "V")
-        for b in range(2):
-            first_product(0, b, 2, 4)
         turn_x(1, 2)
         turn_x(1, 3)
-        unload_t(0, 0, "S")
-        regroup(2, 0)
+        regroup((2, 0))
         quantize_x(1, 0, 2)
         unload_x(1, 2, "S")
         unload_x(1, 3, "S")
-        quantize_a()
-        regroup(2, 1)
-        turn_x(2, 0)
-        turn_x(2, 1)
         for b in range(2):
-            first_product(1, b, 0, 2)
+            first_product(0, b, 2, 4)
+        regroup((2, 1))
+        unload_t(0, 0, "S")
+        unload_t(0, 1, "V")
+        for o in range(4):
+            turn_x(2, o)
         quantize_x(1, 2, 4)
-        turn_x(2, 2)
-        turn_x(2, 3)
-        regroup(3, 0)
+        regroup((3, 0))
         unload_x(2, 0, "S")
         unload_x(2, 1, "S")
         unload_x(2, 2, "V")
-        unload_t(0, 1, "S")
         unload_x(2, 3, "S")
-        for b in range(2):
-            first_product(1, b, 2, 4)
-        regroup(3, 1)
+        for lo in (0, 2):
+            for b in range(2):
+                first_product(1, b, lo, lo + 2)
+        regroup((3, 1))
         quantize_x(2, 0, 2)
         unload_t(1, 0, "S")
-        unload_t(1, 1, "S")
-
-        last = NB - 1
-        for j in range(3, TURN):
-            for o in range(4):
-                turn_x(j, o)
-            if j > 3:
-                unload_t(j - 2, 1, "V")
-            quantize_x(j - 1, 2, 4)
-            if j == 3:
-                quantize_t(j - 3)
-            regroup(j + 1, 0)
-            if j % 2 == 0:
-                add_c(j - 4)
-            elif j > 3:
-                quantize_t(j - 3)
-            for o in range(4):
-                unload_x(j, o, "S")
-            regroup(j + 1, 1)
-            quantize_x(j, 0, 2)
-            if j == TURN - 1:
-                regroup(j + 2, 0)
-            for lo in (0, 2):
-                for b in range(2):
-                    first_product(j - 1, b, lo, lo + 2)
-            unload_t(j - 1, 0, "S")
-            if j % 2 == 0:
-                silu_store(j - 4)
-            else:
-                second_product(j - 3)
-        j = TURN
+        for o in range(4):
+            turn_x(3, o)
+        unload_t(1, 1, "V")
+        quantize_x(2, 2, 4)
+        unload_x(3, 0, "S")
+        unload_x(3, 1, "S")
+        regroup((4, 0))
+        quantize_t(0)
+        unload_x(3, 2, "S")
+        unload_x(3, 3, "S")
+        quantize_x(3, 0, 2)
+        regroup((4, 1))
+        for b in range(2):
+            first_product(2, b, 0, 2)
+        for b in range(2):
+            turn_a(b)
+        for b in range(2):
+            first_product(2, b, 2, 4)
+        unload_a(0, "S")
+        unload_a(1, "S")
+        unload_t(2, 0, "S")
+        j = 4
         for o in range(4):
             turn_x(j, o)
         unload_t(j - 2, 1, "V")
-        regroup(j + 1, 1)
-        for o in range(4):
-            unload_x(j, o, "SV"[o % 2])
         quantize_x(j - 1, 2, 4)
-        regroup(j + 2, 0)
-        add_c(j - 4)
-        regroup(j + 2, 1)
+        quantize_a()
+        regroup_all(j + 1)
+        for o in range(4):
+            unload_x(j, o, "S")
+        quantize_x(j, 0, 2)
+        for lo in (0, 2):
+            for b in range(2):
+                first_product(j - 1, b, lo, lo + 2)
+        unload_t(j - 1, 0, "S")
+        second_product(0)
+        j = 5
+        for o in range(4):
+            turn_x(j, o)
+        unload_t(j - 2, 1, "V")
+        quantize_x(j - 1, 2, 4)
+        regroup_all(j + 1)
+        add_c(0)
+        quantize_t(2)
+        for o in range(4):
+            unload_x(j, o, "S")
+        quantize_x(j, 0, 2)
+        for lo in (0, 2):
+            for b in range(2):
+                first_product(j - 1, b, lo, lo + 2)
+        unload_t(j - 1, 0, "S")
+
+        last = NB - 1
+        done = 0
+        j = TURN
+        for o in range(4):
+            turn_x(j, o)
+        second_product(j - 4)
+        unload_t(j - 2, 1, "V")
+        quantize_x(j - 1, 2, 4)
+        regroup_all(j + 1)
+        for o in range(4):
+            unload_x(j, o, "S")
+        first_product(j - 1, 0)
+        unload_t(j - 1, 0, "S")
         for j in range(TURN + 1, last):
             for o in range(4):
                 turn_x(j, o)
+            helped = j + 1 >= PLAIN
+            if helped:
+                regroup(j + 1, "G", LEAD, 16)
             if j > TURN + 1:
-                if j > TURN + 2:
-                    regroup(j + 1, 1, HELP, LEAD, 16)
                 unload_t(j - 3, 1, "V")
-                if j == TURN + 2:
-                    regroup(j + 1, 1)
-            adds = j % 2 == 1 and j > TURN + 1
-            if adds:
+            if j % 2 == 1:
                 add_c(j - 5)
-            unload_x(j, 0, "V" if j % 2 == 0 and j > TURN + 2 else "S")
+            unload_x(j, 0, "V" if j % 2 == 0 and helped else "S")
+            if not helped:
+                regroup_all(j + 1)
             if j % 2 == 0:
                 quantize_t(j - 4)
+            if PLAIN <= j + 2 < NB:
+                regroup(j + 2, "V", 0, LEAD)
             quantize_x(j - 1, 0, 4)
-            if j + 2 < NB:
-                if j > TURN + 1:
-                    regroup(j + 2, 1, "V", 0, LEAD)
-                regroup(j + 2, 0)
             for o in range(1, 4):
                 unload_x(j, o, "S")
-            if j == TURN + 1:
-                for lo in (0, 2):
-                    for b in range(2):
-                        first_product(j - 2, b, lo, lo + 2)
-                unload_t(j - 2, 0, "S")
-            else:
+            if j > TURN + 1:
                 first_product(j - 2, 0)
                 unload_t(j - 2, 0, "S")
-                first_product(j - 2, 1)
-            if j % 2 == 1:
-                silu_store(j - 5)
+            first_product(j - 2, 1)
             if j % 2 == 0:
                 second_product(j - 4)
+                for k in range(done, min(done + (2 if j == TURN + 2 else 4), j - 4), 2):
+                    silu_store(k)
+                    done = k + 2
 
         for o in range(4):
             turn_x(last, o)

@@ -27,7 +27,7 @@ def tile_ranktwokroneckersumlayer_t_kernel(tc, x, b1, b2_bytes, b2_scale, a1, a2
 
     with ExitStack() as ctx:
         keep = ctx.enter_context(tc.tile_pool(name="keep", bufs=1))
-        xpool = ctx.enter_context(tc.tile_pool(name="xpool", bufs=NB - HALVED))
+        xpool = ctx.enter_context(tc.tile_pool(name="xpool", bufs=NB - HALVED - 1))
         hpool = ctx.enter_context(tc.tile_pool(name="hpool", bufs=2 * HALVED))
         gpool = ctx.enter_context(tc.tile_pool(name="gpool", bufs=3))
         qpool = ctx.enter_context(tc.tile_pool(name="qpool", bufs=3))
@@ -44,6 +44,7 @@ def tile_ranktwokroneckersumlayer_t_kernel(tc, x, b1, b2_bytes, b2_scale, a1, a2
         pick = keep.tile([P, 2, 2, P], BF16, name="pick")
         b2_raw = keep.tile([P, 4, 2, P], U8, name="b2_raw")
         b2_s = keep.tile([P, 4, 2], F32, name="b2_s")
+        s_rows = keep.tile([P, 256], F32, name="s_rows")
         b2_w = keep.tile([P, 4, 2, P], BF16, name="b2_w")
         b1_raw = keep.tile([P, 4, 2, P], BF16, name="b1_raw")
         b_grp = keep.tile([P, 2048], BF16, name="b_grp", align_bytes=64)
@@ -154,10 +155,12 @@ def tile_ranktwokroneckersumlayer_t_kernel(tc, x, b1, b2_bytes, b2_scale, a1, a2
             dst, src = stepped(view, w, 0, 34), stepped(view, w, 2, 32)[:, :, :, ::-1, :]
             engine.tensor_copy(out=dst[:, :, lo:hi], in_=src[:, :, lo:hi])
 
-        def regroup_back(key):
-            view = rows(key)
-            dst, src = stepped(view, PIECE, 65, 34)[:, :, ::-1, ::-1, :], stepped(view, PIECE, 65, 32)[:, :, ::-1, :, :]
-            nc.vector.tensor_copy(out=dst, in_=src)
+        def regroup_back(key, eng="V", lo=0, hi=16):
+            view, w, engine = rows(key), PIECE, nc.vector
+            if eng == "G":
+                view, w, engine = view.bitcast(U32), PIECE // 2, nc.gpsimd
+            dst, src = stepped(view, w, 65, 34)[:, :, ::-1, ::-1, :], stepped(view, w, 65, 32)[:, :, ::-1, :, :]
+            engine.tensor_copy(out=dst[:, :, lo:hi], in_=src[:, :, lo:hi])
 
         def regroup_all(n):
             if n < HALVED:
@@ -303,10 +306,21 @@ def tile_ranktwokroneckersumlayer_t_kernel(tc, x, b1, b2_bytes, b2_scale, a1, a2
                 out=out[first : first + size].rearrange("n (m h) q -> m n (h q)", h=2), in_=o[:].rearrange("p n h q -> p n (h q)")
             )
 
-        def load_b():
+        def load_b1():
             nc.sync.dma_start(out=b1_raw[:], in_=b1.rearrange("(g p t) q -> p g t q", g=4, t=2))
-            nc.sync.dma_start(out=b2_s[:], in_=b2_scale.rearrange("(g p t) o -> p g (t o)", g=4, t=2))
+
+        def load_scale():
+            nc.vector.memset(s_rows[:], 0.0)
+            nc.sync.dma_start(out=s_rows[0:4, :], in_=b2_scale.rearrange("(g k) o -> g (k o)", g=4))
+
+        def load_b2():
             nc.sync.dma_start(out=b2_raw[:], in_=b2_bytes.rearrange("(g p t) q -> p g t q", g=4, t=2))
+
+        def turn_scale():
+            bank = ps_t.tile([P, 2, P], F32, name="t_bank")
+            for t in range(2):
+                nc.tensor.transpose(bank[:, t, :], s_rows[:, t:256:2], ident[:])
+            nc.vector.tensor_copy(out=b2_s[:], in_=bank[:, :, 0:4].rearrange("p t g -> p g t"))
 
         def load_c():
             nc.sync.dma_start(out=c_t[:], in_=c.rearrange("(m h) q -> m h q", h=2))
@@ -326,13 +340,16 @@ def tile_ranktwokroneckersumlayer_t_kernel(tc, x, b1, b2_bytes, b2_scale, a1, a2
                     )
 
         TURN = 6
-        LEAD = 7
+        LEAD = 4
         A_AFTER = 3
         PAIRS = NB - 2
-        load_b()
+        load_b1()
+        load_scale()
         for n in range(NB):
             if n < HALVED:
                 load_half(n, 0)
+                if n == 0:
+                    load_b2()
                 load_half(n, 1)
             else:
                 load_x(n)
@@ -343,34 +360,34 @@ def tile_ranktwokroneckersumlayer_t_kernel(tc, x, b1, b2_bytes, b2_scale, a1, a2
                 load_c()
         constants()
         warm_tensor(3)
+        turn_scale()
         reorder_b(0, b1_raw)
+        regroup((0, 0))
         for i in range(8):
             widen_b2(i // 2, i % 2, "V" if i < 5 else "S")
         unload_b(0, "S")
-        reorder_b(1, b2_w, 0, 1)
-        regroup((0, 0))
-        quantize_b(0)
         turn_x(0, 0)
         turn_x(0, 1)
-        reorder_b(1, b2_w, 1, 2)
-        regroup((0, 1))
-        unload_x(0, 0, "S")
+        reorder_b(1, b2_w)
+        unload_x(0, 0, "V")
         unload_x(0, 1, "S")
+        regroup((0, 1))
+        quantize_b(0)
         unload_b(1, "S")
         turn_x(0, 2)
         turn_x(0, 3)
-        regroup((1, 0))
         quantize_x(0, 0, 2)
+        first_product(0, 0, 0, 2)
+        regroup((1, 0))
         quantize_b(1)
         unload_x(0, 2, "S")
         unload_x(0, 3, "S")
         turn_x(1, 0)
         turn_x(1, 1)
+        first_product(0, 1, 0, 2)
         regroup((1, 1))
-        unload_x(1, 0, "V")
+        unload_x(1, 0, "S")
         unload_x(1, 1, "S")
-        for b in range(2):
-            first_product(0, b, 0, 2)
         quantize_x(0, 2, 4)
         turn_x(1, 2)
         turn_x(1, 3)
@@ -455,7 +472,6 @@ def tile_ranktwokroneckersumlayer_t_kernel(tc, x, b1, b2_bytes, b2_scale, a1, a2
         for o in range(4):
             turn_x(j, o)
         second_product(j - 4)
-        unload_t(j - 2, 1, "V")
         quantize_x(j - 1, 2, 4)
         regroup_all(j + 1)
         for o in range(4):
@@ -465,16 +481,18 @@ def tile_ranktwokroneckersumlayer_t_kernel(tc, x, b1, b2_bytes, b2_scale, a1, a2
         for j in range(TURN + 1, last):
             for o in range(4):
                 turn_x(j, o)
-            helped = j + 1 >= PLAIN
-            if helped:
+            if j + 1 >= PLAIN:
                 regroup(j + 1, "G", LEAD, 16)
-            if j > TURN + 1:
-                unload_t(j - 3, 1, "V")
+            elif j % 2 == 1:
+                regroup_back(j + 1, "V", 0, 1)
+                regroup(j + 1)
+                regroup_back(j + 1, "G", 1, 16)
+            unload_t(j - 3, 1, "V")
             if j % 2 == 1:
                 add_c(j - 5)
-            unload_x(j, 0, "V" if j % 2 == 0 and helped else "S")
-            if not helped:
+            elif j + 1 < PLAIN:
                 regroup_all(j + 1)
+            unload_x(j, 0, "V" if j % 2 == 0 and j + 1 >= PLAIN else "S")
             if j % 2 == 0:
                 quantize_t(j - 4)
             if PLAIN <= j + 2 < NB:

@@ -44,7 +44,6 @@ def tile_ranktwokroneckersumlayer_t_kernel(tc, x, b1, b2_bytes, b2_scale, a1, a2
         pick = keep.tile([P, 2, 2, P], BF16, name="pick")
         b2_raw = keep.tile([P, 4, 2, P], U8, name="b2_raw")
         b2_s = keep.tile([P, 4, 2], F32, name="b2_s")
-        s_rows = keep.tile([P, 256], F32, name="s_rows")
         b2_w = keep.tile([P, 4, 2, P], BF16, name="b2_w")
         b1_raw = keep.tile([P, 4, 2, P], BF16, name="b1_raw")
         b_grp = keep.tile([P, 2048], BF16, name="b_grp", align_bytes=64)
@@ -310,17 +309,10 @@ def tile_ranktwokroneckersumlayer_t_kernel(tc, x, b1, b2_bytes, b2_scale, a1, a2
             nc.sync.dma_start(out=b1_raw[:], in_=b1.rearrange("(g p t) q -> p g t q", g=4, t=2))
 
         def load_scale():
-            nc.vector.memset(s_rows[:], 0.0)
-            nc.sync.dma_start(out=s_rows[0:4, :], in_=b2_scale.rearrange("(g k) o -> g (k o)", g=4))
+            nc.sync.dma_start(out=b2_s[:], in_=b2_scale.rearrange("(g p t) o -> p g (t o)", g=4, t=2))
 
         def load_b2():
             nc.sync.dma_start(out=b2_raw[:], in_=b2_bytes.rearrange("(g p t) q -> p g t q", g=4, t=2))
-
-        def turn_scale():
-            bank = ps_t.tile([P, 2, P], F32, name="t_bank")
-            for t in range(2):
-                nc.tensor.transpose(bank[:, t, :], s_rows[:, t:256:2], ident[:])
-            nc.vector.tensor_copy(out=b2_s[:], in_=bank[:, :, 0:4].rearrange("p t g -> p g t"))
 
         def load_c():
             nc.sync.dma_start(out=c_t[:], in_=c.rearrange("(m h) q -> m h q", h=2))
@@ -340,15 +332,15 @@ def tile_ranktwokroneckersumlayer_t_kernel(tc, x, b1, b2_bytes, b2_scale, a1, a2
                     )
 
         TURN = 6
-        LEAD = 4
+        LEAD = 5
         A_AFTER = 3
         PAIRS = NB - 2
         load_b1()
-        load_scale()
         for n in range(NB):
             if n < HALVED:
                 load_half(n, 0)
                 if n == 0:
+                    load_scale()
                     load_b2()
                 load_half(n, 1)
             else:
@@ -360,7 +352,6 @@ def tile_ranktwokroneckersumlayer_t_kernel(tc, x, b1, b2_bytes, b2_scale, a1, a2
                 load_c()
         constants()
         warm_tensor(3)
-        turn_scale()
         reorder_b(0, b1_raw)
         regroup((0, 0))
         for i in range(8):
@@ -449,11 +440,11 @@ def tile_ranktwokroneckersumlayer_t_kernel(tc, x, b1, b2_bytes, b2_scale, a1, a2
             for b in range(2):
                 first_product(j - 1, b, lo, lo + 2)
         unload_t(j - 1, 0, "S")
+        unload_t(j - 1, 1, "S")
         second_product(0)
         j = 5
         for o in range(4):
             turn_x(j, o)
-        unload_t(j - 2, 1, "V")
         quantize_x(j - 1, 2, 4)
         regroup_all(j + 1)
         add_c(0)
@@ -475,7 +466,7 @@ def tile_ranktwokroneckersumlayer_t_kernel(tc, x, b1, b2_bytes, b2_scale, a1, a2
         quantize_x(j - 1, 2, 4)
         regroup_all(j + 1)
         for o in range(4):
-            unload_x(j, o, "S")
+            unload_x(j, o, "V" if o == 2 else "S")
         first_product(j - 1, 0)
         unload_t(j - 1, 0, "S")
         for j in range(TURN + 1, last):

@@ -10,7 +10,7 @@ NB = 16
 PIECE = 16
 PITCH = 70 * PIECE
 WIDE_PITCH = 134 * PIECE
-PLAIN = 10
+PLAIN = 12
 HALVED = 5
 F32 = mybir.dt.float32
 BF16 = mybir.dt.bfloat16
@@ -332,7 +332,8 @@ def tile_ranktwokroneckersumlayer_t_kernel(tc, x, b1, b2_bytes, b2_scale, a1, a2
                     )
 
         TURN = 6
-        LEAD = 5
+        LEAD = 6
+        NEAR = 10
         A_AFTER = 3
         PAIRS = NB - 2
         load_b1()
@@ -440,11 +441,11 @@ def tile_ranktwokroneckersumlayer_t_kernel(tc, x, b1, b2_bytes, b2_scale, a1, a2
             for b in range(2):
                 first_product(j - 1, b, lo, lo + 2)
         unload_t(j - 1, 0, "S")
-        unload_t(j - 1, 1, "S")
         second_product(0)
         j = 5
         for o in range(4):
             turn_x(j, o)
+        unload_t(j - 2, 1, "V")
         quantize_x(j - 1, 2, 4)
         regroup_all(j + 1)
         add_c(0)
@@ -466,7 +467,7 @@ def tile_ranktwokroneckersumlayer_t_kernel(tc, x, b1, b2_bytes, b2_scale, a1, a2
         quantize_x(j - 1, 2, 4)
         regroup_all(j + 1)
         for o in range(4):
-            unload_x(j, o, "V" if o == 2 else "S")
+            unload_x(j, o, "S")
         first_product(j - 1, 0)
         unload_t(j - 1, 0, "S")
         for j in range(TURN + 1, last):
@@ -474,16 +475,16 @@ def tile_ranktwokroneckersumlayer_t_kernel(tc, x, b1, b2_bytes, b2_scale, a1, a2
                 turn_x(j, o)
             if j + 1 >= PLAIN:
                 regroup(j + 1, "G", LEAD, 16)
-            elif j % 2 == 1:
+            elif j + 1 >= NEAR:
                 regroup_back(j + 1, "V", 0, 1)
                 regroup(j + 1)
                 regroup_back(j + 1, "G", 1, 16)
             unload_t(j - 3, 1, "V")
             if j % 2 == 1:
                 add_c(j - 5)
-            elif j + 1 < PLAIN:
+            if j + 1 < NEAR:
                 regroup_all(j + 1)
-            unload_x(j, 0, "V" if j % 2 == 0 and j + 1 >= PLAIN else "S")
+            unload_x(j, 0, "V" if j % 2 == 0 and j + 1 >= NEAR else "S")
             if j % 2 == 0:
                 quantize_t(j - 4)
             if PLAIN <= j + 2 < NB:

@@ -8,10 +8,16 @@ FLOPS = 2 * 16 * 512 * 1024 * 256 + 2 * 2 * 16 * 256 * 512 * 128
 P = 128
 NB = 16
 PIECE = 16
-PITCH = 70 * PIECE
-WIDE_PITCH = 134 * PIECE
+FREE = 7
+PITCH = 72 * PIECE
+WIDE_PITCH = 136 * PIECE
+DATA = (FREE + 1) * PIECE
 PLAIN = 12
 HALVED = 5
+T_BANKS = (0, 1, 2, 3)
+S_BANKS = (4, 5, 6)
+Z_BANK = (7,)
+ANY = T_BANKS + S_BANKS
 F32 = mybir.dt.float32
 BF16 = mybir.dt.bfloat16
 U32 = mybir.dt.uint32
@@ -33,27 +39,25 @@ def tile_ranktwokroneckersumlayer_t_kernel(tc, x, b1, b2_bytes, b2_scale, a1, a2
         qpool = ctx.enter_context(tc.tile_pool(name="qpool", bufs=3))
         tpool = ctx.enter_context(tc.tile_pool(name="tpool", bufs=2))
         zpool = ctx.enter_context(tc.tile_pool(name="zpool", bufs=5))
-        ps_t = ctx.enter_context(tc.psum_pool(name="ps_t", bufs=4))
-        ps_s = ctx.enter_context(tc.psum_pool(name="ps_s", bufs=3))
-        ps_z = ctx.enter_context(tc.psum_pool(name="ps_z", bufs=1))
+        psum = ctx.enter_context(tc.psum_pool(name="psum", bufs=1))
         ctx.enter_context(tc.manual_schedule())
 
         ident = keep.tile([P, P], F32, name="ident")
         table = keep.tile([P, 1], F32, name="table")
         zero = keep.tile([P, 512], BF16, name="zero")
         pick = keep.tile([P, 2, 2, P], BF16, name="pick")
-        b2_raw = keep.tile([P, 4, 2, P], U8, name="b2_raw")
+        b2_raw = keep.tile([P, 4, 2, P], U8, name="b2_raw", align_bytes=256)
         b2_s = keep.tile([P, 4, 2], F32, name="b2_s")
         b2_w = keep.tile([P, 4, 2, P], BF16, name="b2_w")
-        b1_raw = keep.tile([P, 4, 2, P], BF16, name="b1_raw")
+        b1_raw = keep.tile([P, 4, 2, P], BF16, name="b1_raw", align_bytes=256)
         b_grp = keep.tile([P, 2048], BF16, name="b_grp", align_bytes=64)
         b_codes = keep.tile([P, 512], U32, name="b_codes", align_bytes=64)
         b_scales = keep.tile([P, 512], U8, name="b_scales", align_bytes=64)
-        a_raw = keep.tile([P, 2, 1024], BF16, name="a_raw")
+        a_raw = keep.tile([P, 2, 1024], BF16, name="a_raw", align_bytes=256)
         a_grp = keep.tile([P, 2048], BF16, name="a_grp", align_bytes=64)
         a_codes = keep.tile([P, 512], U32, name="a_codes", align_bytes=64)
         a_scales = keep.tile([P, 512], U8, name="a_scales", align_bytes=64)
-        c_t = keep.tile([P, 2, P], BF16, name="c_t")
+        c_t = keep.tile([P, 2, P], BF16, name="c_t", align_bytes=256)
 
         xs = {}
         banks = {}
@@ -65,30 +69,40 @@ def tile_ranktwokroneckersumlayer_t_kernel(tc, x, b1, b2_bytes, b2_scale, a1, a2
         zb = {}
         zs = {}
 
+        age = list(range(8))
+
+        def take(among, shape, dtype=F32):
+            k = [i for i in age if i in among][0]
+            age.remove(k)
+            age.append(k)
+            return psum.tile(shape, dtype, name="bank%d" % k)
+
         def wide(key):
             return key in range(HALVED, PLAIN)
 
-        def rows(key):
-            return xs[key][:].rearrange("p (d y) -> p d y", y=WIDE_PITCH if wide(key) else PITCH)[:, :, PIECE:]
+        def rows(key, skip=0):
+            pitch = WIDE_PITCH if wide(key) else PITCH
+            count = 4 if key in range(PLAIN, NB) else 2
+            return xs[key][:, skip * PIECE : skip * PIECE + count * pitch].rearrange("p (d y) -> p d y", y=pitch)
 
         def load_x(n):
             if wide(n):
-                xs[n] = xpool.tile([P, 2 * WIDE_PITCH], BF16, name="x_t", align_bytes=64)
-                nc.sync.dma_start(out=rows(n)[:, :, PIECE : PIECE + 2048], in_=x[n].rearrange("(m d f) k -> m d (f k)", d=2, f=2))
+                xs[n] = xpool.tile([P, 2 * WIDE_PITCH + DATA], BF16, name="x_t", align_bytes=256)
+                nc.sync.dma_start(out=rows(n)[:, :, DATA:], in_=x[n].rearrange("(m d f) k -> m d (f k)", d=2, f=2))
             else:
-                xs[n] = xpool.tile([P, 4 * PITCH], BF16, name="x_t", align_bytes=64)
-                nc.sync.dma_start(out=rows(n)[:, :, PIECE : PIECE + 1024], in_=x[n].rearrange("(m s) k -> m s k", s=4))
+                xs[n] = xpool.tile([P, 4 * PITCH], BF16, name="x_t", align_bytes=256)
+                nc.sync.dma_start(out=rows(n)[:, :, DATA:], in_=x[n].rearrange("(m s) k -> m s k", s=4))
 
         def load_half(n, f):
-            xs[n, f] = hpool.tile([P, 2 * PITCH], BF16, name="x_h", align_bytes=64)
-            nc.sync.dma_start(out=rows((n, f))[:, :, PIECE : PIECE + 1024], in_=x[n].rearrange("(m d f) k -> f m d k", d=2, f=2)[f])
+            xs[n, f] = hpool.tile([P, 2 * PITCH], BF16, name="x_h", align_bytes=256)
+            nc.sync.dma_start(out=rows((n, f))[:, :, DATA:], in_=x[n].rearrange("(m d f) k -> f m d k", d=2, f=2)[f])
 
         def load_a(b):
             nc.sync.dma_start(out=a_raw[:, b, :], in_=(a1, a2)[b].rearrange("(m h) k -> m (h k)", h=2))
 
         def warm_tensor(count):
             for i in range(count):
-                bank = ps_z.tile([P, 512], F32, name="z_bank")
+                bank = take(Z_BANK, [P, 512])
                 nc.tensor.matmul(bank[:], lhsT=zero[:, :P], rhs=zero[:], start=True, stop=True)
 
         def widen_b2(g, t, eng):
@@ -108,10 +122,10 @@ def tile_ranktwokroneckersumlayer_t_kernel(tc, x, b1, b2_bytes, b2_scale, a1, a2
 
         def reorder_b(b, src, lo=0, hi=2):
             if lo == 0:
-                banks["b", b] = ps_s.tile([P, 2, P, 2, 2], BF16, name="s_bank")
+                banks["b", b] = take(S_BANKS, [P, 2, P, 2, 2], BF16)
             bank = banks["b", b]
-            for g in range(lo, hi):
-                for u in range(2):
+            for u in range(2):
+                for g in range(lo, hi):
                     for r in range(2):
                         nc.tensor.matmul(
                             bank[:, g, :, u, :],
@@ -129,7 +143,7 @@ def tile_ranktwokroneckersumlayer_t_kernel(tc, x, b1, b2_bytes, b2_scale, a1, a2
             nc.vector.quantize_mx(out=b_codes[:, cols].bitcast(FP8X4), scales=b_scales[:, cols], in_=b_grp[:, 1024 * b : 1024 * (b + 1)])
 
         def turn_a(b):
-            bank = ps_t.tile([P, 4, P], F32, name="t_bank")
+            bank = take(T_BANKS, [P, 4, P])
             w = a_raw[:, b, :].bitcast(F32)
             for h in range(2):
                 for u in range(2):
@@ -144,21 +158,22 @@ def tile_ranktwokroneckersumlayer_t_kernel(tc, x, b1, b2_bytes, b2_scale, a1, a2
             nc.vector.quantize_mx(out=a_codes[:].bitcast(FP8X4), scales=a_scales[:], in_=a_grp[:])
 
         def stepped(view, w, first, far):
-            view = view[:, :, w * first : w * (first + 2 * far)].rearrange("p d (r y) -> p d r y", r=2)[:, :, :, : 32 * w]
-            return view.rearrange("p d r (i t w) -> p d i r t w", t=2, w=w)[:, :, :, :, 0, :]
+            end = first + far + 31
+            view = view[:, :, w * (end - 2 * far) : w * end].rearrange("p d (r y) -> p d r y", r=2)[:, :, :, (far - 32) * w :]
+            return view.rearrange("p d r (i t w) -> p d i r t w", t=2, w=w)[:, :, :, :, 1, :]
 
         def regroup(key, eng="V", lo=0, hi=16):
             view, w, engine = rows(key), PIECE, nc.vector
             if eng == "G":
                 view, w, engine = view.bitcast(U32), PIECE // 2, nc.gpsimd
-            dst, src = stepped(view, w, 0, 34), stepped(view, w, 2, 32)[:, :, :, ::-1, :]
+            dst, src = stepped(view, w, FREE, 34), stepped(view, w, FREE + 2, 32)[:, :, :, ::-1, :]
             engine.tensor_copy(out=dst[:, :, lo:hi], in_=src[:, :, lo:hi])
 
         def regroup_back(key, eng="V", lo=0, hi=16):
-            view, w, engine = rows(key), PIECE, nc.vector
+            view, w, engine = rows(key, FREE + 1), PIECE, nc.vector
             if eng == "G":
                 view, w, engine = view.bitcast(U32), PIECE // 2, nc.gpsimd
-            dst, src = stepped(view, w, 65, 34)[:, :, ::-1, ::-1, :], stepped(view, w, 65, 32)[:, :, ::-1, :, :]
+            dst, src = stepped(view, w, 64, 34)[:, :, ::-1, ::-1, :], stepped(view, w, 64, 32)[:, :, ::-1, :, :]
             engine.tensor_copy(out=dst[:, :, lo:hi], in_=src[:, :, lo:hi])
 
         def regroup_all(n):
@@ -170,9 +185,9 @@ def tile_ranktwokroneckersumlayer_t_kernel(tc, x, b1, b2_bytes, b2_scale, a1, a2
                 if wide(n):
                     regroup_back(n)
 
-        def turn_x(n, o):
+        def turn_x(n, o, among=T_BANKS):
             f, d = divmod(o, 2)
-            bank = ps_t.tile([P, 4, P], F32, name="t_bank")
+            bank = take(among, [P, 4, P])
             key, row = ((n, f), d) if n < HALVED else (n, 2 * d + f)
             start, windows = PITCH * row, (0, 33)
             if wide(n):
@@ -180,7 +195,7 @@ def tile_ranktwokroneckersumlayer_t_kernel(tc, x, b1, b2_bytes, b2_scale, a1, a2
             words = xs[key][:].bitcast(F32)
             for g in range(2):
                 for u in range(2):
-                    lo = (start + PIECE * (1 + windows[u] + 16 * g)) // 2
+                    lo = (start + PIECE * (FREE + windows[u] + 16 * g)) // 2
                     nc.tensor.transpose(bank[:, 2 * g + u, :], words[:, lo : lo + P], ident[:])
             banks[n, o] = bank
 
@@ -199,9 +214,9 @@ def tile_ranktwokroneckersumlayer_t_kernel(tc, x, b1, b2_bytes, b2_scale, a1, a2
             cols = slice(256 * lo, 256 * hi)
             nc.vector.quantize_mx(out=q[:, cols].bitcast(FP8X4), scales=sc[:, cols], in_=grp[n][:, 1024 * lo : 1024 * hi])
 
-        def first_product(n, b, lo=0, hi=4, pool=ps_s, tag="s_bank"):
+        def first_product(n, b, lo=0, hi=4, among=S_BANKS):
             if lo == 0:
-                s1[n, b] = pool.tile([P, 4, P], F32, name=tag)
+                s1[n, b] = take(among, [P, 4, P])
             q, sc = codes[n]
             for o in range(lo, hi):
                 f, d = divmod(o, 2)
@@ -239,9 +254,9 @@ def tile_ranktwokroneckersumlayer_t_kernel(tc, x, b1, b2_bytes, b2_scale, a1, a2
             cols = slice(P * size * lo, P * size * hi)
             nc.vector.quantize_mx(out=q[:, cols].bitcast(FP8X4), scales=sc[:, cols], in_=tg[first][:, 4 * cols.start : 4 * cols.stop])
 
-        def second_product(n, pool=ps_z, tag="z_bank"):
+        def second_product(n, among=Z_BANK):
             first, size = group(n)
-            bank = pool.tile([P, 2, P * size], F32, name=tag)
+            bank = take(among, [P, 2, P * size])
             q, sc = tcodes[first]
             for h in range(2):
                 for b in range(2):
@@ -262,7 +277,7 @@ def tile_ranktwokroneckersumlayer_t_kernel(tc, x, b1, b2_bytes, b2_scale, a1, a2
             q, sc = tcodes[n]
             for h in range(2):
                 if b == 0:
-                    zb[n, h] = ps_t.tile([P, P], F32, name="t_bank")
+                    zb[n, h] = take(T_BANKS, [P, P])
                 acols = slice(P * (2 * b + h), P * (2 * b + h + 1))
                 tcols = slice(P * b, P * (b + 1))
                 nc.tensor.matmul_mx(
@@ -281,7 +296,7 @@ def tile_ranktwokroneckersumlayer_t_kernel(tc, x, b1, b2_bytes, b2_scale, a1, a2
             zs[n, h] = z
 
         def last_silu_store(n, h):
-            o = zpool.tile([P, P], F32, name="o_t")
+            o = zpool.tile([P, P], F32, name="o_last", bufs=2, align_bytes=256)
             nc.scalar.activation(out=o[:], in_=zs[n, h][:], func=ACT.Silu)
             queue = nc.scalar if h == 1 else nc.sync
             queue.dma_start(out=out[n].rearrange("(m h) q -> h m q", h=2)[h], in_=o[:])
@@ -299,11 +314,21 @@ def tile_ranktwokroneckersumlayer_t_kernel(tc, x, b1, b2_bytes, b2_scale, a1, a2
 
         def silu_store(n, queue=nc.sync):
             first, size = group(n)
-            o = zpool.tile([P, size, 2, P], F32, name="o_t")
+            o = zpool.tile([P, size, 2, P], F32, name="o_t", align_bytes=256)
             nc.scalar.activation(out=o[:], in_=zs[first][:], func=ACT.Silu)
             queue.dma_start(
                 out=out[first : first + size].rearrange("n (m h) q -> m n (h q)", h=2), in_=o[:].rearrange("p n h q -> p n (h q)")
             )
+
+        def add_c_one(first, i):
+            z = zpool.tile([P, 2, P], F32, name="z_s")
+            nc.vector.tensor_tensor(out=z[:], in0=zb[first][:, :, P * i : P * (i + 1)], in1=c_t[:], op=ALU.add)
+            zs[first + i] = z
+
+        def silu_store_one(n):
+            o = zpool.tile([P, 2, P], F32, name="o_t", align_bytes=256)
+            nc.scalar.activation(out=o[:], in_=zs[n][:], func=ACT.Silu)
+            nc.sync.dma_start(out=out[n].rearrange("(m h) q -> m (h q)", h=2), in_=o[:].rearrange("p h q -> p (h q)"))
 
         def load_b1():
             nc.sync.dma_start(out=b1_raw[:], in_=b1.rearrange("(g p t) q -> p g t q", g=4, t=2))
@@ -324,12 +349,12 @@ def tile_ranktwokroneckersumlayer_t_kernel(tc, x, b1, b2_bytes, b2_scale, a1, a2
             nc.vector.memset(zero[:], 0.0)
             nc.scalar.activation(out=table[:], in_=table[:], func=ACT.Silu)
             nc.vector.memset(pick[:], 0.0)
-            for u in range(2):
-                for r in range(2):
-                    nc.vector.tensor_copy(
-                        out=pick[:, u, r, :].rearrange("p (j o i) -> p j o i", o=2, i=8)[:, :, 1 - r, :],
-                        in_=ident[:].rearrange("p (j o i) -> p j o i", o=2, i=8)[:, :, u if r == 0 else 1 - u, :],
-                    )
+            halves = ident[:].rearrange("p (j o i) -> p j o i", o=2, i=8)
+            picks = pick[:].rearrange("p u r (j o i) -> p u r j o i", o=2, i=8)
+            nc.vector.tensor_copy(out=picks[:, 0, 0, :, 1, :], in_=halves[:, :, 0, :])
+            nc.gpsimd.tensor_copy(out=picks[:, 1, 1, :, 0, :].bitcast(U32), in_=picks[:, 0, 0, :, 1, :].bitcast(U32))
+            nc.vector.tensor_copy(out=picks[:, 0, 1, :, 0, :], in_=halves[:, :, 1, :])
+            nc.vector.tensor_copy(out=picks[:, 1, 0, :, 1, :], in_=halves[:, :, 1, :])
 
         TURN = 6
         LEAD = 6
@@ -349,7 +374,7 @@ def tile_ranktwokroneckersumlayer_t_kernel(tc, x, b1, b2_bytes, b2_scale, a1, a2
             if n == A_AFTER:
                 load_a(0)
                 load_a(1)
-            if n == 5:
+            if n == 6:
                 load_c()
         constants()
         warm_tensor(3)
@@ -441,13 +466,15 @@ def tile_ranktwokroneckersumlayer_t_kernel(tc, x, b1, b2_bytes, b2_scale, a1, a2
             for b in range(2):
                 first_product(j - 1, b, lo, lo + 2)
         unload_t(j - 1, 0, "S")
-        second_product(0)
         j = 5
         for o in range(4):
             turn_x(j, o)
-        unload_t(j - 2, 1, "V")
         quantize_x(j - 1, 2, 4)
-        regroup_all(j + 1)
+        regroup_back(j + 1, "V", 0, 1)
+        regroup(j + 1)
+        regroup_back(j + 1, "G", 1, 16)
+        unload_t(j - 2, 1, "V")
+        second_product(0)
         add_c(0)
         quantize_t(2)
         for o in range(4):
@@ -470,7 +497,20 @@ def tile_ranktwokroneckersumlayer_t_kernel(tc, x, b1, b2_bytes, b2_scale, a1, a2
             unload_x(j, o, "S")
         first_product(j - 1, 0)
         unload_t(j - 1, 0, "S")
-        for j in range(TURN + 1, last):
+        j = TURN + 1
+        for o in range(4):
+            turn_x(j, o)
+        quantize_x(j - 1, 0, 2)
+        regroup_back(j + 1, "V", 0, 1)
+        regroup(j + 1)
+        regroup_back(j + 1, "G", 1, 16)
+        unload_t(j - 3, 1, "V")
+        add_c(j - 5)
+        quantize_x(j - 1, 2, 4)
+        for o in range(4):
+            unload_x(j, o, "S")
+        first_product(j - 2, 1)
+        for j in range(TURN + 2, last):
             for o in range(4):
                 turn_x(j, o)
             if j + 1 >= PLAIN:
@@ -516,7 +556,7 @@ def tile_ranktwokroneckersumlayer_t_kernel(tc, x, b1, b2_bytes, b2_scale, a1, a2
         unload_t(last - 2, 1, "S")
         quantize_x(last, 2, 4)
         first_product(last - 1, 0)
-        first_product(last - 1, 1, 0, 4, ps_t, "t_bank")
+        first_product(last - 1, 1, 0, 4, T_BANKS)
         unload_t(last - 1, 0, "S")
         quantize_t(last - 3)
         unload_t(last - 1, 1, "S")
@@ -526,16 +566,18 @@ def tile_ranktwokroneckersumlayer_t_kernel(tc, x, b1, b2_bytes, b2_scale, a1, a2
                 first_product(last, b, lo, lo + 2)
         second_product(last - 3)
         quantize_t(last - 1)
-        second_product(last - 1, ps_t, "t_bank")
+        second_product(last - 1, T_BANKS)
         unload_t(last, 0, "V")
         unload_t(last, 1, "S")
-        add_c(last - 3)
+        add_c_one(last - 3, 0)
         quantize_t(last, 0, 1)
         last_second_product(last, 0)
         quantize_t(last, 1, 2)
         last_second_product(last, 1)
+        add_c_one(last - 3, 1)
         add_c(last - 1)
-        silu_store(last - 3)
+        silu_store_one(last - 3)
+        silu_store_one(last - 2)
         silu_store(last - 1)
         for h in range(2):
             last_add_c(last, h)

@@ -142,8 +142,8 @@ def tile_ranktwokroneckersumlayer_t_kernel(tc, x, b1, b2_bytes, b2_scale, a1, a2
             cols = slice(256 * b, 256 * (b + 1))
             nc.vector.quantize_mx(out=b_codes[:, cols].bitcast(FP8X4), scales=b_scales[:, cols], in_=b_grp[:, 1024 * b : 1024 * (b + 1)])
 
-        def turn_a(b):
-            bank = take(T_BANKS, [P, 4, P])
+        def turn_a(b, among):
+            bank = take(among, [P, 4, P])
             w = a_raw[:, b, :].bitcast(F32)
             for h in range(2):
                 for u in range(2):
@@ -239,7 +239,8 @@ def tile_ranktwokroneckersumlayer_t_kernel(tc, x, b1, b2_bytes, b2_scale, a1, a2
         def unload_t(n, b, eng):
             first, size = group(n)
             if first not in tg:
-                tg[first] = tpool.tile([P, 1024 * size], BF16, name="t_g", align_bytes=64)
+                pool = keep if n == NB - 1 else tpool
+                tg[first] = pool.tile([P, 1024 * size], BF16, name="t_g", align_bytes=64)
             lo = 512 * (size * b + n - first)
             dst = tg[first][:, lo : lo + 512].rearrange("p (q i s) -> p q s i", i=2, s=4)
             copy(eng, dst, s1[n, b][:].rearrange("p s (q i) -> p q s i", i=2))
@@ -247,8 +248,9 @@ def tile_ranktwokroneckersumlayer_t_kernel(tc, x, b1, b2_bytes, b2_scale, a1, a2
         def quantize_t(n, lo=0, hi=2):
             first, size = group(n)
             if lo == 0:
-                q = tpool.tile([P, 256 * size], U32, name="t_q", align_bytes=64)
-                sc = tpool.tile([P, 256 * size], U8, name="t_s", align_bytes=64)
+                pool = keep if n == NB - 1 else tpool
+                q = pool.tile([P, 256 * size], U32, name="t_q", align_bytes=64)
+                sc = pool.tile([P, 256 * size], U8, name="t_s", align_bytes=64)
                 tcodes[first] = (q, sc)
             q, sc = tcodes[first]
             cols = slice(P * size * lo, P * size * hi)
@@ -433,6 +435,7 @@ def tile_ranktwokroneckersumlayer_t_kernel(tc, x, b1, b2_bytes, b2_scale, a1, a2
         unload_t(1, 0, "S")
         for o in range(4):
             turn_x(3, o)
+        turn_a(0, Z_BANK)
         unload_t(1, 1, "V")
         quantize_x(2, 2, 4)
         unload_x(3, 0, "S")
@@ -443,15 +446,13 @@ def tile_ranktwokroneckersumlayer_t_kernel(tc, x, b1, b2_bytes, b2_scale, a1, a2
         unload_x(3, 3, "S")
         quantize_x(3, 0, 2)
         regroup((4, 1))
-        for b in range(2):
-            first_product(2, b, 0, 2)
-        for b in range(2):
-            turn_a(b)
-        for b in range(2):
-            first_product(2, b, 2, 4)
+        for lo in (0, 2):
+            for b in range(2):
+                first_product(2, b, lo, lo + 2)
+        turn_a(1, S_BANKS)
         unload_a(0, "S")
-        unload_a(1, "S")
         unload_t(2, 0, "S")
+        unload_a(1, "S")
         j = 4
         for o in range(4):
             turn_x(j, o)
@@ -510,9 +511,9 @@ def tile_ranktwokroneckersumlayer_t_kernel(tc, x, b1, b2_bytes, b2_scale, a1, a2
         for o in range(4):
             unload_x(j, o, "S")
         first_product(j - 2, 1)
-        for j in range(TURN + 2, last):
+        for j in range(TURN + 2, last - 2):
             for o in range(4):
-                turn_x(j, o)
+                turn_x(j, o, ANY)
             if j + 1 >= PLAIN:
                 regroup(j + 1, "G", LEAD, 16)
             elif j + 1 >= NEAR:
@@ -523,58 +524,85 @@ def tile_ranktwokroneckersumlayer_t_kernel(tc, x, b1, b2_bytes, b2_scale, a1, a2
             if j % 2 == 1:
                 add_c(j - 5)
             if j + 1 < NEAR:
-                regroup_all(j + 1)
+                regroup(j + 1)
             unload_x(j, 0, "V" if j % 2 == 0 and j + 1 >= NEAR else "S")
             if j % 2 == 0:
                 quantize_t(j - 4)
+            if j + 1 < NEAR:
+                regroup_back(j + 1)
             if PLAIN <= j + 2 < NB:
                 regroup(j + 2, "V", 0, LEAD)
             quantize_x(j - 1, 0, 4)
             for o in range(1, 4):
                 unload_x(j, o, "S")
             if j > TURN + 1:
-                first_product(j - 2, 0)
+                first_product(j - 2, 0, 0, 4, ANY)
                 unload_t(j - 2, 0, "S")
-            first_product(j - 2, 1)
+            first_product(j - 2, 1, 0, 4, ANY)
             if j % 2 == 0:
                 second_product(j - 4)
                 for k in range(done, min(done + (2 if j == TURN + 2 else 4), j - 4), 2):
                     silu_store(k)
                     done = k + 2
 
+        j = last - 2
         for o in range(4):
-            turn_x(last, o)
-        unload_t(last - 3, 1, "V")
-        quantize_x(last - 1, 0, 4)
-        add_c(last - 5)
+            turn_x(j, o, ANY)
+        regroup(j + 1, "G", LEAD, 16)
+        unload_t(j - 3, 1, "V")
+        add_c(j - 5)
+        regroup(j + 2, "V", 0, LEAD)
+        quantize_x(j - 1, 0, 2)
         for o in range(4):
-            unload_x(last, o, "S")
-        first_product(last - 2, 0)
-        first_product(last - 2, 1)
-        unload_t(last - 2, 0, "V")
-        quantize_x(last, 0, 2)
-        unload_t(last - 2, 1, "S")
-        quantize_x(last, 2, 4)
-        first_product(last - 1, 0)
-        first_product(last - 1, 1, 0, 4, T_BANKS)
-        unload_t(last - 1, 0, "S")
-        quantize_t(last - 3)
-        unload_t(last - 1, 1, "S")
-        silu_store(last - 5)
-        for lo in (0, 2):
+            unload_x(j, o, "S")
+        for b in range(2):
+            first_product(j - 2, b, 0, 4, ANY)
+        regroup(j + 2, "G", LEAD, 16)
+        for b in range(2):
+            unload_t(j - 2, b, "V")
+        quantize_x(j - 1, 2, 4)
+
+        j = last - 1
+        for o in range(4):
+            turn_x(j, o, ANY)
+        silu_store(j - 6)
+        for o in range(4):
+            unload_x(j, o, "S")
+            turn_x(last, o, ANY)
+        quantize_t(j - 4)
+        quantize_x(j - 1, 0, 4)
+        for o in range(4):
+            unload_x(last, o, "SSSV"[o])
+        for b in range(2):
+            first_product(j - 2, b, 0, 4, ANY)
+        second_product(j - 4)
+        quantize_x(j, 0, 4)
+        for b in range(2):
+            first_product(j - 1, b, 0, 4, ANY)
+        quantize_x(last, 0, 4)
+        add_c(j - 4)
+        for n in (j - 2, j - 1):
             for b in range(2):
-                first_product(last, b, lo, lo + 2)
+                unload_t(n, b, "S")
+        for b in range(2):
+            first_product(j, b, 0, 4, ANY)
+        quantize_t(last - 3)
+        unload_t(j, 0, "S")
+        unload_t(j, 1, "S")
+        silu_store(j - 4)
+        for b in range(2):
+            first_product(last, b, 0, 4, ANY)
         second_product(last - 3)
-        quantize_t(last - 1)
-        second_product(last - 1, T_BANKS)
         unload_t(last, 0, "V")
+        quantize_t(last - 1)
+        second_product(last - 1, ANY)
         unload_t(last, 1, "S")
-        add_c_one(last - 3, 0)
         quantize_t(last, 0, 1)
         last_second_product(last, 0)
+        add_c_one(last - 3, 0)
+        add_c_one(last - 3, 1)
         quantize_t(last, 1, 2)
         last_second_product(last, 1)
-        add_c_one(last - 3, 1)
         add_c(last - 1)
         silu_store_one(last - 3)
         silu_store_one(last - 2)

@@ -185,6 +185,11 @@ def tile_ranktwokroneckersumlayer_t_kernel(tc, x, b1, b2_bytes, b2_scale, a1, a2
                 if wide(n):
                     regroup_back(n)
 
+        def share_regroup(n, lead=1):
+            regroup_back(n, "V", 0, lead)
+            regroup(n)
+            regroup_back(n, "G", lead, 16)
+
         def turn_x(n, o, among=T_BANKS):
             f, d = divmod(o, 2)
             bank = take(among, [P, 4, P])
@@ -370,12 +375,13 @@ def tile_ranktwokroneckersumlayer_t_kernel(tc, x, b1, b2_bytes, b2_scale, a1, a2
                 if n == 0:
                     load_scale()
                     load_b2()
+                if n == A_AFTER + 1:
+                    load_a(1)
                 load_half(n, 1)
             else:
                 load_x(n)
             if n == A_AFTER:
                 load_a(0)
-                load_a(1)
             if n == 6:
                 load_c()
         constants()
@@ -471,11 +477,9 @@ def tile_ranktwokroneckersumlayer_t_kernel(tc, x, b1, b2_bytes, b2_scale, a1, a2
         for o in range(4):
             turn_x(j, o)
         quantize_x(j - 1, 2, 4)
-        regroup_back(j + 1, "V", 0, 1)
-        regroup(j + 1)
-        regroup_back(j + 1, "G", 1, 16)
         unload_t(j - 2, 1, "V")
         second_product(0)
+        share_regroup(j + 1, 8)
         add_c(0)
         quantize_t(2)
         for o in range(4):
@@ -488,30 +492,75 @@ def tile_ranktwokroneckersumlayer_t_kernel(tc, x, b1, b2_bytes, b2_scale, a1, a2
 
         last = NB - 1
         done = 0
-        j = TURN
+        j = 6
         for o in range(4):
             turn_x(j, o)
         second_product(j - 4)
         quantize_x(j - 1, 2, 4)
-        regroup_all(j + 1)
+        share_regroup(j + 1)
+        unload_t(j - 2, 1, "V")
+        add_c(j - 4)
         for o in range(4):
             unload_x(j, o, "S")
-        first_product(j - 1, 0)
+        quantize_x(j, 0, 2)
+        for lo in (0, 2):
+            for b in range(2):
+                first_product(j - 1, b, lo, lo + 2)
+        silu_store(0)
         unload_t(j - 1, 0, "S")
-        j = TURN + 1
+        j = 7
         for o in range(4):
             turn_x(j, o)
-        quantize_x(j - 1, 0, 2)
-        regroup_back(j + 1, "V", 0, 1)
-        regroup(j + 1)
-        regroup_back(j + 1, "G", 1, 16)
-        unload_t(j - 3, 1, "V")
-        add_c(j - 5)
         quantize_x(j - 1, 2, 4)
+        share_regroup(j + 1, 8)
+        unload_t(j - 2, 1, "V")
         for o in range(4):
             unload_x(j, o, "S")
-        first_product(j - 2, 1)
-        for j in range(TURN + 2, last - 2):
+        quantize_x(j, 0, 2)
+        quantize_t(j - 3)
+        for lo in (0, 2):
+            for b in range(2):
+                first_product(j - 1, b, lo, lo + 2)
+        silu_store(2)
+        unload_t(j - 1, 0, "S")
+        j = 8
+        for o in range(4):
+            turn_x(j, o)
+        second_product(j - 4)
+        quantize_x(j - 1, 2, 4)
+        share_regroup(j + 1)
+        unload_t(j - 2, 1, "V")
+        add_c(j - 4)
+        for o in range(4):
+            unload_x(j, o, "S")
+        for lo in (0, 2):
+            for b in range(2):
+                first_product(j - 1, b, lo, lo + 2)
+        unload_t(j - 1, 0, "S")
+        silu_store(4)
+        j = 9
+        for o in range(4):
+            turn_x(j, o, ANY)
+        share_regroup(j + 1)
+        unload_t(j - 2, 1, "V")
+        for o in range(4):
+            unload_x(j, o, "VSSS"[o])
+            turn_x(j + 1, o, ANY)
+        quantize_x(j - 1, 0, 2)
+        quantize_x(j - 1, 2, 4)
+        quantize_t(j - 3)
+        regroup_all(j + 2)
+        regroup(j + 3, "V", 0, LEAD)
+        quantize_x(j, 0, 4)
+        for o in range(4):
+            unload_x(j + 1, o, "S")
+        for lo in (0, 2):
+            for b in range(2):
+                first_product(j - 1, b, lo, lo + 2, ANY)
+        unload_t(j - 1, 0, "S")
+        second_product(j - 3)
+        done = 6
+        for j in range(11, last - 2):
             for o in range(4):
                 turn_x(j, o, ANY)
             if j + 1 >= PLAIN:

@@ -12,12 +12,8 @@ FREE = 7
 PITCH = 72 * PIECE
 WIDE_PITCH = 136 * PIECE
 DATA = (FREE + 1) * PIECE
-PLAIN = 12
 HALVED = 5
-T_BANKS = (0, 1, 2, 3)
-S_BANKS = (4, 5, 6)
-Z_BANK = (7,)
-ANY = T_BANKS + S_BANKS
+PLAIN = 7
 F32 = mybir.dt.float32
 BF16 = mybir.dt.bfloat16
 U32 = mybir.dt.uint32
@@ -33,7 +29,7 @@ def tile_ranktwokroneckersumlayer_t_kernel(tc, x, b1, b2_bytes, b2_scale, a1, a2
 
     with ExitStack() as ctx:
         keep = ctx.enter_context(tc.tile_pool(name="keep", bufs=1))
-        xpool = ctx.enter_context(tc.tile_pool(name="xpool", bufs=NB - HALVED - 1))
+        xpool = ctx.enter_context(tc.tile_pool(name="xpool", bufs=10))
         hpool = ctx.enter_context(tc.tile_pool(name="hpool", bufs=2 * HALVED))
         gpool = ctx.enter_context(tc.tile_pool(name="gpool", bufs=3))
         qpool = ctx.enter_context(tc.tile_pool(name="qpool", bufs=3))
@@ -69,273 +65,40 @@ def tile_ranktwokroneckersumlayer_t_kernel(tc, x, b1, b2_bytes, b2_scale, a1, a2
         zb = {}
         zs = {}
 
-        age = list(range(8))
+        idle = list(range(8))
+        held = {}
 
-        def take(among, shape, dtype=F32):
-            k = [i for i in age if i in among][0]
-            age.remove(k)
-            age.append(k)
+        def take(key, shape, dtype=F32, k=None):
+            if k is None:
+                k = idle[0]
+            idle.remove(k)
+            held[key] = k
             return psum.tile(shape, dtype, name="bank%d" % k)
 
-        def wide(key):
-            return key in range(HALVED, PLAIN)
+        def give(key):
+            idle.append(held[key])
+
+        def plain(key):
+            return key in range(PLAIN, NB)
 
         def rows(key, skip=0):
-            pitch = WIDE_PITCH if wide(key) else PITCH
-            count = 4 if key in range(PLAIN, NB) else 2
+            pitch, count = (PITCH, 4) if plain(key) else (WIDE_PITCH, 2 if key in range(NB) else 1)
             return xs[key][:, skip * PIECE : skip * PIECE + count * pitch].rearrange("p (d y) -> p d y", y=pitch)
 
         def load_x(n):
-            if wide(n):
-                xs[n] = xpool.tile([P, 2 * WIDE_PITCH + DATA], BF16, name="x_t", align_bytes=256)
-                nc.sync.dma_start(out=rows(n)[:, :, DATA:], in_=x[n].rearrange("(m d f) k -> m d (f k)", d=2, f=2))
-            else:
+            if plain(n):
                 xs[n] = xpool.tile([P, 4 * PITCH], BF16, name="x_t", align_bytes=256)
                 nc.sync.dma_start(out=rows(n)[:, :, DATA:], in_=x[n].rearrange("(m s) k -> m s k", s=4))
+            else:
+                xs[n] = xpool.tile([P, 2 * WIDE_PITCH + DATA], BF16, name="x_t", align_bytes=256)
+                nc.sync.dma_start(out=rows(n)[:, :, DATA:], in_=x[n].rearrange("(m d f) k -> m d (f k)", d=2, f=2))
 
-        def load_half(n, f):
-            xs[n, f] = hpool.tile([P, 2 * PITCH], BF16, name="x_h", align_bytes=256)
-            nc.sync.dma_start(out=rows((n, f))[:, :, DATA:], in_=x[n].rearrange("(m d f) k -> f m d k", d=2, f=2)[f])
+        def load_half(n, d):
+            xs[n, d] = hpool.tile([P, WIDE_PITCH + DATA], BF16, name="x_h", align_bytes=256)
+            nc.sync.dma_start(out=xs[n, d][:, DATA:WIDE_PITCH], in_=x[n].rearrange("(m d f) k -> d m (f k)", d=2, f=2)[d])
 
         def load_a(b):
             nc.sync.dma_start(out=a_raw[:, b, :], in_=(a1, a2)[b].rearrange("(m h) k -> m (h k)", h=2))
-
-        def warm_tensor(count):
-            for i in range(count):
-                bank = take(Z_BANK, [P, 512])
-                nc.tensor.matmul(bank[:], lhsT=zero[:, :P], rhs=zero[:], start=True, stop=True)
-
-        def widen_b2(g, t, eng):
-            src = b2_raw[:, g, t, :].bitcast(FP8)
-            if eng == "V":
-                nc.vector.tensor_scalar(
-                    out=b2_w[:, g, t, :], in0=src, scalar1=b2_s[:, g, t : t + 1], scalar2=None, op0=ALU.mult
-                )
-            else:
-                nc.scalar.activation(out=b2_w[:, g, t, :], in_=src, func=ACT.Copy, scale=b2_s[:, g, t : t + 1])
-
-        def copy(eng, dst, src):
-            if eng == "S":
-                nc.scalar.copy(out=dst, in_=src)
-            else:
-                nc.vector.tensor_copy(out=dst, in_=src)
-
-        def reorder_b(b, src, lo=0, hi=2):
-            if lo == 0:
-                banks["b", b] = take(S_BANKS, [P, 2, P, 2, 2], BF16)
-            bank = banks["b", b]
-            for u in range(2):
-                for g in range(lo, hi):
-                    for r in range(2):
-                        nc.tensor.matmul(
-                            bank[:, g, :, u, :],
-                            lhsT=pick[:, u, r, :],
-                            rhs=src[:, 2 * r + g, :, :].rearrange("p e q -> p q e"),
-                            start=(r == 0),
-                            stop=(r == 1),
-                        )
-
-        def unload_b(b, eng):
-            copy(eng, b_grp[:, 1024 * b : 1024 * (b + 1)], banks["b", b][:].rearrange("p g q u e -> p (g q u e)"))
-
-        def quantize_b(b):
-            cols = slice(256 * b, 256 * (b + 1))
-            nc.vector.quantize_mx(out=b_codes[:, cols].bitcast(FP8X4), scales=b_scales[:, cols], in_=b_grp[:, 1024 * b : 1024 * (b + 1)])
-
-        def turn_a(b, among):
-            bank = take(among, [P, 4, P])
-            w = a_raw[:, b, :].bitcast(F32)
-            for h in range(2):
-                for u in range(2):
-                    nc.tensor.transpose(bank[:, 2 * h + u, :], w[:, 256 * h + u : 256 * (h + 1) : 2], ident[:])
-            banks["a", b] = bank
-
-        def unload_a(b, eng):
-            dst = a_grp[:].bitcast(F32)[:, 512 * b : 512 * (b + 1)].rearrange("p (h m u) -> p h m u", h=2, u=2)
-            copy(eng, dst, banks["a", b][:].rearrange("p (h u) m -> p h m u", h=2))
-
-        def quantize_a():
-            nc.vector.quantize_mx(out=a_codes[:].bitcast(FP8X4), scales=a_scales[:], in_=a_grp[:])
-
-        def stepped(view, w, first, far):
-            end = first + far + 31
-            view = view[:, :, w * (end - 2 * far) : w * end].rearrange("p d (r y) -> p d r y", r=2)[:, :, :, (far - 32) * w :]
-            return view.rearrange("p d r (i t w) -> p d i r t w", t=2, w=w)[:, :, :, :, 1, :]
-
-        def regroup(key, eng="V", lo=0, hi=16):
-            view, w, engine = rows(key), PIECE, nc.vector
-            if eng == "G":
-                view, w, engine = view.bitcast(U32), PIECE // 2, nc.gpsimd
-            dst, src = stepped(view, w, FREE, 34), stepped(view, w, FREE + 2, 32)[:, :, :, ::-1, :]
-            engine.tensor_copy(out=dst[:, :, lo:hi], in_=src[:, :, lo:hi])
-
-        def regroup_back(key, eng="V", lo=0, hi=16):
-            view, w, engine = rows(key, FREE + 1), PIECE, nc.vector
-            if eng == "G":
-                view, w, engine = view.bitcast(U32), PIECE // 2, nc.gpsimd
-            dst, src = stepped(view, w, 64, 34)[:, :, ::-1, ::-1, :], stepped(view, w, 64, 32)[:, :, ::-1, :, :]
-            engine.tensor_copy(out=dst[:, :, lo:hi], in_=src[:, :, lo:hi])
-
-        def regroup_all(n):
-            if n < HALVED:
-                regroup((n, 0))
-                regroup((n, 1))
-            else:
-                regroup(n)
-                if wide(n):
-                    regroup_back(n)
-
-        def share_regroup(n, lead=1):
-            regroup_back(n, "V", 0, lead)
-            regroup(n)
-            regroup_back(n, "G", lead, 16)
-
-        def turn_x(n, o, among=T_BANKS):
-            f, d = divmod(o, 2)
-            bank = take(among, [P, 4, P])
-            key, row = ((n, f), d) if n < HALVED else (n, 2 * d + f)
-            start, windows = PITCH * row, (0, 33)
-            if wide(n):
-                start, windows = WIDE_PITCH * d, ((0, 33), (98, 65))[f]
-            words = xs[key][:].bitcast(F32)
-            for g in range(2):
-                for u in range(2):
-                    lo = (start + PIECE * (FREE + windows[u] + 16 * g)) // 2
-                    nc.tensor.transpose(bank[:, 2 * g + u, :], words[:, lo : lo + P], ident[:])
-            banks[n, o] = bank
-
-        def unload_x(n, o, eng):
-            if n not in grp:
-                grp[n] = gpool.tile([P, 4096], BF16, name="x_g", align_bytes=64)
-            dst = grp[n][:].bitcast(F32)[:, 512 * o : 512 * (o + 1)].rearrange("p (g m u) -> p g m u", g=2, u=2)
-            copy(eng, dst, banks[n, o][:].rearrange("p (g u) m -> p g m u", g=2))
-
-        def quantize_x(n, lo, hi):
-            if lo == 0:
-                q = qpool.tile([P, 1024], U32, name="x_q", align_bytes=64)
-                sc = qpool.tile([P, 1024], U8, name="x_s", align_bytes=64)
-                codes[n] = (q, sc)
-            q, sc = codes[n]
-            cols = slice(256 * lo, 256 * hi)
-            nc.vector.quantize_mx(out=q[:, cols].bitcast(FP8X4), scales=sc[:, cols], in_=grp[n][:, 1024 * lo : 1024 * hi])
-
-        def first_product(n, b, lo=0, hi=4, among=S_BANKS):
-            if lo == 0:
-                s1[n, b] = take(among, [P, 4, P])
-            q, sc = codes[n]
-            for o in range(lo, hi):
-                f, d = divmod(o, 2)
-                for g in range(2):
-                    cols = slice(256 * o + P * g, 256 * o + P * (g + 1))
-                    bcols = slice(256 * b + P * g, 256 * b + P * (g + 1))
-                    nc.tensor.matmul_mx(
-                        out=s1[n, b][:, 2 * d + f, :],
-                        lhsT=q[:, cols].bitcast(FP8X4),
-                        lhsT_scale=sc[:, cols],
-                        rhs=b_codes[:, bcols].bitcast(FP8X4),
-                        rhs_scale=b_scales[:, bcols],
-                        start=(g == 0),
-                        stop=(g == 1),
-                    )
-
-        def group(k):
-            return (k - k % 2, 2) if k < PAIRS else (k, 1)
-
-        def unload_t(n, b, eng):
-            first, size = group(n)
-            if first not in tg:
-                pool = keep if n == NB - 1 else tpool
-                tg[first] = pool.tile([P, 1024 * size], BF16, name="t_g", align_bytes=64)
-            lo = 512 * (size * b + n - first)
-            dst = tg[first][:, lo : lo + 512].rearrange("p (q i s) -> p q s i", i=2, s=4)
-            copy(eng, dst, s1[n, b][:].rearrange("p s (q i) -> p q s i", i=2))
-
-        def quantize_t(n, lo=0, hi=2):
-            first, size = group(n)
-            if lo == 0:
-                pool = keep if n == NB - 1 else tpool
-                q = pool.tile([P, 256 * size], U32, name="t_q", align_bytes=64)
-                sc = pool.tile([P, 256 * size], U8, name="t_s", align_bytes=64)
-                tcodes[first] = (q, sc)
-            q, sc = tcodes[first]
-            cols = slice(P * size * lo, P * size * hi)
-            nc.vector.quantize_mx(out=q[:, cols].bitcast(FP8X4), scales=sc[:, cols], in_=tg[first][:, 4 * cols.start : 4 * cols.stop])
-
-        def second_product(n, among=Z_BANK):
-            first, size = group(n)
-            bank = take(among, [P, 2, P * size])
-            q, sc = tcodes[first]
-            for h in range(2):
-                for b in range(2):
-                    acols = slice(P * (2 * b + h), P * (2 * b + h + 1))
-                    tcols = slice(P * size * b, P * size * (b + 1))
-                    nc.tensor.matmul_mx(
-                        out=bank[:, h, :],
-                        lhsT=a_codes[:, acols].bitcast(FP8X4),
-                        lhsT_scale=a_scales[:, acols],
-                        rhs=q[:, tcols].bitcast(FP8X4),
-                        rhs_scale=sc[:, tcols],
-                        start=(b == 0),
-                        stop=(b == 1),
-                    )
-            zb[first] = bank
-
-        def last_second_product(n, b):
-            q, sc = tcodes[n]
-            for h in range(2):
-                if b == 0:
-                    zb[n, h] = take(T_BANKS, [P, P])
-                acols = slice(P * (2 * b + h), P * (2 * b + h + 1))
-                tcols = slice(P * b, P * (b + 1))
-                nc.tensor.matmul_mx(
-                    out=zb[n, h][:],
-                    lhsT=a_codes[:, acols].bitcast(FP8X4),
-                    lhsT_scale=a_scales[:, acols],
-                    rhs=q[:, tcols].bitcast(FP8X4),
-                    rhs_scale=sc[:, tcols],
-                    start=(b == 0),
-                    stop=(b == 1),
-                )
-
-        def last_add_c(n, h):
-            z = zpool.tile([P, P], F32, name="z_s")
-            nc.vector.tensor_tensor(out=z[:], in0=zb[n, h][:], in1=c_t[:, h, :], op=ALU.add)
-            zs[n, h] = z
-
-        def last_silu_store(n, h):
-            o = zpool.tile([P, P], F32, name="o_last", bufs=2, align_bytes=256)
-            nc.scalar.activation(out=o[:], in_=zs[n, h][:], func=ACT.Silu)
-            queue = nc.scalar if h == 1 else nc.sync
-            queue.dma_start(out=out[n].rearrange("(m h) q -> h m q", h=2)[h], in_=o[:])
-
-        def add_c(n):
-            first, size = group(n)
-            z = zpool.tile([P, size, 2, P], F32, name="z_s")
-            nc.vector.tensor_tensor(
-                out=z[:],
-                in0=zb[first][:].rearrange("p h (n q) -> p n h q", n=size),
-                in1=c_t[:].unsqueeze(1).to_broadcast([P, size, 2, P]),
-                op=ALU.add,
-            )
-            zs[first] = z
-
-        def silu_store(n, queue=nc.sync):
-            first, size = group(n)
-            o = zpool.tile([P, size, 2, P], F32, name="o_t", align_bytes=256)
-            nc.scalar.activation(out=o[:], in_=zs[first][:], func=ACT.Silu)
-            queue.dma_start(
-                out=out[first : first + size].rearrange("n (m h) q -> m n (h q)", h=2), in_=o[:].rearrange("p n h q -> p n (h q)")
-            )
-
-        def add_c_one(first, i):
-            z = zpool.tile([P, 2, P], F32, name="z_s")
-            nc.vector.tensor_tensor(out=z[:], in0=zb[first][:, :, P * i : P * (i + 1)], in1=c_t[:], op=ALU.add)
-            zs[first + i] = z
-
-        def silu_store_one(n):
-            o = zpool.tile([P, 2, P], F32, name="o_t", align_bytes=256)
-            nc.scalar.activation(out=o[:], in_=zs[n][:], func=ACT.Silu)
-            nc.sync.dma_start(out=out[n].rearrange("(m h) q -> m (h q)", h=2), in_=o[:].rearrange("p h q -> p (h q)"))
 
         def load_b1():
             nc.sync.dma_start(out=b1_raw[:], in_=b1.rearrange("(g p t) q -> p g t q", g=4, t=2))
@@ -363,11 +126,245 @@ def tile_ranktwokroneckersumlayer_t_kernel(tc, x, b1, b2_bytes, b2_scale, a1, a2
             nc.vector.tensor_copy(out=picks[:, 0, 1, :, 0, :], in_=halves[:, :, 1, :])
             nc.vector.tensor_copy(out=picks[:, 1, 0, :, 1, :], in_=halves[:, :, 1, :])
 
-        TURN = 6
-        LEAD = 6
-        NEAR = 10
-        A_AFTER = 3
-        PAIRS = NB - 2
+        def warm_tensor(count):
+            for i in range(count):
+                bank = take("warm", [P, 512], k=7)
+                nc.tensor.matmul(bank[:], lhsT=zero[:, :P], rhs=zero[:], start=True, stop=True)
+                give("warm")
+
+        def widen_b2(g, t, eng):
+            src = b2_raw[:, g, t, :].bitcast(FP8)
+            if eng == "V":
+                nc.vector.tensor_scalar(
+                    out=b2_w[:, g, t, :], in0=src, scalar1=b2_s[:, g, t : t + 1], scalar2=None, op0=ALU.mult
+                )
+            else:
+                nc.scalar.activation(out=b2_w[:, g, t, :], in_=src, func=ACT.Copy, scale=b2_s[:, g, t : t + 1])
+
+        def copy(eng, dst, src):
+            if eng == "S":
+                nc.scalar.copy(out=dst, in_=src)
+            else:
+                nc.vector.tensor_copy(out=dst, in_=src)
+
+        def reorder_b(b, src):
+            bank = take(("b", b), [P, 2, P, 2, 2], BF16, k=5 + b)
+            banks["b", b] = bank
+            for u in range(2):
+                for g in range(2):
+                    for r in range(2):
+                        nc.tensor.matmul(
+                            bank[:, g, :, u, :],
+                            lhsT=pick[:, u, r, :],
+                            rhs=src[:, 2 * r + g, :, :].rearrange("p e q -> p q e"),
+                            start=(r == 0),
+                            stop=(r == 1),
+                        )
+
+        def unload_b(b, eng):
+            copy(eng, b_grp[:, 1024 * b : 1024 * (b + 1)], banks["b", b][:].rearrange("p g q u e -> p (g q u e)"))
+            give(("b", b))
+
+        def quantize_b(b):
+            cols = slice(256 * b, 256 * (b + 1))
+            nc.vector.quantize_mx(out=b_codes[:, cols].bitcast(FP8X4), scales=b_scales[:, cols], in_=b_grp[:, 1024 * b : 1024 * (b + 1)])
+
+        def turn_a(b):
+            bank = take(("a", b), [P, 4, P])
+            w = a_raw[:, b, :].bitcast(F32)
+            for h in range(2):
+                for u in range(2):
+                    nc.tensor.transpose(bank[:, 2 * h + u, :], w[:, 256 * h + u : 256 * (h + 1) : 2], ident[:])
+            banks["a", b] = bank
+
+        def unload_a(b, eng):
+            dst = a_grp[:].bitcast(F32)[:, 512 * b : 512 * (b + 1)].rearrange("p (h m u) -> p h m u", h=2, u=2)
+            copy(eng, dst, banks["a", b][:].rearrange("p (h u) m -> p h m u", h=2))
+            give(("a", b))
+
+        def quantize_a():
+            nc.vector.quantize_mx(out=a_codes[:].bitcast(FP8X4), scales=a_scales[:], in_=a_grp[:])
+
+        def stepped(view, w, first, far):
+            end = first + far + 31
+            count = view.shape[1]
+            view = view[:, :, w * (end - 2 * far) : w * end].rearrange("p d (r y) -> p d r y", r=2)[:, :, :, (far - 32) * w :]
+            view = view.rearrange("p d r (i t w) -> p d i r t w", t=2, w=w)[:, :, :, :, 1, :]
+            if count == 1:
+                view = view[:, 0].rearrange("p i r (h e) -> p h i r e", h=2)
+            return view
+
+        def regroup(key, eng="V", lo=0, hi=16):
+            view, w, engine = rows(key), PIECE, nc.vector
+            if eng == "G":
+                view, w, engine = view.bitcast(U32), PIECE // 2, nc.gpsimd
+            dst, src = stepped(view, w, FREE, 34), stepped(view, w, FREE + 2, 32)[:, :, :, ::-1, :]
+            engine.tensor_copy(out=dst[:, :, lo:hi], in_=src[:, :, lo:hi])
+
+        def regroup_back(key, eng="V", lo=0, hi=16):
+            view, w, engine = rows(key, FREE + 1), PIECE, nc.vector
+            if eng == "G":
+                view, w, engine = view.bitcast(U32), PIECE // 2, nc.gpsimd
+            dst, src = stepped(view, w, 64, 34)[:, :, ::-1, ::-1, :], stepped(view, w, 64, 32)[:, :, ::-1, :, :]
+            engine.tensor_copy(out=dst[:, :, lo:hi], in_=src[:, :, lo:hi])
+
+        def regroup_all(key, eng="V", lo=0):
+            regroup(key, eng, lo, 16)
+            if not plain(key):
+                regroup_back(key, eng)
+
+        def turn_x(n, lo=0, hi=4):
+            for s in range(lo, hi):
+                d, f = divmod(s, 2)
+                bank = take(("x", n, s), [P, 4, P])
+                key, start, windows = n, PITCH * s, (0, 33)
+                if not plain(n):
+                    start, windows = WIDE_PITCH * d, ((0, 33), (98, 65))[f]
+                if n < HALVED:
+                    key, start = (n, d), 0
+                words = xs[key][:].bitcast(F32)
+                for g in range(2):
+                    for u in range(2):
+                        at = (start + PIECE * (FREE + windows[u] + 16 * g)) // 2
+                        nc.tensor.transpose(bank[:, 2 * g + u, :], words[:, at : at + P], ident[:])
+                banks[n, s] = bank
+
+        def unload_x(n, s, eng):
+            if n not in grp:
+                grp[n] = gpool.tile([P, 4096], BF16, name="x_g", align_bytes=64)
+            dst = grp[n][:].bitcast(F32)[:, 512 * s : 512 * (s + 1)].rearrange("p (g m u) -> p g m u", g=2, u=2)
+            copy(eng, dst, banks[n, s][:].rearrange("p (g u) m -> p g m u", g=2))
+            give(("x", n, s))
+
+        def quantize_x(n, lo=0, hi=4):
+            if lo == 0:
+                q = qpool.tile([P, 1024], U32, name="x_q", align_bytes=64)
+                sc = qpool.tile([P, 1024], U8, name="x_s", align_bytes=64)
+                codes[n] = (q, sc)
+            q, sc = codes[n]
+            cols = slice(256 * lo, 256 * hi)
+            nc.vector.quantize_mx(out=q[:, cols].bitcast(FP8X4), scales=sc[:, cols], in_=grp[n][:, 1024 * lo : 1024 * hi])
+
+        def first_product(n, b, lo=0, hi=4):
+            if lo == 0:
+                s1[n, b] = take(("t", n, b), [P, 4, P])
+            q, sc = codes[n]
+            for s in range(lo, hi):
+                for g in range(2):
+                    cols = slice(256 * s + P * g, 256 * s + P * (g + 1))
+                    bcols = slice(256 * b + P * g, 256 * b + P * (g + 1))
+                    nc.tensor.matmul_mx(
+                        out=s1[n, b][:, s, :],
+                        lhsT=q[:, cols].bitcast(FP8X4),
+                        lhsT_scale=sc[:, cols],
+                        rhs=b_codes[:, bcols].bitcast(FP8X4),
+                        rhs_scale=b_scales[:, bcols],
+                        start=(g == 0),
+                        stop=(g == 1),
+                    )
+
+        def group(k):
+            return (k - k % 2, 2) if k < NB - 2 else (k, 1)
+
+        def unload_t(n, b, eng):
+            first, size = group(n)
+            if first not in tg:
+                pool = keep if n == NB - 1 else tpool
+                tg[first] = pool.tile([P, 1024 * size], BF16, name="t_g", align_bytes=64)
+            lo = 512 * (size * b + n - first)
+            dst = tg[first][:, lo : lo + 512].rearrange("p (q i s) -> p q s i", i=2, s=4)
+            copy(eng, dst, s1[n, b][:].rearrange("p s (q i) -> p q s i", i=2))
+            give(("t", n, b))
+
+        def quantize_t(n, lo=0, hi=2):
+            first, size = group(n)
+            if lo == 0:
+                pool = keep if n == NB - 1 else tpool
+                q = pool.tile([P, 256 * size], U32, name="t_q", align_bytes=64)
+                sc = pool.tile([P, 256 * size], U8, name="t_s", align_bytes=64)
+                tcodes[first] = (q, sc)
+            q, sc = tcodes[first]
+            cols = slice(P * size * lo, P * size * hi)
+            nc.vector.quantize_mx(out=q[:, cols].bitcast(FP8X4), scales=sc[:, cols], in_=tg[first][:, 4 * cols.start : 4 * cols.stop])
+
+        def second_pass(bank, first, size, h, b):
+            q, sc = tcodes[first]
+            acols = slice(P * (2 * b + h), P * (2 * b + h + 1))
+            tcols = slice(P * size * b, P * size * (b + 1))
+            nc.tensor.matmul_mx(
+                out=bank,
+                lhsT=a_codes[:, acols].bitcast(FP8X4),
+                lhsT_scale=a_scales[:, acols],
+                rhs=q[:, tcols].bitcast(FP8X4),
+                rhs_scale=sc[:, tcols],
+                start=(b == 0),
+                stop=(b == 1),
+            )
+
+        def second_product(n):
+            first, size = group(n)
+            zb[first] = take(("z", first), [P, 2, P * size])
+            for h in range(2):
+                for b in range(2):
+                    second_pass(zb[first][:, h, :], first, size, h, b)
+
+        def last_second_product(n, b):
+            for h in range(2):
+                if b == 0:
+                    zb[n, h] = take(("z", n, h), [P, P])
+                second_pass(zb[n, h][:], n, 1, h, b)
+
+        def last_add_c(n, h):
+            z = zpool.tile([P, P], F32, name="z_s")
+            nc.vector.tensor_tensor(out=z[:], in0=zb[n, h][:], in1=c_t[:, h, :], op=ALU.add)
+            zs[n, h] = z
+
+        def last_silu_store(n, h):
+            o = zpool.tile([P, P], F32, name="o_last", bufs=2, align_bytes=256)
+            nc.scalar.activation(out=o[:], in_=zs[n, h][:], func=ACT.Silu)
+            queue = nc.scalar if h == 1 else nc.sync
+            queue.dma_start(out=out[n].rearrange("(m h) q -> h m q", h=2)[h], in_=o[:])
+
+        def add_c(n):
+            first, size = group(n)
+            z = zpool.tile([P, size, 2, P], F32, name="z_s")
+            nc.vector.tensor_tensor(
+                out=z[:],
+                in0=zb[first][:].rearrange("p h (n q) -> p n h q", n=size),
+                in1=c_t[:].unsqueeze(1).to_broadcast([P, size, 2, P]),
+                op=ALU.add,
+            )
+            zs[first] = z
+            give(("z", first))
+
+        def silu_store(n):
+            first, size = group(n)
+            o = zpool.tile([P, size, 2, P], F32, name="o_t", align_bytes=256)
+            nc.scalar.activation(out=o[:], in_=zs[first][:], func=ACT.Silu)
+            nc.sync.dma_start(
+                out=out[first : first + size].rearrange("n (m h) q -> m n (h q)", h=2), in_=o[:].rearrange("p n h q -> p n (h q)")
+            )
+
+        def add_c_one(first, i):
+            z = zpool.tile([P, 2, P], F32, name="z_s")
+            nc.vector.tensor_tensor(out=z[:], in0=zb[first][:, :, P * i : P * (i + 1)], in1=c_t[:], op=ALU.add)
+            zs[first + i] = z
+
+        def silu_store_one(n):
+            o = zpool.tile([P, 2, P], F32, name="o_t", align_bytes=256)
+            nc.scalar.activation(out=o[:], in_=zs[n][:], func=ACT.Silu)
+            nc.sync.dma_start(out=out[n].rearrange("(m h) q -> m (h q)", h=2), in_=o[:].rearrange("p h q -> p (h q)"))
+
+        def both(n, lo=0, hi=4):
+            for b in range(2):
+                first_product(n, b, lo, hi)
+
+        def unload_row(n, engs, lo=0):
+            for i in range(len(engs)):
+                unload_x(n, lo + i, engs[i])
+
+        LEAD = 3
+
         load_b1()
         for n in range(NB):
             if n < HALVED:
@@ -375,276 +372,200 @@ def tile_ranktwokroneckersumlayer_t_kernel(tc, x, b1, b2_bytes, b2_scale, a1, a2
                 if n == 0:
                     load_scale()
                     load_b2()
-                if n == A_AFTER + 1:
+                if n == 4:
                     load_a(1)
                 load_half(n, 1)
             else:
                 load_x(n)
-            if n == A_AFTER:
+            if n == 3:
                 load_a(0)
-            if n == 6:
+            if n == 5:
                 load_c()
+
         constants()
         warm_tensor(3)
         reorder_b(0, b1_raw)
-        regroup((0, 0))
+        regroup_all((0, 0))
+        unload_b(0, "S")
+        turn_x(0, 0, 2)
         for i in range(8):
             widen_b2(i // 2, i % 2, "V" if i < 5 else "S")
-        unload_b(0, "S")
-        turn_x(0, 0)
-        turn_x(0, 1)
         reorder_b(1, b2_w)
-        unload_x(0, 0, "V")
-        unload_x(0, 1, "S")
-        regroup((0, 1))
+        unload_row(0, "VS")
+        regroup_all((0, 1))
         quantize_b(0)
         unload_b(1, "S")
-        turn_x(0, 2)
-        turn_x(0, 3)
+        turn_x(0, 2, 4)
         quantize_x(0, 0, 2)
         first_product(0, 0, 0, 2)
-        regroup((1, 0))
+        regroup_all((1, 0))
         quantize_b(1)
-        unload_x(0, 2, "S")
-        unload_x(0, 3, "S")
-        turn_x(1, 0)
-        turn_x(1, 1)
+        unload_row(0, "SS", 2)
+        turn_x(1, 0, 2)
         first_product(0, 1, 0, 2)
-        regroup((1, 1))
-        unload_x(1, 0, "S")
-        unload_x(1, 1, "S")
+        regroup_all((1, 1))
+        unload_row(1, "SS")
         quantize_x(0, 2, 4)
-        turn_x(1, 2)
-        turn_x(1, 3)
-        regroup((2, 0))
+        turn_x(1, 2, 4)
+        regroup_all((2, 0))
         quantize_x(1, 0, 2)
-        unload_x(1, 2, "S")
-        unload_x(1, 3, "S")
-        for b in range(2):
-            first_product(0, b, 2, 4)
-        regroup((2, 1))
+        unload_row(1, "SS", 2)
+        both(0, 2, 4)
+        regroup_all((2, 1))
         unload_t(0, 0, "S")
         unload_t(0, 1, "V")
-        for o in range(4):
-            turn_x(2, o)
+        turn_x(2)
         quantize_x(1, 2, 4)
-        regroup((3, 0))
-        unload_x(2, 0, "S")
-        unload_x(2, 1, "S")
-        unload_x(2, 2, "V")
-        unload_x(2, 3, "S")
-        for lo in (0, 2):
-            for b in range(2):
-                first_product(1, b, lo, lo + 2)
-        regroup((3, 1))
+        regroup_all((3, 0))
+        unload_row(2, "SSVS")
+        both(1, 0, 2)
+        both(1, 2, 4)
+        regroup_all((3, 1))
         quantize_x(2, 0, 2)
         unload_t(1, 0, "S")
-        for o in range(4):
-            turn_x(3, o)
-        turn_a(0, Z_BANK)
+        turn_x(3)
+        turn_a(0)
         unload_t(1, 1, "V")
         quantize_x(2, 2, 4)
-        unload_x(3, 0, "S")
-        unload_x(3, 1, "S")
-        regroup((4, 0))
+        unload_row(3, "SS")
+        regroup_all((4, 0))
         quantize_t(0)
-        unload_x(3, 2, "S")
-        unload_x(3, 3, "S")
+        unload_row(3, "SS", 2)
         quantize_x(3, 0, 2)
-        regroup((4, 1))
-        for lo in (0, 2):
-            for b in range(2):
-                first_product(2, b, lo, lo + 2)
-        turn_a(1, S_BANKS)
+        regroup_all((4, 1))
+        both(2, 0, 2)
+        both(2, 2, 4)
+        turn_a(1)
         unload_a(0, "S")
         unload_t(2, 0, "S")
         unload_a(1, "S")
-        j = 4
-        for o in range(4):
-            turn_x(j, o)
-        unload_t(j - 2, 1, "V")
-        quantize_x(j - 1, 2, 4)
+        turn_x(4)
+        unload_t(2, 1, "V")
+        quantize_x(3, 2, 4)
         quantize_a()
-        regroup_all(j + 1)
-        for o in range(4):
-            unload_x(j, o, "S")
-        quantize_x(j, 0, 2)
-        for lo in (0, 2):
-            for b in range(2):
-                first_product(j - 1, b, lo, lo + 2)
-        unload_t(j - 1, 0, "S")
-        j = 5
-        for o in range(4):
-            turn_x(j, o)
-        quantize_x(j - 1, 2, 4)
-        unload_t(j - 2, 1, "V")
+        regroup_all(5)
+        unload_row(4, "SSSS")
+        quantize_x(4, 0, 2)
+        both(3, 0, 2)
+        both(3, 2, 4)
+        unload_t(3, 0, "S")
+
+        turn_x(5)
         second_product(0)
-        share_regroup(j + 1, 8)
+        quantize_x(4, 2, 4)
+        regroup_back(6, "V", 0, 1)
+        regroup(6)
+        regroup_back(6, "G", 1, 16)
+        unload_t(3, 1, "V")
         add_c(0)
-        quantize_t(2)
-        for o in range(4):
-            unload_x(j, o, "S")
-        quantize_x(j, 0, 2)
-        for lo in (0, 2):
-            for b in range(2):
-                first_product(j - 1, b, lo, lo + 2)
-        unload_t(j - 1, 0, "S")
+        unload_row(5, "SSSS")
+        both(4, 0, 2)
+        both(4, 2, 4)
+        quantize_x(5, 0, 2)
+        PAIRED = 8
+        for j in range(6, PAIRED):
+            turn_x(j)
+            if j % 2 == 0:
+                quantize_x(j - 1, 2, 4)
+                regroup(j + 1, "V", 0, LEAD)
+                quantize_t(j - 4)
+                regroup_all(j + 1, "G", LEAD)
+                unload_t(j - 2, 0, "V")
+                unload_t(j - 2, 1, "V")
+                unload_row(j, "SSSS")
+                both(j - 1, 0, 2)
+                both(j - 1, 2, 4)
+                second_product(j - 4)
+                silu_store(j - 6)
+                quantize_x(j, 0, 2)
+                unload_t(j - 1, 0, "S")
+            else:
+                regroup(j + 1, "V", 0, LEAD)
+                quantize_x(j - 1, 2, 4)
+                regroup_all(j + 1, "G", LEAD)
+                if j + 1 == PAIRED:
+                    regroup_all(j + 2, "G")
+                unload_t(j - 2, 1, "V")
+                add_c(j - 5)
+                unload_row(j, "SSSS")
+                both(j - 1, 0, 2)
+                both(j - 1, 2, 4)
+                if j + 1 == PAIRED:
+                    unload_t(j - 1, 0, "V")
+                    unload_t(j - 1, 1, "V")
+                    silu_store(j - 5)
+                else:
+                    quantize_x(j, 0, 2)
+
+        j = PAIRED
+        turn_x(j)
+        unload_row(j, "SSSS")
+        turn_x(j + 1)
+        quantize_x(j - 1)
+        regroup(j + 2, "V", 0, LEAD)
+        quantize_t(j - 4)
+        regroup_all(j + 2, "G", LEAD)
+        regroup_all(j + 3, "G")
+        both(j - 1)
+        second_product(j - 4)
+        unload_row(j + 1, "VV")
+        unload_row(j + 1, "SS", 2)
+        unload_t(j - 1, 0, "V")
+        unload_t(j - 1, 1, "S")
+        add_c(j - 4)
+
+        for j in range(PAIRED + 2, NB - 2, 2):
+            turn_x(j)
+            unload_row(j, "SSSS")
+            turn_x(j + 1)
+            silu_store(j - 6)
+            quantize_x(j - 2)
+            quantize_x(j - 1)
+            regroup(j + 2, "V", 0, LEAD)
+            quantize_t(j - 4)
+            regroup_all(j + 2, "G", LEAD)
+            regroup_all(j + 3, "G")
+            both(j - 2)
+            both(j - 1)
+            unload_row(j + 1, "SS")
+            unload_t(j - 2, 0, "V")
+            second_product(j - 4)
+            unload_row(j + 1, "SS", 2)
+            unload_t(j - 2, 1, "V")
+            unload_t(j - 1, 0, "V")
+            unload_t(j - 1, 1, "S")
+            add_c(j - 4)
 
         last = NB - 1
-        done = 0
-        j = 6
-        for o in range(4):
-            turn_x(j, o)
-        second_product(j - 4)
-        quantize_x(j - 1, 2, 4)
-        share_regroup(j + 1)
-        unload_t(j - 2, 1, "V")
-        add_c(j - 4)
-        for o in range(4):
-            unload_x(j, o, "S")
-        quantize_x(j, 0, 2)
-        for lo in (0, 2):
-            for b in range(2):
-                first_product(j - 1, b, lo, lo + 2)
-        silu_store(0)
-        unload_t(j - 1, 0, "S")
-        j = 7
-        for o in range(4):
-            turn_x(j, o)
-        quantize_x(j - 1, 2, 4)
-        share_regroup(j + 1, 8)
-        unload_t(j - 2, 1, "V")
-        for o in range(4):
-            unload_x(j, o, "S")
-        quantize_x(j, 0, 2)
-        quantize_t(j - 3)
-        for lo in (0, 2):
-            for b in range(2):
-                first_product(j - 1, b, lo, lo + 2)
-        silu_store(2)
-        unload_t(j - 1, 0, "S")
-        j = 8
-        for o in range(4):
-            turn_x(j, o)
-        second_product(j - 4)
-        quantize_x(j - 1, 2, 4)
-        share_regroup(j + 1)
-        unload_t(j - 2, 1, "V")
-        add_c(j - 4)
-        for o in range(4):
-            unload_x(j, o, "S")
-        for lo in (0, 2):
-            for b in range(2):
-                first_product(j - 1, b, lo, lo + 2)
-        unload_t(j - 1, 0, "S")
-        silu_store(4)
-        j = 9
-        for o in range(4):
-            turn_x(j, o, ANY)
-        share_regroup(j + 1)
-        unload_t(j - 2, 1, "V")
-        for o in range(4):
-            unload_x(j, o, "VSSS"[o])
-            turn_x(j + 1, o, ANY)
-        quantize_x(j - 1, 0, 2)
-        quantize_x(j - 1, 2, 4)
-        quantize_t(j - 3)
-        regroup_all(j + 2)
-        regroup(j + 3, "V", 0, LEAD)
-        quantize_x(j, 0, 4)
-        for o in range(4):
-            unload_x(j + 1, o, "S")
-        for lo in (0, 2):
-            for b in range(2):
-                first_product(j - 1, b, lo, lo + 2, ANY)
-        unload_t(j - 1, 0, "S")
-        second_product(j - 3)
-        done = 6
-        for j in range(11, last - 2):
-            for o in range(4):
-                turn_x(j, o, ANY)
-            if j + 1 >= PLAIN:
-                regroup(j + 1, "G", LEAD, 16)
-            elif j + 1 >= NEAR:
-                regroup_back(j + 1, "V", 0, 1)
-                regroup(j + 1)
-                regroup_back(j + 1, "G", 1, 16)
-            unload_t(j - 3, 1, "V")
-            if j % 2 == 1:
-                add_c(j - 5)
-            if j + 1 < NEAR:
-                regroup(j + 1)
-            unload_x(j, 0, "V" if j % 2 == 0 and j + 1 >= NEAR else "S")
-            if j % 2 == 0:
-                quantize_t(j - 4)
-            if j + 1 < NEAR:
-                regroup_back(j + 1)
-            if PLAIN <= j + 2 < NB:
-                regroup(j + 2, "V", 0, LEAD)
-            quantize_x(j - 1, 0, 4)
-            for o in range(1, 4):
-                unload_x(j, o, "S")
-            if j > TURN + 1:
-                first_product(j - 2, 0, 0, 4, ANY)
-                unload_t(j - 2, 0, "S")
-            first_product(j - 2, 1, 0, 4, ANY)
-            if j % 2 == 0:
-                second_product(j - 4)
-                for k in range(done, min(done + (2 if j == TURN + 2 else 4), j - 4), 2):
-                    silu_store(k)
-                    done = k + 2
-
-        j = last - 2
-        for o in range(4):
-            turn_x(j, o, ANY)
-        regroup(j + 1, "G", LEAD, 16)
-        unload_t(j - 3, 1, "V")
-        add_c(j - 5)
-        regroup(j + 2, "V", 0, LEAD)
-        quantize_x(j - 1, 0, 2)
-        for o in range(4):
-            unload_x(j, o, "S")
-        for b in range(2):
-            first_product(j - 2, b, 0, 4, ANY)
-        regroup(j + 2, "G", LEAD, 16)
-        for b in range(2):
-            unload_t(j - 2, b, "V")
-        quantize_x(j - 1, 2, 4)
-
         j = last - 1
-        for o in range(4):
-            turn_x(j, o, ANY)
-        silu_store(j - 6)
-        for o in range(4):
-            unload_x(j, o, "S")
-            turn_x(last, o, ANY)
+        turn_x(j)
+        unload_row(j, "SSSS")
+        turn_x(j + 1)
+        quantize_x(j - 2)
+        quantize_x(j - 1)
         quantize_t(j - 4)
-        quantize_x(j - 1, 0, 4)
-        for o in range(4):
-            unload_x(last, o, "SSSV"[o])
-        for b in range(2):
-            first_product(j - 2, b, 0, 4, ANY)
+        unload_row(last, "SSSS")
+        quantize_x(j)
+        both(j - 2)
+        both(j - 1)
+        unload_t(j - 2, 0, "V")
         second_product(j - 4)
-        quantize_x(j, 0, 4)
-        for b in range(2):
-            first_product(j - 1, b, 0, 4, ANY)
-        quantize_x(last, 0, 4)
+        quantize_x(last)
+        unload_t(j - 2, 1, "S")
+        unload_t(j - 1, 0, "S")
+        unload_t(j - 1, 1, "S")
+        both(j)
         add_c(j - 4)
-        for n in (j - 2, j - 1):
-            for b in range(2):
-                unload_t(n, b, "S")
-        for b in range(2):
-            first_product(j, b, 0, 4, ANY)
+        silu_store(j - 6)
         quantize_t(last - 3)
-        unload_t(j, 0, "S")
-        unload_t(j, 1, "S")
-        silu_store(j - 4)
-        for b in range(2):
-            first_product(last, b, 0, 4, ANY)
+        unload_t(last - 1, 0, "S")
+        unload_t(last - 1, 1, "S")
+        both(last)
         second_product(last - 3)
+        silu_store(last - 5)
         unload_t(last, 0, "V")
         quantize_t(last - 1)
-        second_product(last - 1, ANY)
+        second_product(last - 1)
         unload_t(last, 1, "S")
         quantize_t(last, 0, 1)
         last_second_product(last, 0)

@@ -386,10 +386,10 @@ def tile_ranktwokroneckersumlayer_t_kernel(tc, x, b1, b2_bytes, b2_scale, a1, a2
         warm_tensor(3)
         reorder_b(0, b1_raw)
         regroup_all((0, 0))
-        unload_b(0, "S")
         turn_x(0, 0, 2)
         for i in range(8):
             widen_b2(i // 2, i % 2, "V" if i < 5 else "S")
+        unload_b(0, "S")
         reorder_b(1, b2_w)
         unload_row(0, "VS")
         regroup_all((0, 1))

@@ -363,7 +363,8 @@ def tile_ranktwokroneckersumlayer_t_kernel(tc, x, b1, b2_bytes, b2_scale, a1, a2
             for i in range(len(engs)):
                 unload_x(n, lo + i, engs[i])
 
-        LEAD = 3
+        LEAD = 12
+        LEAD_ONE = 6
 
         load_b1()
         for n in range(NB):
@@ -467,9 +468,9 @@ def tile_ranktwokroneckersumlayer_t_kernel(tc, x, b1, b2_bytes, b2_scale, a1, a2
             turn_x(j)
             if j % 2 == 0:
                 quantize_x(j - 1, 2, 4)
-                regroup(j + 1, "V", 0, LEAD)
+                regroup(j + 1, "V", 0, LEAD_ONE)
                 quantize_t(j - 4)
-                regroup_all(j + 1, "G", LEAD)
+                regroup_all(j + 1, "G", LEAD_ONE)
                 unload_t(j - 2, 0, "V")
                 unload_t(j - 2, 1, "V")
                 unload_row(j, "SSSS")
@@ -480,9 +481,10 @@ def tile_ranktwokroneckersumlayer_t_kernel(tc, x, b1, b2_bytes, b2_scale, a1, a2
                 quantize_x(j, 0, 2)
                 unload_t(j - 1, 0, "S")
             else:
-                regroup(j + 1, "V", 0, LEAD)
+                lead = LEAD if j + 1 == PAIRED else LEAD_ONE
+                regroup(j + 1, "V", 0, lead)
                 quantize_x(j - 1, 2, 4)
-                regroup_all(j + 1, "G", LEAD)
+                regroup_all(j + 1, "G", lead)
                 if j + 1 == PAIRED:
                     regroup_all(j + 2, "G")
                 unload_t(j - 2, 1, "V")

@@ -13,7 +13,7 @@ PITCH = 72 * PIECE
 WIDE_PITCH = 136 * PIECE
 DATA = (FREE + 1) * PIECE
 HALVED = 5
-PLAIN = 7
+PLAIN = 8
 F32 = mybir.dt.float32
 BF16 = mybir.dt.bfloat16
 U32 = mybir.dt.uint32
@@ -82,7 +82,7 @@ def tile_ranktwokroneckersumlayer_t_kernel(tc, x, b1, b2_bytes, b2_scale, a1, a2
             return key in range(PLAIN, NB)
 
         def rows(key, skip=0):
-            pitch, count = (PITCH, 4) if plain(key) else (WIDE_PITCH, 2 if key in range(NB) else 1)
+            pitch, count = (PITCH, 4) if plain(key) else (WIDE_PITCH, 2) if key in range(NB) else (PITCH, 2)
             return xs[key][:, skip * PIECE : skip * PIECE + count * pitch].rearrange("p (d y) -> p d y", y=pitch)
 
         def load_x(n):
@@ -94,8 +94,8 @@ def tile_ranktwokroneckersumlayer_t_kernel(tc, x, b1, b2_bytes, b2_scale, a1, a2
                 nc.sync.dma_start(out=rows(n)[:, :, DATA:], in_=x[n].rearrange("(m d f) k -> m d (f k)", d=2, f=2))
 
         def load_half(n, d):
-            xs[n, d] = hpool.tile([P, WIDE_PITCH + DATA], BF16, name="x_h", align_bytes=256)
-            nc.sync.dma_start(out=xs[n, d][:, DATA:WIDE_PITCH], in_=x[n].rearrange("(m d f) k -> d m (f k)", d=2, f=2)[d])
+            xs[n, d] = hpool.tile([P, 2 * PITCH], BF16, name="x_h", align_bytes=256)
+            nc.sync.dma_start(out=rows((n, d))[:, :, DATA:], in_=x[n].rearrange("(m d f) k -> d m f k", d=2, f=2)[d])
 
         def load_a(b):
             nc.sync.dma_start(out=a_raw[:, b, :], in_=(a1, a2)[b].rearrange("(m h) k -> m (h k)", h=2))
@@ -187,12 +187,8 @@ def tile_ranktwokroneckersumlayer_t_kernel(tc, x, b1, b2_bytes, b2_scale, a1, a2
 
         def stepped(view, w, first, far):
             end = first + far + 31
-            count = view.shape[1]
             view = view[:, :, w * (end - 2 * far) : w * end].rearrange("p d (r y) -> p d r y", r=2)[:, :, :, (far - 32) * w :]
-            view = view.rearrange("p d r (i t w) -> p d i r t w", t=2, w=w)[:, :, :, :, 1, :]
-            if count == 1:
-                view = view[:, 0].rearrange("p i r (h e) -> p h i r e", h=2)
-            return view
+            return view.rearrange("p d r (i t w) -> p d i r t w", t=2, w=w)[:, :, :, :, 1, :]
 
         def regroup(key, eng="V", lo=0, hi=16):
             view, w, engine = rows(key), PIECE, nc.vector
@@ -210,7 +206,7 @@ def tile_ranktwokroneckersumlayer_t_kernel(tc, x, b1, b2_bytes, b2_scale, a1, a2
 
         def regroup_all(key, eng="V", lo=0):
             regroup(key, eng, lo, 16)
-            if not plain(key):
+            if key in range(HALVED, PLAIN):
                 regroup_back(key, eng)
 
         def turn_x(n, lo=0, hi=4):
@@ -221,7 +217,7 @@ def tile_ranktwokroneckersumlayer_t_kernel(tc, x, b1, b2_bytes, b2_scale, a1, a2
                 if not plain(n):
                     start, windows = WIDE_PITCH * d, ((0, 33), (98, 65))[f]
                 if n < HALVED:
-                    key, start = (n, d), 0
+                    key, start, windows = (n, d), PITCH * f, (0, 33)
                 words = xs[key][:].bitcast(F32)
                 for g in range(2):
                     for u in range(2):
@@ -245,23 +241,25 @@ def tile_ranktwokroneckersumlayer_t_kernel(tc, x, b1, b2_bytes, b2_scale, a1, a2
             cols = slice(256 * lo, 256 * hi)
             nc.vector.quantize_mx(out=q[:, cols].bitcast(FP8X4), scales=sc[:, cols], in_=grp[n][:, 1024 * lo : 1024 * hi])
 
-        def first_product(n, b, lo=0, hi=4):
+        def first_product(n, which, lo=0, hi=4):
             if lo == 0:
-                s1[n, b] = take(("t", n, b), [P, 4, P])
+                for b in which:
+                    s1[n, b] = take(("t", n, b), [P, 4, P])
             q, sc = codes[n]
             for s in range(lo, hi):
                 for g in range(2):
                     cols = slice(256 * s + P * g, 256 * s + P * (g + 1))
-                    bcols = slice(256 * b + P * g, 256 * b + P * (g + 1))
-                    nc.tensor.matmul_mx(
-                        out=s1[n, b][:, s, :],
-                        lhsT=q[:, cols].bitcast(FP8X4),
-                        lhsT_scale=sc[:, cols],
-                        rhs=b_codes[:, bcols].bitcast(FP8X4),
-                        rhs_scale=b_scales[:, bcols],
-                        start=(g == 0),
-                        stop=(g == 1),
-                    )
+                    for b in which:
+                        bcols = slice(256 * b + P * g, 256 * b + P * (g + 1))
+                        nc.tensor.matmul_mx(
+                            out=s1[n, b][:, s, :],
+                            lhsT=q[:, cols].bitcast(FP8X4),
+                            lhsT_scale=sc[:, cols],
+                            rhs=b_codes[:, bcols].bitcast(FP8X4),
+                            rhs_scale=b_scales[:, bcols],
+                            start=(g == 0),
+                            stop=(g == 1),
+                        )
 
         def group(k):
             return (k - k % 2, 2) if k < NB - 2 else (k, 1)
@@ -356,15 +354,14 @@ def tile_ranktwokroneckersumlayer_t_kernel(tc, x, b1, b2_bytes, b2_scale, a1, a2
             nc.sync.dma_start(out=out[n].rearrange("(m h) q -> m (h q)", h=2), in_=o[:].rearrange("p h q -> p (h q)"))
 
         def both(n, lo=0, hi=4):
-            for b in range(2):
-                first_product(n, b, lo, hi)
+            first_product(n, (0, 1), lo, hi)
 
         def unload_row(n, engs, lo=0):
             for i in range(len(engs)):
                 unload_x(n, lo + i, engs[i])
 
-        LEAD = 12
-        LEAD_ONE = 6
+        LEAD = 10
+        LEAD_ONE = 5
 
         load_b1()
         for n in range(NB):
@@ -398,12 +395,12 @@ def tile_ranktwokroneckersumlayer_t_kernel(tc, x, b1, b2_bytes, b2_scale, a1, a2
         unload_b(1, "S")
         turn_x(0, 2, 4)
         quantize_x(0, 0, 2)
-        first_product(0, 0, 0, 2)
+        first_product(0, (0,), 0, 2)
         regroup_all((1, 0))
         quantize_b(1)
         unload_row(0, "SS", 2)
         turn_x(1, 0, 2)
-        first_product(0, 1, 0, 2)
+        first_product(0, (1,), 0, 2)
         regroup_all((1, 1))
         unload_row(1, "SS")
         quantize_x(0, 2, 4)
@@ -562,19 +559,20 @@ def tile_ranktwokroneckersumlayer_t_kernel(tc, x, b1, b2_bytes, b2_scale, a1, a2
         quantize_t(last - 3)
         unload_t(last - 1, 0, "S")
         unload_t(last - 1, 1, "S")
-        both(last)
+        first_product(last, (0,))
+        first_product(last, (1,))
         second_product(last - 3)
-        silu_store(last - 5)
         unload_t(last, 0, "V")
-        quantize_t(last - 1)
-        second_product(last - 1)
         unload_t(last, 1, "S")
         quantize_t(last, 0, 1)
         last_second_product(last, 0)
+        quantize_t(last - 1)
+        second_product(last - 1)
+        silu_store(last - 5)
         add_c_one(last - 3, 0)
-        add_c_one(last - 3, 1)
         quantize_t(last, 1, 2)
         last_second_product(last, 1)
+        add_c_one(last - 3, 1)
         add_c(last - 1)
         silu_store_one(last - 3)
         silu_store_one(last - 2)

@@ -13,7 +13,7 @@ PITCH = 72 * PIECE
 WIDE_PITCH = 136 * PIECE
 DATA = (FREE + 1) * PIECE
 HALVED = 5
-PLAIN = 8
+PLAIN = 7
 F32 = mybir.dt.float32
 BF16 = mybir.dt.bfloat16
 U32 = mybir.dt.uint32
@@ -354,13 +354,14 @@ def tile_ranktwokroneckersumlayer_t_kernel(tc, x, b1, b2_bytes, b2_scale, a1, a2
             nc.sync.dma_start(out=out[n].rearrange("(m h) q -> m (h q)", h=2), in_=o[:].rearrange("p h q -> p (h q)"))
 
         def both(n, lo=0, hi=4):
-            first_product(n, (0, 1), lo, hi)
+            for b in range(2):
+                first_product(n, (b,), lo, hi)
 
         def unload_row(n, engs, lo=0):
             for i in range(len(engs)):
                 unload_x(n, lo + i, engs[i])
 
-        LEAD = 10
+        LEAD = 8
         LEAD_ONE = 5
 
         load_b1()
@@ -454,9 +455,9 @@ def tile_ranktwokroneckersumlayer_t_kernel(tc, x, b1, b2_bytes, b2_scale, a1, a2
         regroup_back(6, "V", 0, 1)
         regroup(6)
         regroup_back(6, "G", 1, 16)
-        unload_t(3, 1, "V")
         add_c(0)
         unload_row(5, "SSSS")
+        unload_t(3, 1, "S")
         both(4, 0, 2)
         both(4, 2, 4)
         quantize_x(5, 0, 2)
@@ -513,27 +514,50 @@ def tile_ranktwokroneckersumlayer_t_kernel(tc, x, b1, b2_bytes, b2_scale, a1, a2
         unload_t(j - 1, 1, "S")
         add_c(j - 4)
 
-        for j in range(PAIRED + 2, NB - 2, 2):
-            turn_x(j)
-            unload_row(j, "SSSS")
-            turn_x(j + 1)
-            silu_store(j - 6)
-            quantize_x(j - 2)
-            quantize_x(j - 1)
-            regroup(j + 2, "V", 0, LEAD)
-            quantize_t(j - 4)
-            regroup_all(j + 2, "G", LEAD)
-            regroup_all(j + 3, "G")
-            both(j - 2)
-            both(j - 1)
-            unload_row(j + 1, "SS")
-            unload_t(j - 2, 0, "V")
-            second_product(j - 4)
-            unload_row(j + 1, "SS", 2)
-            unload_t(j - 2, 1, "V")
-            unload_t(j - 1, 0, "V")
-            unload_t(j - 1, 1, "S")
-            add_c(j - 4)
+
+        j = 10
+        turn_x(j)
+        unload_row(j, "SSSS")
+        turn_x(j + 1)
+        silu_store(j - 6)
+        quantize_x(j - 2)
+        quantize_x(j - 1)
+        regroup(j + 2, "V", 0, LEAD)
+        quantize_t(j - 4)
+        regroup_all(j + 2, "G", LEAD)
+        regroup_all(j + 3, "G")
+        both(j - 2)
+        both(j - 1)
+        unload_row(j + 1, "SS")
+        unload_t(j - 2, 0, "V")
+        second_product(j - 4)
+        unload_row(j + 1, "SS", 2)
+        unload_t(j - 2, 1, "V")
+        unload_t(j - 1, 0, "V")
+        unload_t(j - 1, 1, "S")
+        add_c(j - 4)
+
+        j = 12
+        turn_x(j)
+        unload_row(j, "SSSS")
+        turn_x(j + 1)
+        silu_store(j - 6)
+        quantize_x(j - 2)
+        quantize_x(j - 1)
+        regroup(j + 2, "V", 0, LEAD)
+        quantize_t(j - 4)
+        regroup_all(j + 2, "G", LEAD)
+        regroup_all(j + 3, "G")
+        both(j - 2)
+        both(j - 1)
+        unload_row(j + 1, "SS")
+        unload_t(j - 2, 0, "V")
+        second_product(j - 4)
+        unload_row(j + 1, "SS", 2)
+        unload_t(j - 2, 1, "V")
+        unload_t(j - 1, 0, "V")
+        unload_t(j - 1, 1, "S")
+        add_c(j - 4)
 
         last = NB - 1
         j = last - 1
@@ -562,17 +586,17 @@ def tile_ranktwokroneckersumlayer_t_kernel(tc, x, b1, b2_bytes, b2_scale, a1, a2
         first_product(last, (0,))
         first_product(last, (1,))
         second_product(last - 3)
+        silu_store(last - 5)
         unload_t(last, 0, "V")
+        quantize_t(last - 1)
+        second_product(last - 1)
         unload_t(last, 1, "S")
         quantize_t(last, 0, 1)
         last_second_product(last, 0)
-        quantize_t(last - 1)
-        second_product(last - 1)
-        silu_store(last - 5)
         add_c_one(last - 3, 0)
+        add_c_one(last - 3, 1)
         quantize_t(last, 1, 2)
         last_second_product(last, 1)
-        add_c_one(last - 3, 1)
         add_c(last - 1)
         silu_store_one(last - 3)
         silu_store_one(last - 2)

from contextlib import ExitStack

import concourse.mybir as mybir
from concourse.masks import make_identity

FLOPS = 2 * 16 * 512 * 1024 * 256 + 2 * 2 * 16 * 256 * 512 * 128

P = 128
NB = 16
PIECE = 16
FREE = 7
PITCH = 72 * PIECE
WIDE_PITCH = 136 * PIECE
DATA = (FREE + 1) * PIECE
HALVED = 5
PLAIN = 7
F32 = mybir.dt.float32
BF16 = mybir.dt.bfloat16
U32 = mybir.dt.uint32
U8 = mybir.dt.uint8
FP8 = mybir.dt.float8_e4m3fn
FP8X4 = mybir.dt.float8_e4m3fn_x4
ACT = mybir.ActivationFunctionType
ALU = mybir.AluOpType


def tile_ranktwokroneckersumlayer_t_kernel(tc, x, b1, b2_bytes, b2_scale, a1, a2, c, out):
    nc = tc.nc

    with ExitStack() as ctx:
        keep = ctx.enter_context(tc.tile_pool(name="keep", bufs=1))
        xpool = ctx.enter_context(tc.tile_pool(name="xpool", bufs=10))
        hpool = ctx.enter_context(tc.tile_pool(name="hpool", bufs=2 * HALVED))
        gpool = ctx.enter_context(tc.tile_pool(name="gpool", bufs=3))
        qpool = ctx.enter_context(tc.tile_pool(name="qpool", bufs=3))
        tpool = ctx.enter_context(tc.tile_pool(name="tpool", bufs=2))
        zpool = ctx.enter_context(tc.tile_pool(name="zpool", bufs=5))
        psum = ctx.enter_context(tc.psum_pool(name="psum", bufs=1))
        ctx.enter_context(tc.manual_schedule())

        ident = keep.tile([P, P], F32, name="ident")
        table = keep.tile([P, 1], F32, name="table")
        zero = keep.tile([P, 512], BF16, name="zero")
        pick = keep.tile([P, 2, 2, P], BF16, name="pick")
        b2_raw = keep.tile([P, 4, 2, P], U8, name="b2_raw", align_bytes=256)
        b2_s = keep.tile([P, 4, 2], F32, name="b2_s")
        b2_w = keep.tile([P, 4, 2, P], BF16, name="b2_w")
        b1_raw = keep.tile([P, 4, 2, P], BF16, name="b1_raw", align_bytes=256)
        b_grp = keep.tile([P, 2048], BF16, name="b_grp", align_bytes=64)
        b_codes = keep.tile([P, 512], U32, name="b_codes", align_bytes=64)
        b_scales = keep.tile([P, 512], U8, name="b_scales", align_bytes=64)
        a_raw = keep.tile([P, 2, 1024], BF16, name="a_raw", align_bytes=256)
        a_grp = keep.tile([P, 2048], BF16, name="a_grp", align_bytes=64)
        a_codes = keep.tile([P, 512], U32, name="a_codes", align_bytes=64)
        a_scales = keep.tile([P, 512], U8, name="a_scales", align_bytes=64)
        c_t = keep.tile([P, 2, P], BF16, name="c_t", align_bytes=256)

        xs = {}
        banks = {}
        grp = {}
        codes = {}
        s1 = {}
        tg = {}
        tcodes = {}
        zb = {}
        zs = {}

        idle = list(range(8))
        held = {}

        def take(key, shape, dtype=F32, k=None):
            if k is None:
                k = idle[0]
            idle.remove(k)
            held[key] = k
            return psum.tile(shape, dtype, name="bank%d" % k)

        def give(key):
            idle.append(held[key])

        def plain(key):
            return key in range(PLAIN, NB)

        def rows(key, skip=0):
            pitch, count = (PITCH, 4) if plain(key) else (WIDE_PITCH, 2) if key in range(NB) else (PITCH, 2)
            return xs[key][:, skip * PIECE : skip * PIECE + count * pitch].rearrange("p (d y) -> p d y", y=pitch)

        def load_x(n):
            if plain(n):
                xs[n] = xpool.tile([P, 4 * PITCH], BF16, name="x_t", align_bytes=256)
                nc.sync.dma_start(out=rows(n)[:, :, DATA:], in_=x[n].rearrange("(m s) k -> m s k", s=4))
            else:
                xs[n] = xpool.tile([P, 2 * WIDE_PITCH + DATA], BF16, name="x_t", align_bytes=256)
                nc.sync.dma_start(out=rows(n)[:, :, DATA:], in_=x[n].rearrange("(m d f) k -> m d (f k)", d=2, f=2))

        def load_half(n, d):
            xs[n, d] = hpool.tile([P, 2 * PITCH], BF16, name="x_h", align_bytes=256)
            nc.sync.dma_start(out=rows((n, d))[:, :, DATA:], in_=x[n].rearrange("(m d f) k -> d m f k", d=2, f=2)[d])

        def load_a(b):
            nc.sync.dma_start(out=a_raw[:, b, :], in_=(a1, a2)[b].rearrange("(m h) k -> m (h k)", h=2))

        def load_b1():
            nc.sync.dma_start(out=b1_raw[:], in_=b1.rearrange("(g p t) q -> p g t q", g=4, t=2))

        def load_scale():
            nc.sync.dma_start(out=b2_s[:], in_=b2_scale.rearrange("(g p t) o -> p g (t o)", g=4, t=2))

        def load_b2():
            nc.sync.dma_start(out=b2_raw[:], in_=b2_bytes.rearrange("(g p t) q -> p g t q", g=4, t=2))

        def load_c():
            nc.sync.dma_start(out=c_t[:], in_=c.rearrange("(m h) q -> m h q", h=2))

        def constants():
            nc.vector.memset(ident[:], 0.0)
            make_identity(nc, ident[:], nomemset=True)
            nc.vector.memset(table[:], 0.0)
            nc.vector.memset(zero[:], 0.0)
            nc.scalar.activation(out=table[:], in_=table[:], func=ACT.Silu)
            nc.vector.memset(pick[:], 0.0)
            halves = ident[:].rearrange("p (j o i) -> p j o i", o=2, i=8)
            picks = pick[:].rearrange("p u r (j o i) -> p u r j o i", o=2, i=8)
            nc.vector.tensor_copy(out=picks[:, 0, 0, :, 1, :], in_=halves[:, :, 0, :])
            nc.gpsimd.tensor_copy(out=picks[:, 1, 1, :, 0, :].bitcast(U32), in_=picks[:, 0, 0, :, 1, :].bitcast(U32))
            nc.vector.tensor_copy(out=picks[:, 0, 1, :, 0, :], in_=halves[:, :, 1, :])
            nc.vector.tensor_copy(out=picks[:, 1, 0, :, 1, :], in_=halves[:, :, 1, :])

        def warm_tensor(count):
            for i in range(count):
                bank = take("warm", [P, 512], k=7)
                nc.tensor.matmul(bank[:], lhsT=zero[:, :P], rhs=zero[:], start=True, stop=True)
                give("warm")

        def widen_b2(g, t, eng):
            src = b2_raw[:, g, t, :].bitcast(FP8)
            if eng == "V":
                nc.vector.tensor_scalar(
                    out=b2_w[:, g, t, :], in0=src, scalar1=b2_s[:, g, t : t + 1], scalar2=None, op0=ALU.mult
                )
            else:
                nc.scalar.activation(out=b2_w[:, g, t, :], in_=src, func=ACT.Copy, scale=b2_s[:, g, t : t + 1])

        def copy(eng, dst, src):
            if eng == "S":
                nc.scalar.copy(out=dst, in_=src)
            else:
                nc.vector.tensor_copy(out=dst, in_=src)

        def reorder_b(b, src):
            bank = take(("b", b), [P, 2, P, 2, 2], BF16, k=5 + b)
            banks["b", b] = bank
            for u in range(2):
                for g in range(2):
                    for r in range(2):
                        nc.tensor.matmul(
                            bank[:, g, :, u, :],
                            lhsT=pick[:, u, r, :],
                            rhs=src[:, 2 * r + g, :, :].rearrange("p e q -> p q e"),
                            start=(r == 0),
                            stop=(r == 1),
                        )

        def unload_b(b, eng):
            copy(eng, b_grp[:, 1024 * b : 1024 * (b + 1)], banks["b", b][:].rearrange("p g q u e -> p (g q u e)"))
            give(("b", b))

        def quantize_b(b):
            cols = slice(256 * b, 256 * (b + 1))
            nc.vector.quantize_mx(out=b_codes[:, cols].bitcast(FP8X4), scales=b_scales[:, cols], in_=b_grp[:, 1024 * b : 1024 * (b + 1)])

        def turn_a(b):
            bank = take(("a", b), [P, 4, P])
            w = a_raw[:, b, :].bitcast(F32)
            for h in range(2):
                for u in range(2):
                    nc.tensor.transpose(bank[:, 2 * h + u, :], w[:, 256 * h + u : 256 * (h + 1) : 2], ident[:])
            banks["a", b] = bank

        def unload_a(b, eng):
            dst = a_grp[:].bitcast(F32)[:, 512 * b : 512 * (b + 1)].rearrange("p (h m u) -> p h m u", h=2, u=2)
            copy(eng, dst, banks["a", b][:].rearrange("p (h u) m -> p h m u", h=2))
            give(("a", b))

        def quantize_a():
            nc.vector.quantize_mx(out=a_codes[:].bitcast(FP8X4), scales=a_scales[:], in_=a_grp[:])

        def stepped(view, w, first, far):
            end = first + far + 31
            view = view[:, :, w * (end - 2 * far) : w * end].rearrange("p d (r y) -> p d r y", r=2)[:, :, :, (far - 32) * w :]
            return view.rearrange("p d r (i t w) -> p d i r t w", t=2, w=w)[:, :, :, :, 1, :]

        def regroup(key, eng="V", lo=0, hi=16):
            view, w, engine = rows(key), PIECE, nc.vector
            if eng == "G":
                view, w, engine = view.bitcast(U32), PIECE // 2, nc.gpsimd
            dst, src = stepped(view, w, FREE, 34), stepped(view, w, FREE + 2, 32)[:, :, :, ::-1, :]
            engine.tensor_copy(out=dst[:, :, lo:hi], in_=src[:, :, lo:hi])

        def regroup_back(key, eng="V", lo=0, hi=16):
            view, w, engine = rows(key, FREE + 1), PIECE, nc.vector
            if eng == "G":
                view, w, engine = view.bitcast(U32), PIECE // 2, nc.gpsimd
            dst, src = stepped(view, w, 64, 34)[:, :, ::-1, ::-1, :], stepped(view, w, 64, 32)[:, :, ::-1, :, :]
            engine.tensor_copy(out=dst[:, :, lo:hi], in_=src[:, :, lo:hi])

        def regroup_all(key, eng="V", lo=0):
            regroup(key, eng, lo, 16)
            if key in range(HALVED, PLAIN):
                regroup_back(key, eng)

        def turn_x(n, lo=0, hi=4):
            for s in range(lo, hi):
                d, f = divmod(s, 2)
                bank = take(("x", n, s), [P, 4, P])
                key, start, windows = n, PITCH * s, (0, 33)
                if not plain(n):
                    start, windows = WIDE_PITCH * d, ((0, 33), (98, 65))[f]
                if n < HALVED:
                    key, start, windows = (n, d), PITCH * f, (0, 33)
                words = xs[key][:].bitcast(F32)
                for g in range(2):
                    for u in range(2):
                        at = (start + PIECE * (FREE + windows[u] + 16 * g)) // 2
                        nc.tensor.transpose(bank[:, 2 * g + u, :], words[:, at : at + P], ident[:])
                banks[n, s] = bank

        def unload_x(n, s, eng):
            if n not in grp:
                grp[n] = gpool.tile([P, 4096], BF16, name="x_g", align_bytes=64)
            dst = grp[n][:].bitcast(F32)[:, 512 * s : 512 * (s + 1)].rearrange("p (g m u) -> p g m u", g=2, u=2)
            copy(eng, dst, banks[n, s][:].rearrange("p (g u) m -> p g m u", g=2))
            give(("x", n, s))

        def quantize_x(n, lo=0, hi=4):
            if lo == 0:
                q = qpool.tile([P, 1024], U32, name="x_q", align_bytes=64)
                sc = qpool.tile([P, 1024], U8, name="x_s", align_bytes=64)
                codes[n] = (q, sc)
            q, sc = codes[n]
            cols = slice(256 * lo, 256 * hi)
            nc.vector.quantize_mx(out=q[:, cols].bitcast(FP8X4), scales=sc[:, cols], in_=grp[n][:, 1024 * lo : 1024 * hi])

        def first_product(n, which, lo=0, hi=4):
            if lo == 0:
                for b in which:
                    s1[n, b] = take(("t", n, b), [P, 4, P])
            q, sc = codes[n]
            for s in range(lo, hi):
                for g in range(2):
                    cols = slice(256 * s + P * g, 256 * s + P * (g + 1))
                    for b in which:
                        bcols = slice(256 * b + P * g, 256 * b + P * (g + 1))
                        nc.tensor.matmul_mx(
                            out=s1[n, b][:, s, :],
                            lhsT=q[:, cols].bitcast(FP8X4),
                            lhsT_scale=sc[:, cols],
                            rhs=b_codes[:, bcols].bitcast(FP8X4),
                            rhs_scale=b_scales[:, bcols],
                            start=(g == 0),
                            stop=(g == 1),
                        )

        def group(k):
            return (k - k % 2, 2) if k < NB - 2 else (k, 1)

        def unload_t(n, b, eng):
            first, size = group(n)
            if first not in tg:
                pool = keep if n == NB - 1 else tpool
                tg[first] = pool.tile([P, 1024 * size], BF16, name="t_g", align_bytes=64)
            lo = 512 * (size * b + n - first)
            dst = tg[first][:, lo : lo + 512].rearrange("p (q i s) -> p q s i", i=2, s=4)
            copy(eng, dst, s1[n, b][:].rearrange("p s (q i) -> p q s i", i=2))
            give(("t", n, b))

        def quantize_t(n, lo=0, hi=2):
            first, size = group(n)
            if lo == 0:
                pool = keep if n == NB - 1 else tpool
                q = pool.tile([P, 256 * size], U32, name="t_q", align_bytes=64)
                sc = pool.tile([P, 256 * size], U8, name="t_s", align_bytes=64)
                tcodes[first] = (q, sc)
            q, sc = tcodes[first]
            cols = slice(P * size * lo, P * size * hi)
            nc.vector.quantize_mx(out=q[:, cols].bitcast(FP8X4), scales=sc[:, cols], in_=tg[first][:, 4 * cols.start : 4 * cols.stop])

        def second_pass(bank, first, size, h, b):
            q, sc = tcodes[first]
            acols = slice(P * (2 * b + h), P * (2 * b + h + 1))
            tcols = slice(P * size * b, P * size * (b + 1))
            nc.tensor.matmul_mx(
                out=bank,
                lhsT=a_codes[:, acols].bitcast(FP8X4),
                lhsT_scale=a_scales[:, acols],
                rhs=q[:, tcols].bitcast(FP8X4),
                rhs_scale=sc[:, tcols],
                start=(b == 0),
                stop=(b == 1),
            )

        def second_product(n):
            first, size = group(n)
            zb[first] = take(("z", first), [P, 2, P * size])
            for h in range(2):
                for b in range(2):
                    second_pass(zb[first][:, h, :], first, size, h, b)

        def last_second_product(n, b):
            for h in range(2):
                if b == 0:
                    zb[n, h] = take(("z", n, h), [P, P])
                second_pass(zb[n, h][:], n, 1, h, b)

        def last_add_c(n, h):
            z = zpool.tile([P, P], F32, name="z_s")
            nc.vector.tensor_tensor(out=z[:], in0=zb[n, h][:], in1=c_t[:, h, :], op=ALU.add)
            zs[n, h] = z

        def last_silu_store(n, h):
            o = zpool.tile([P, P], F32, name="o_last", bufs=2, align_bytes=256)
            nc.scalar.activation(out=o[:], in_=zs[n, h][:], func=ACT.Silu)
            queue = nc.scalar if h == 1 else nc.sync
            queue.dma_start(out=out[n].rearrange("(m h) q -> h m q", h=2)[h], in_=o[:])

        def add_c(n):
            first, size = group(n)
            z = zpool.tile([P, size, 2, P], F32, name="z_s")
            nc.vector.tensor_tensor(
                out=z[:],
                in0=zb[first][:].rearrange("p h (n q) -> p n h q", n=size),
                in1=c_t[:].unsqueeze(1).to_broadcast([P, size, 2, P]),
                op=ALU.add,
            )
            zs[first] = z
            give(("z", first))

        def silu_store(n):
            first, size = group(n)
            o = zpool.tile([P, size, 2, P], F32, name="o_t", align_bytes=256)
            nc.scalar.activation(out=o[:], in_=zs[first][:], func=ACT.Silu)
            nc.sync.dma_start(
                out=out[first : first + size].rearrange("n (m h) q -> m n (h q)", h=2), in_=o[:].rearrange("p n h q -> p n (h q)")
            )

        def add_c_one(first, i):
            z = zpool.tile([P, 2, P], F32, name="z_s")
            nc.vector.tensor_tensor(out=z[:], in0=zb[first][:, :, P * i : P * (i + 1)], in1=c_t[:], op=ALU.add)
            zs[first + i] = z

        def silu_store_one(n):
            o = zpool.tile([P, 2, P], F32, name="o_t", align_bytes=256)
            nc.scalar.activation(out=o[:], in_=zs[n][:], func=ACT.Silu)
            nc.sync.dma_start(out=out[n].rearrange("(m h) q -> m (h q)", h=2), in_=o[:].rearrange("p h q -> p (h q)"))

        def both(n, lo=0, hi=4):
            for b in range(2):
                first_product(n, (b,), lo, hi)

        def unload_row(n, engs, lo=0):
            for i in range(len(engs)):
                unload_x(n, lo + i, engs[i])

        LEAD = 8
        LEAD_ONE = 5

        load_b1()
        for n in range(NB):
            if n < HALVED:
                load_half(n, 0)
                if n == 0:
                    load_scale()
                    load_b2()
                if n == 4:
                    load_a(1)
                load_half(n, 1)
            else:
                load_x(n)
            if n == 3:
                load_a(0)
            if n == 5:
                load_c()

        constants()
        warm_tensor(3)
        reorder_b(0, b1_raw)
        regroup_all((0, 0))
        turn_x(0, 0, 2)
        for i in range(8):
            widen_b2(i // 2, i % 2, "V" if i < 5 else "S")
        unload_b(0, "S")
        reorder_b(1, b2_w)
        unload_row(0, "VS")
        regroup_all((0, 1))
        quantize_b(0)
        unload_b(1, "S")
        turn_x(0, 2, 4)
        quantize_x(0, 0, 2)
        first_product(0, (0,), 0, 2)
        regroup_all((1, 0))
        quantize_b(1)
        unload_row(0, "SS", 2)
        turn_x(1, 0, 2)
        first_product(0, (1,), 0, 2)
        regroup_all((1, 1))
        unload_row(1, "SS")
        quantize_x(0, 2, 4)
        turn_x(1, 2, 4)
        regroup_all((2, 0))
        quantize_x(1, 0, 2)
        unload_row(1, "SS", 2)
        both(0, 2, 4)
        regroup_all((2, 1))
        unload_t(0, 0, "S")
        unload_t(0, 1, "V")
        turn_x(2)
        quantize_x(1, 2, 4)
        regroup_all((3, 0))
        unload_row(2, "SSVS")
        both(1, 0, 2)
        both(1, 2, 4)
        regroup_all((3, 1))
        quantize_x(2, 0, 2)
        unload_t(1, 0, "S")
        turn_x(3)
        turn_a(0)
        unload_t(1, 1, "V")
        quantize_x(2, 2, 4)
        unload_row(3, "SS")
        regroup_all((4, 0))
        quantize_t(0)
        unload_row(3, "SS", 2)
        quantize_x(3, 0, 2)
        regroup_all((4, 1))
        both(2, 0, 2)
        both(2, 2, 4)
        turn_a(1)
        unload_a(0, "S")
        unload_t(2, 0, "S")
        unload_a(1, "S")
        turn_x(4)
        unload_t(2, 1, "V")
        quantize_x(3, 2, 4)
        quantize_a()
        regroup_all(5)
        unload_row(4, "SSSS")
        quantize_x(4, 0, 2)
        both(3, 0, 2)
        both(3, 2, 4)
        unload_t(3, 0, "S")

        turn_x(5)
        second_product(0)
        quantize_x(4, 2, 4)
        regroup_back(6, "V", 0, 1)
        regroup(6)
        regroup_back(6, "G", 1, 16)
        add_c(0)
        unload_row(5, "SSSS")
        unload_t(3, 1, "S")
        both(4, 0, 2)
        both(4, 2, 4)
        quantize_x(5, 0, 2)
        PAIRED = 8
        for j in range(6, PAIRED):
            turn_x(j)
            if j % 2 == 0:
                quantize_x(j - 1, 2, 4)
                regroup(j + 1, "V", 0, LEAD_ONE)
                quantize_t(j - 4)
                regroup_all(j + 1, "G", LEAD_ONE)
                unload_t(j - 2, 0, "V")
                unload_t(j - 2, 1, "V")
                unload_row(j, "SSSS")
                both(j - 1, 0, 2)
                both(j - 1, 2, 4)
                second_product(j - 4)
                silu_store(j - 6)
                quantize_x(j, 0, 2)
                unload_t(j - 1, 0, "S")
            else:
                lead = LEAD if j + 1 == PAIRED else LEAD_ONE
                regroup(j + 1, "V", 0, lead)
                quantize_x(j - 1, 2, 4)
                regroup_all(j + 1, "G", lead)
                if j + 1 == PAIRED:
                    regroup_all(j + 2, "G")
                unload_t(j - 2, 1, "V")
                add_c(j - 5)
                unload_row(j, "SSSS")
                both(j - 1, 0, 2)
                both(j - 1, 2, 4)
                if j + 1 == PAIRED:
                    unload_t(j - 1, 0, "V")
                    unload_t(j - 1, 1, "V")
                    silu_store(j - 5)
                else:
                    quantize_x(j, 0, 2)

        j = PAIRED
        turn_x(j)
        unload_row(j, "SSSS")
        turn_x(j + 1)
        quantize_x(j - 1)
        regroup(j + 2, "V", 0, LEAD)
        quantize_t(j - 4)
        regroup_all(j + 2, "G", LEAD)
        regroup_all(j + 3, "G")
        both(j - 1)
        second_product(j - 4)
        unload_row(j + 1, "VV")
        unload_row(j + 1, "SS", 2)
        unload_t(j - 1, 0, "V")
        unload_t(j - 1, 1, "S")
        add_c(j - 4)


        j = 10
        turn_x(j)
        unload_row(j, "SSSS")
        turn_x(j + 1)
        silu_store(j - 6)
        quantize_x(j - 2)
        quantize_x(j - 1)
        regroup(j + 2, "V", 0, LEAD)
        quantize_t(j - 4)
        regroup_all(j + 2, "G", LEAD)
        regroup_all(j + 3, "G")
        both(j - 2)
        both(j - 1)
        unload_row(j + 1, "SS")
        unload_t(j - 2, 0, "V")
        second_product(j - 4)
        unload_row(j + 1, "SS", 2)
        unload_t(j - 2, 1, "V")
        unload_t(j - 1, 0, "V")
        unload_t(j - 1, 1, "S")
        add_c(j - 4)

        j = 12
        turn_x(j)
        unload_row(j, "SSSS")
        turn_x(j + 1)
        silu_store(j - 6)
        quantize_x(j - 2)
        quantize_x(j - 1)
        regroup(j + 2, "V", 0, LEAD)
        quantize_t(j - 4)
        regroup_all(j + 2, "G", LEAD)
        regroup_all(j + 3, "G")
        both(j - 2)
        both(j - 1)
        unload_row(j + 1, "SS")
        unload_t(j - 2, 0, "V")
        second_product(j - 4)
        unload_row(j + 1, "SS", 2)
        unload_t(j - 2, 1, "V")
        unload_t(j - 1, 0, "V")
        unload_t(j - 1, 1, "S")
        add_c(j - 4)

        last = NB - 1
        j = last - 1
        turn_x(j)
        unload_row(j, "SSSS")
        turn_x(j + 1)
        quantize_x(j - 2)
        quantize_x(j - 1)
        quantize_t(j - 4)
        unload_row(last, "SSSS")
        quantize_x(j)
        both(j - 2)
        both(j - 1)
        unload_t(j - 2, 0, "V")
        second_product(j - 4)
        quantize_x(last)
        unload_t(j - 2, 1, "S")
        unload_t(j - 1, 0, "S")
        unload_t(j - 1, 1, "S")
        both(j)
        add_c(j - 4)
        silu_store(j - 6)
        quantize_t(last - 3)
        unload_t(last - 1, 0, "S")
        unload_t(last - 1, 1, "S")
        first_product(last, (0,))
        first_product(last, (1,))
        second_product(last - 3)
        silu_store(last - 5)
        unload_t(last, 0, "V")
        quantize_t(last - 1)
        second_product(last - 1)
        unload_t(last, 1, "S")
        quantize_t(last, 0, 1)
        last_second_product(last, 0)
        add_c_one(last - 3, 0)
        add_c_one(last - 3, 1)
        quantize_t(last, 1, 2)
        last_second_product(last, 1)
        add_c(last - 1)
        silu_store_one(last - 3)
        silu_store_one(last - 2)
        silu_store(last - 1)
        for h in range(2):
            last_add_c(last, h)
            last_silu_store(last, h)
